import numpy as np
import ml_dtypes


def mxq(x, axis, fmt="e4m3"):
    dtype, down = {"e4m3": (ml_dtypes.float8_e4m3fn, 7), "e5m2": (ml_dtypes.float8_e5m2, 14)}[fmt]
    v = np.moveaxis(np.asarray(x, np.float32).astype(ml_dtypes.bfloat16).astype(np.float64), axis, -1)
    blocks = v.reshape(v.shape[:-1] + (-1, 32))
    amax = np.abs(blocks).max(-1, keepdims=True)
    byte = np.maximum(np.where(amax > 0, np.frexp(amax)[1] - 1 + 127, 0) - down, 1)
    scale = np.exp2(byte - 127.0)
    codes = (blocks / scale).astype(np.float32).astype(dtype).astype(np.float64)
    return np.moveaxis((codes * scale).reshape(v.shape), -1, axis)


WIDE = False


def mx_kscale(k):
    if not WIDE:
        return np.ones(k)
    levels = np.array([10, -10, 5, -5, 0])
    if k % 512:
        return np.exp2(np.random.permutation(np.resize(levels, k // 32))).repeat(32)
    a = np.empty((k // 512, 16))
    for p in range(k // 512):
        a[p, :8] = np.random.permutation(np.resize(levels, 8))
        for g in range(8):
            far = levels[np.abs(levels - a[p, g]) >= 10]
            a[p, g + 8] = far[np.random.randint(len(far))]
    return np.exp2(a.ravel()).repeat(32)


def f64(x):
    return np.asarray(x).astype(np.float64)


def striped(idx):
    return np.tile(idx.reshape(-1, 16).T, (8, 1)).astype(np.uint16)


def unstriped(offs):
    return offs[:16].T.reshape(-1).astype(np.int64)


E2M1 = np.array([0.0, 0.5, 1.0, 1.5, 2.0, 3.0, 4.0, 6.0, -0.0, -0.5, -1.0, -1.5, -2.0, -3.0, -4.0, -6.0])


def pack_weight(w, fmt):
    k, n = w.shape
    w = f64(np.asarray(w, np.float32).astype(ml_dtypes.bfloat16)).reshape(k // 32, 32, n)
    amax = np.abs(w).max(1)
    if fmt == "e4m3":
        byte = np.frexp(amax)[1] - 1 + 127 - 7
    else:
        mant, ex = np.frexp(amax / 6.0)
        byte = np.where(mant > 0.5, ex, ex - 1) + 127
    byte = np.clip(np.where(amax > 0, byte, 1), 1, 254)
    scaled = (w * np.exp2(127.0 - byte)[:, None, :]).reshape(k, n).astype(np.float32)
    by_word = np.ascontiguousarray(scaled.reshape(k // 512, 128, 4, n).transpose(0, 1, 3, 2))
    if fmt == "e4m3":
        words = by_word.astype(ml_dtypes.float8_e4m3fn).view(np.uint8)
    else:
        c = by_word.astype(ml_dtypes.float4_e2m1fn).view(np.uint8) & 0xF
        words = (c[..., 0::2] | (c[..., 1::2] << 4)).reshape(k // 512, 128, 2 * n)
    return np.ascontiguousarray(words), np.ascontiguousarray(byte.astype(np.uint8).reshape(k // 512, 16, n))


def unpack_weight(words, scales, fmt):
    g, _, n = scales.shape
    words = np.ascontiguousarray(words).reshape(g, 128, n, -1)
    if fmt == "e4m3":
        vals = words.view(ml_dtypes.float8_e4m3fn).astype(np.float64)
    else:
        nib = np.empty((g, 128, n, 4), np.uint8)
        nib[..., 0::2] = words & 0xF
        nib[..., 1::2] = words >> 4
        vals = E2M1[nib]
    vals = vals * np.repeat(np.exp2(scales.astype(np.float64) - 127.0), 8, axis=1)[..., None]
    return vals.transpose(0, 1, 3, 2).reshape(g * 512, n)


def gelu(v):
    return 0.5 * v * (1.0 + np.tanh(np.sqrt(2.0 / np.pi) * (v + 0.044715 * v**3)))


K, H, N, T, S, P = 1024, 1024, 512, 4096, 1024, 512

def setup_inputs():
    n = np.random.standard_normal
    s = mx_kscale(K)[:, None]
    u = mx_kscale(H)[:, None]
    tab_words, tab_scales = pack_weight(n((K, T)) * s, "e4m3")
    w4_words, w4_scales = pack_weight(1.5 * n((K, H)) / np.sqrt(K) / s, "e2m1")
    wd = (1.2 * n((K, H)) / np.sqrt(K) / s * u.T).astype(np.float32)
    w8_words, w8_scales = pack_weight(1.2 * n((H, N)) / np.sqrt(H) / u, "e4m3")
    return {"tab_words": tab_words, "tab_scales": tab_scales,
            "offs": striped(np.random.permutation(T)[:S]),
            "pos1": striped(np.random.permutation(S)[:P]),
            "pos2": striped(np.random.permutation(S)[:P]),
            "pos3": striped(np.random.permutation(S)[:P]),
            "w4_words": w4_words, "w4_scales": w4_scales, "wd": wd,
            "w8_words": w8_words, "w8_scales": w8_scales,
            "crumb0": (0.5 * n(N)).astype(np.float32)}

def reference(tab_words, tab_scales, offs, pos1, pos2, pos3, w4_words, w4_scales,
              wd, w8_words, w8_scales, crumb0):
    v = unpack_weight(tab_words, tab_scales, "e4m3")[:, unstriped(offs)]
    w4 = unpack_weight(w4_words, w4_scales, "e2m1")
    w8 = unpack_weight(w8_words, w8_scales, "e4m3")
    act = w4.T @ v
    dough = mxq(f64(wd), 0, "e4m3").T @ v
    share = 1.0 / (1.0 + np.exp(-act[:, unstriped(pos1)]))
    starter = dough[:, unstriped(pos2)]
    previous = dough[:, unstriped(pos3)]
    z = previous + share * (starter - previous)
    y = w8.T @ mxq(z, 0, "e4m3")
    return y + f64(crumb0)[:, None]

@@ -1,0 +1,218 @@
+from contextlib import ExitStack
+
+import concourse.mybir as mybir
+
+K, H, N, T, S, M = 1024, 1024, 512, 4096, 1024, 512
+FLOPS = 2 * (2 * K * H * S + H * N * M)
+
+F32 = mybir.dt.float32
+BF16 = mybir.dt.bfloat16
+I32 = mybir.dt.int32
+U32 = mybir.dt.uint32
+U16 = mybir.dt.uint16
+U8 = mybir.dt.uint8
+FP8X4 = mybir.dt.float8_e4m3fn_x4
+FP4X4 = mybir.dt.float4_e2m1fn_x4
+ALU = mybir.AluOpType
+ACT = mybir.ActivationFunctionType
+
+P = 128
+PACK = 4
+PASS = P * PACK
+BANK = 512
+HALF = M // 2
+
+
+def load_scale_rows(queue, plane, scales):
+    for q in range(4):
+        queue.dma_start(
+            out=plane[32 * q : 32 * q + 4, :, :].bitcast(I32),
+            in_=scales[:, 4 * q : 4 * q + 4, :].rearrange("a r c -> r a c").bitcast(I32),
+        )
+
+
+def tile_list_sourdough_order_blend_kernel(
+    tc, tab_words, tab_scales, offs, pos1, pos2, pos3, w4_words, w4_scales, wd, w8_words, w8_scales, crumb0, out
+):
+    nc = tc.nc
+    with ExitStack() as ctx:
+        lists = ctx.enter_context(tc.tile_pool(name="lists", bufs=1))
+        keep = ctx.enter_context(tc.tile_pool(name="keep", bufs=1))
+        ring = ctx.enter_context(tc.tile_pool(name="ring", bufs=2))
+        psum = ctx.enter_context(tc.psum_pool(name="psum", bufs=8))
+
+        offs_sb = lists.tile([P, S // 16], U16, name="offs_sb")
+        pos1_sb = lists.tile([P, M // 16], U16, name="pos1_sb")
+        pos2_sb = lists.tile([P, M // 16], U16, name="pos2_sb")
+        pos3_sb = lists.tile([P, M // 16], U16, name="pos3_sb")
+
+        tab_sc = keep.tile([P, 2, T], U8, name="tab_sc", align_bytes=64)
+        w4_sc_raw = keep.tile([P, 2, H], U8, name="w4_sc_raw", align_bytes=64)
+        w8_sc = keep.tile([P, 2, N], U8, name="w8_sc", align_bytes=64)
+        nc.gpsimd.memset(tab_sc[:, 0, :].bitcast(I32), 0)
+        nc.vector.memset(tab_sc[:, 1, :].bitcast(I32), 0)
+        nc.vector.memset(w4_sc_raw[:].bitcast(I32), 0)
+        nc.gpsimd.memset(w8_sc[:].bitcast(I32), 0)
+
+        warm = keep.tile([P, 2], F32, name="warm")
+        nc.vector.memset(warm[:, 0:1], 0.0)
+        nc.scalar.activation(out=warm[:, 1:2], in_=warm[:, 0:1], func=ACT.Sigmoid)
+
+        nc.sync.dma_start(offs_sb[:], offs)
+        w4_raw = keep.tile([P, 2, 2 * H], U8, name="w4_raw", align_bytes=64)
+        nc.sync.dma_start(out=w4_raw[:].bitcast(I32), in_=w4_words.rearrange("a p c -> p a c").bitcast(I32))
+        load_scale_rows(nc.sync, tab_sc, tab_scales)
+        tab = []
+        for a in range(2):
+            if a == 1:
+                load_scale_rows(nc.sync, w4_sc_raw, w4_scales)
+            tab.append(keep.tile([P, T], U32, name="tab%d" % a, align_bytes=64))
+            nc.sync.dma_start(out=tab[a][:].bitcast(I32), in_=tab_words[a].rearrange("p n t -> p (n t)").bitcast(I32))
+        nc.sync.dma_start(pos1_sb[:], pos1)
+        nc.sync.dma_start(pos2_sb[:], pos2)
+        nc.sync.dma_start(pos3_sb[:], pos3)
+        wd_raw = {}
+        for b in range(2):
+            for a in range(2):
+                wd_raw[a, b] = keep.tile([P, PACK, PASS], F32, name="wd_raw%d%d" % (a, b), align_bytes=64)
+                nc.sync.dma_start(
+                    out=wd_raw[a, b][:],
+                    in_=wd[a * PASS : (a + 1) * PASS, b * PASS : (b + 1) * PASS].rearrange("(p j) c -> p j c", j=PACK),
+                )
+        w8 = keep.tile([P, 2, N], U32, name="w8", align_bytes=64)
+        nc.sync.dma_start(out=w8[:].bitcast(I32), in_=w8_words.rearrange("a p n t -> p a (n t)").bitcast(I32))
+        load_scale_rows(nc.sync, w8_sc, w8_scales)
+        bias = keep.tile([P, N // P], F32, name="bias")
+        with nc.allow_non_contiguous_dma(reason="one bias value a partition and output tile"):
+            nc.sync.dma_start(out=bias[:], in_=crumb0.rearrange("(c p) -> p c", p=P))
+
+        w4 = keep.tile([P, 2, 2 * H], U8, name="w4", align_bytes=64)
+        w4_sc = keep.tile([P, 2, H], U8, name="w4_sc", align_bytes=64)
+        for a in range(2):
+            nc.vector.tensor_copy(
+                out=w4[:, a, :].bitcast(U16).rearrange("p (b t m) -> p b m t", b=2, t=PACK),
+                in_=w4_raw[:, a, :].bitcast(U16).rearrange("p (b m t) -> p b m t", b=2, t=PACK),
+            )
+
+        v_sc = []
+        for a in range(2):
+            v_sc.append(keep.tile([P, S], U8, name="v_sc%d" % a, align_bytes=64))
+            nc.vector.tensor_copy(out=v_sc[a][:], in_=tab_sc[:, a, :].indirect(offs_sb[:]))
+        v = {}
+        for h in range(2):
+            v[0, h] = keep.tile([P, BANK], U32, name="v0%d" % h, align_bytes=64)
+            nc.vector.tensor_copy(out=v[0, h][:], in_=tab[0][:].indirect(offs_sb[:, 32 * h : 32 * h + 32]))
+        for a in range(2):
+            nc.vector.tensor_copy(
+                out=w4_sc[:, a, :].rearrange("p (b t m) -> p b m t", b=2, t=PACK),
+                in_=w4_sc_raw[:, a, :].rearrange("p (b m t) -> p b m t", b=2, t=PACK),
+            )
+        for h in range(2):
+            v[1, h] = keep.tile([P, BANK], U32, name="v1%d" % h, align_bytes=64)
+            nc.vector.tensor_copy(out=v[1, h][:], in_=tab[1][:].indirect(offs_sb[:, 32 * h : 32 * h + 32]))
+
+        wq = {}
+        wq_sc = {}
+
+        def prepare_wd(a, b, copy):
+            grouped = ring.tile([P, PACK, P, PACK], BF16, name="wd_bf", align_bytes=64)
+            copy(out=grouped[:].rearrange("p t m j -> p m j t"), in_=wd_raw[a, b][:].rearrange("p j (m t) -> p m j t", t=PACK))
+            wq[a, b] = keep.tile([P, PASS], U32, name="wq%d%d" % (a, b), align_bytes=64)
+            wq_sc[a, b] = keep.tile([P, PASS], U8, name="wq_sc%d%d" % (a, b), align_bytes=64)
+            nc.vector.quantize_mx(
+                out=wq[a, b][:].bitcast(FP8X4), scales=wq_sc[a, b][:], in_=grouped[:].rearrange("p t m j -> p (t m j)")
+            )
+
+        def first_stage(s, is_act, copy):
+            b, t = divmod(s, PACK)
+            window = ring.tile([P, S], F32, name="act_w" if is_act else "dough_w", bufs=3 if is_act else 4)
+            for h in range(2):
+                acc = psum.tile([P, BANK], F32, name="acc")
+                for a in range(2):
+                    if is_act:
+                        lhs = w4[:, a, 2 * P * s : 2 * P * (s + 1)].bitcast(FP4X4)
+                        lhs_sc = w4_sc[:, a, P * s : P * (s + 1)]
+                    else:
+                        lhs = wq[a, b][:, P * t : P * (t + 1)].bitcast(FP8X4)
+                        lhs_sc = wq_sc[a, b][:, P * t : P * (t + 1)]
+                    nc.tensor.matmul_mx(
+                        out=acc[:], lhsT=lhs, lhsT_scale=lhs_sc, rhs=v[a, h][:].bitcast(FP8X4),
+                        rhs_scale=v_sc[a][:, BANK * h : BANK * (h + 1)], start=(a == 0), stop=(a == 1),
+                    )
+                copy(out=window[:, BANK * h : BANK * (h + 1)], in_=acc[:])
+            return window
+
+        share = [keep.tile([P, M], F32, name="share%d" % s) for s in range(8)]
+        rest = [keep.tile([P, M], F32, name="rest%d" % s) for s in range(8)]
+        prev = [keep.tile([P, PACK, M], F32, name="prev%d" % b) for b in range(2)]
+        diff = [keep.tile([P, PACK, M], F32, name="diff%d" % b) for b in range(2)]
+        z_bf = [keep.tile([P, M, PACK], BF16, name="z_bf%d" % b, align_bytes=64) for b in range(2)]
+        zq = [keep.tile([P, M], U32, name="zq%d" % b, align_bytes=64) for b in range(2)]
+        zq_sc = [keep.tile([P, M], U8, name="zq_sc%d" % b, align_bytes=64) for b in range(2)]
+
+        def activity(s, copy):
+            window = first_stage(s, True, copy)
+            nc.scalar.activation(out=share[s][:], in_=window[:].indirect(pos1_sb[:]), func=ACT.Sigmoid)
+            nc.scalar.activation(out=rest[s][:], in_=share[s][:], func=ACT.Identity, scale=-1.0, bias=1.0)
+
+        def pick(s, window):
+            b, t = divmod(s, PACK)
+            nc.vector.tensor_tensor(out=diff[b][:, t, :], in0=window[:].indirect(pos2_sb[:]), in1=share[s][:], op=ALU.mult)
+            nc.vector.tensor_tensor(out=prev[b][:, t, :], in0=window[:].indirect(pos3_sb[:]), in1=rest[s][:], op=ALU.mult)
+
+        def blend(b, h):
+            cols = slice(HALF * h, HALF * (h + 1))
+            nc.vector.tensor_tensor(
+                out=z_bf[b][:, cols, :].rearrange("p (c i) t -> p c t i", i=4),
+                in0=diff[b][:, :, cols].rearrange("p t (c i) -> p c t i", i=4),
+                in1=prev[b][:, :, cols].rearrange("p t (c i) -> p c t i", i=4),
+                op=ALU.add,
+            )
+
+        def quantize_z(b, h):
+            cols = slice(HALF * h, HALF * (h + 1))
+            nc.vector.quantize_mx(
+                out=zq[b][:, cols].bitcast(FP8X4), scales=zq_sc[b][:, cols], in_=z_bf[b][:, cols, :].rearrange("p m t -> p (m t)")
+            )
+
+        activity(0, nc.scalar.copy)
+        prepare_wd(0, 0, nc.vector.tensor_copy)
+        activity(1, nc.scalar.copy)
+        prepare_wd(1, 0, nc.vector.tensor_copy)
+        window = first_stage(0, False, nc.scalar.copy)
+        for s in range(8):
+            if s + 1 < 8:
+                following = first_stage(s + 1, False, nc.scalar.copy)
+            pick(s, window)
+            if s + 2 < 8:
+                activity(s + 2, nc.scalar.copy)
+            if s < 2:
+                prepare_wd(s, 1, nc.vector.tensor_copy)
+            if s == 4:
+                for h in range(2):
+                    blend(0, h)
+            if s == 5:
+                for h in range(2):
+                    quantize_z(0, h)
+            window = following
+        blend(1, 0)
+        blend(1, 1)
+        for h in range(2):
+            quantize_z(1, h)
+            cols = slice(HALF * h, HALF * (h + 1))
+            result = ring.tile([P, N // P, HALF], F32, name="result")
+            for c in range(N // P):
+                acc = psum.tile([P, BANK], F32, name="acc")
+                for b in range(2):
+                    nc.tensor.matmul_mx(
+                        out=acc[:, :HALF], lhsT=w8[:, b, P * c : P * (c + 1)].bitcast(FP8X4), lhsT_scale=w8_sc[:, b, P * c : P * (c + 1)],
+                        rhs=zq[b][:, cols].bitcast(FP8X4), rhs_scale=zq_sc[b][:, cols], start=(b == 0), stop=(b == 1),
+                    )
+                if h == 1 and c % 2 == 1:
+                    nc.vector.tensor_scalar(out=result[:, c, :], in0=acc[:, :HALF], scalar1=bias[:, c : c + 1], scalar2=None, op0=ALU.add)
+                else:
+                    nc.scalar.activation(out=result[:, c, :], in_=acc[:, :HALF], func=ACT.Identity, bias=bias[:, c : c + 1])
+                if c % 2 == 1:
+                    nc.sync.dma_start(
+                        out=out[P * (c - 1) : P * (c + 1), cols].rearrange("(c p) m -> p c m", p=P), in_=result[:, c - 1 : c + 1, :]
+                    )

@@ -39,52 +39,56 @@ def tile_list_sourdough_order_blend_kernel(
         lists = ctx.enter_context(tc.tile_pool(name="lists", bufs=1))
         keep = ctx.enter_context(tc.tile_pool(name="keep", bufs=1))
         ring = ctx.enter_context(tc.tile_pool(name="ring", bufs=2))
-        psum = ctx.enter_context(tc.psum_pool(name="psum", bufs=8))
+        psum = ctx.enter_context(tc.psum_pool(name="psum", bufs=2))
 
         offs_sb = lists.tile([P, S // 16], U16, name="offs_sb")
         pos1_sb = lists.tile([P, M // 16], U16, name="pos1_sb")
         pos2_sb = lists.tile([P, M // 16], U16, name="pos2_sb")
         pos3_sb = lists.tile([P, M // 16], U16, name="pos3_sb")
 
-        tab_sc = keep.tile([P, 2, T], U8, name="tab_sc", align_bytes=64)
-        w4_sc_raw = keep.tile([P, 2, H], U8, name="w4_sc_raw", align_bytes=64)
-        w8_sc = keep.tile([P, 2, N], U8, name="w8_sc", align_bytes=64)
-        nc.gpsimd.memset(tab_sc[:, 0, :].bitcast(I32), 0)
-        nc.vector.memset(tab_sc[:, 1, :].bitcast(I32), 0)
+        tab_sc = keep.tile([P, T], U8, name="tab_sc", tag="late_table", align_bytes=64)
+        w4_sc_raw = keep.tile([P, 2, H], U8, name="w4_sc_raw", tag="w4_sc_raw", align_bytes=64)
+        v_sc = keep.tile([P, 2, S], U8, name="v_sc", align_bytes=64)
+        nc.gpsimd.memset(tab_sc[:, : T // 2].bitcast(I32), 0)
+        nc.vector.memset(tab_sc[:, T // 2 :].bitcast(I32), 0)
         nc.vector.memset(w4_sc_raw[:].bitcast(I32), 0)
-        nc.gpsimd.memset(w8_sc[:].bitcast(I32), 0)
+        nc.vector.memset(v_sc[:].bitcast(I32), 0)
 
         warm = keep.tile([P, 2], F32, name="warm")
         nc.vector.memset(warm[:, 0:1], 0.0)
         nc.scalar.activation(out=warm[:, 1:2], in_=warm[:, 0:1], func=ACT.Sigmoid)
 
+        load_scale_rows(nc.gpsimd, w4_sc_raw, w4_scales)
+
+        def load_wd(dst, a, b):
+            nc.sync.dma_start(
+                out=dst, in_=wd[a * PASS : (a + 1) * PASS, b * PASS : (b + 1) * PASS].rearrange("(p j) c -> p j c", j=PACK)
+            )
+
+        def load_table(dst, a):
+            nc.sync.dma_start(out=dst[:].bitcast(I32), in_=tab_words[a].rearrange("p n t -> p (n t)").bitcast(I32))
+
         nc.sync.dma_start(offs_sb[:], offs)
-        w4_raw = keep.tile([P, 2, 2 * H], U8, name="w4_raw", align_bytes=64)
+        nc.sync.dma_start(out=tab_sc[0:P:4, :].bitcast(I32), in_=tab_scales.rearrange("a q t -> (a q) t").bitcast(I32))
+        w4_raw = keep.tile([P, 2, 2 * H], U8, name="w4_raw", tag="wd_raw1", align_bytes=64)
         nc.sync.dma_start(out=w4_raw[:].bitcast(I32), in_=w4_words.rearrange("a p c -> p a c").bitcast(I32))
-        load_scale_rows(nc.sync, tab_sc, tab_scales)
-        tab = []
-        for a in range(2):
-            if a == 1:
-                load_scale_rows(nc.sync, w4_sc_raw, w4_scales)
-            tab.append(keep.tile([P, T], U32, name="tab%d" % a, align_bytes=64))
-            nc.sync.dma_start(out=tab[a][:].bitcast(I32), in_=tab_words[a].rearrange("p n t -> p (n t)").bitcast(I32))
         nc.sync.dma_start(pos1_sb[:], pos1)
         nc.sync.dma_start(pos2_sb[:], pos2)
         nc.sync.dma_start(pos3_sb[:], pos3)
+        tab0 = keep.tile([P, T], U32, name="tab0", tag="early_table", align_bytes=64)
+        load_table(tab0, 0)
         wd_raw = {}
-        for b in range(2):
-            for a in range(2):
-                wd_raw[a, b] = keep.tile([P, PACK, PASS], F32, name="wd_raw%d%d" % (a, b), align_bytes=64)
+
+        picked_sc = keep.tile([P, S], U8, name="picked_sc", tag="picked_sc", align_bytes=64)
+        nc.vector.tensor_copy(out=picked_sc[:], in_=tab_sc[:].indirect(offs_sb[:]))
+        tab1 = keep.tile([P, T], U32, name="tab1", tag="late_table", align_bytes=64)
+        for a in range(2):
+            for r in range(4):
+                if (a, r) == (1, 0):
+                    load_table(tab1, 1)
                 nc.sync.dma_start(
-                    out=wd_raw[a, b][:],
-                    in_=wd[a * PASS : (a + 1) * PASS, b * PASS : (b + 1) * PASS].rearrange("(p j) c -> p j c", j=PACK),
+                    out=v_sc[r:P:32, a, :].bitcast(I32), in_=picked_sc[64 * a + 4 * r : 64 * a + 64 : 16, :].bitcast(I32)
                 )
-        w8 = keep.tile([P, 2, N], U32, name="w8", align_bytes=64)
-        nc.sync.dma_start(out=w8[:].bitcast(I32), in_=w8_words.rearrange("a p n t -> p a (n t)").bitcast(I32))
-        load_scale_rows(nc.sync, w8_sc, w8_scales)
-        bias = keep.tile([P, N // P], F32, name="bias")
-        with nc.allow_non_contiguous_dma(reason="one bias value a partition and output tile"):
-            nc.sync.dma_start(out=bias[:], in_=crumb0.rearrange("(c p) -> p c", p=P))
 
         w4 = keep.tile([P, 2, 2 * H], U8, name="w4", align_bytes=64)
         w4_sc = keep.tile([P, 2, H], U8, name="w4_sc", align_bytes=64)
@@ -93,41 +97,47 @@ def tile_list_sourdough_order_blend_kernel(
                 out=w4[:, a, :].bitcast(U16).rearrange("p (b t m) -> p b m t", b=2, t=PACK),
                 in_=w4_raw[:, a, :].bitcast(U16).rearrange("p (b m t) -> p b m t", b=2, t=PACK),
             )
-
-        v_sc = []
+        early_raw = keep.tile([P, 2 * PACK * PASS], F32, name="early_raw", tag="wd_raw1", align_bytes=64)
         for a in range(2):
-            v_sc.append(keep.tile([P, S], U8, name="v_sc%d" % a, align_bytes=64))
-            nc.vector.tensor_copy(out=v_sc[a][:], in_=tab_sc[:, a, :].indirect(offs_sb[:]))
+            wd_raw[a, 0] = early_raw[:, a * PACK * PASS : (a + 1) * PACK * PASS].rearrange("p (j c) -> p j c", j=PACK)
+            load_wd(wd_raw[a, 0], a, 0)
         v = {}
         for h in range(2):
             v[0, h] = keep.tile([P, BANK], U32, name="v0%d" % h, align_bytes=64)
-            nc.vector.tensor_copy(out=v[0, h][:], in_=tab[0][:].indirect(offs_sb[:, 32 * h : 32 * h + 32]))
+            nc.vector.tensor_copy(out=v[0, h][:], in_=tab0[:].indirect(offs_sb[:, 32 * h : 32 * h + 32]))
         for a in range(2):
             nc.vector.tensor_copy(
                 out=w4_sc[:, a, :].rearrange("p (b t m) -> p b m t", b=2, t=PACK),
                 in_=w4_sc_raw[:, a, :].rearrange("p (b m t) -> p b m t", b=2, t=PACK),
             )
-        for h in range(2):
-            v[1, h] = keep.tile([P, BANK], U32, name="v1%d" % h, align_bytes=64)
-            nc.vector.tensor_copy(out=v[1, h][:], in_=tab[1][:].indirect(offs_sb[:, 32 * h : 32 * h + 32]))
 
         wq = {}
         wq_sc = {}
 
         def prepare_wd(a, b, copy):
-            grouped = ring.tile([P, PACK, P, PACK], BF16, name="wd_bf", align_bytes=64)
-            copy(out=grouped[:].rearrange("p t m j -> p m j t"), in_=wd_raw[a, b][:].rearrange("p j (m t) -> p m j t", t=PACK))
+            pieces = [(slice(0, P), slice(0, 1)), (slice(P, 2 * P), slice(1, 2)), (slice(2 * P, PASS), slice(2, 4))] if (a, b) == (1, 0) else [(slice(0, PASS), slice(0, 4))]
+            grouped = keep.tile([P, PACK, P, PACK], BF16, name="wd_bf", tag="wd_bf%d%d" % (a, b), align_bytes=64)
+            copy(out=grouped[:].rearrange("p t m j -> p m j t"), in_=wd_raw[a, b].rearrange("p j (m t) -> p m j t", t=PACK))
             wq[a, b] = keep.tile([P, PASS], U32, name="wq%d%d" % (a, b), align_bytes=64)
             wq_sc[a, b] = keep.tile([P, PASS], U8, name="wq_sc%d%d" % (a, b), align_bytes=64)
-            nc.vector.quantize_mx(
-                out=wq[a, b][:].bitcast(FP8X4), scales=wq_sc[a, b][:], in_=grouped[:].rearrange("p t m j -> p (t m j)")
-            )
+            for cols, ts in pieces:
+                nc.vector.quantize_mx(
+                    out=wq[a, b][:, cols].bitcast(FP8X4), scales=wq_sc[a, b][:, cols], in_=grouped[:, ts, :, :].rearrange("p t m j -> p (t m j)")
+                )
 
-        def first_stage(s, is_act, copy):
+        def bank(is_act):
+            return psum.tile([P, BANK], F32, name="act_acc" if is_act else "dough_acc", bufs=4)
+
+        def first_stage(s, is_act, copies):
             b, t = divmod(s, PACK)
-            window = ring.tile([P, S], F32, name="act_w" if is_act else "dough_w", bufs=3 if is_act else 4)
+            if is_act and s in (2, 3):
+                window = keep.tile([P, S], F32, name="held_act_w", tag="wd_bf10" if s == 2 else "wd_raw1", align_bytes=64)
+            elif is_act or s > 1:
+                window = ring.tile([P, S], F32, name="act_w" if is_act else "dough_w", bufs=2 if is_act else 3)
+            else:
+                window = keep.tile([P, S], F32, name="first_dough_w", tag="wd_bf%d1" % s, align_bytes=64)
             for h in range(2):
-                acc = psum.tile([P, BANK], F32, name="acc")
+                acc = bank(is_act)
                 for a in range(2):
                     if is_act:
                         lhs = w4[:, a, 2 * P * s : 2 * P * (s + 1)].bitcast(FP4X4)
@@ -137,28 +147,40 @@ def tile_list_sourdough_order_blend_kernel(
                         lhs_sc = wq_sc[a, b][:, P * t : P * (t + 1)]
                     nc.tensor.matmul_mx(
                         out=acc[:], lhsT=lhs, lhsT_scale=lhs_sc, rhs=v[a, h][:].bitcast(FP8X4),
-                        rhs_scale=v_sc[a][:, BANK * h : BANK * (h + 1)], start=(a == 0), stop=(a == 1),
+                        rhs_scale=v_sc[:, a, BANK * h : BANK * (h + 1)], start=(a == 0), stop=(a == 1),
                     )
-                copy(out=window[:, BANK * h : BANK * (h + 1)], in_=acc[:])
+                copies[h](out=window[:, BANK * h : BANK * (h + 1)], in_=acc[:])
             return window
 
-        share = [keep.tile([P, M], F32, name="share%d" % s) for s in range(8)]
-        rest = [keep.tile([P, M], F32, name="rest%d" % s) for s in range(8)]
+        share = {}
         prev = [keep.tile([P, PACK, M], F32, name="prev%d" % b) for b in range(2)]
         diff = [keep.tile([P, PACK, M], F32, name="diff%d" % b) for b in range(2)]
         z_bf = [keep.tile([P, M, PACK], BF16, name="z_bf%d" % b, align_bytes=64) for b in range(2)]
         zq = [keep.tile([P, M], U32, name="zq%d" % b, align_bytes=64) for b in range(2)]
         zq_sc = [keep.tile([P, M], U8, name="zq_sc%d" % b, align_bytes=64) for b in range(2)]
 
-        def activity(s, copy):
-            window = first_stage(s, True, copy)
+        def share_of(s, window):
+            share[s] = ring.tile([P, M], F32, name="share", bufs=4)
             nc.scalar.activation(out=share[s][:], in_=window[:].indirect(pos1_sb[:]), func=ACT.Sigmoid)
-            nc.scalar.activation(out=rest[s][:], in_=share[s][:], func=ACT.Identity, scale=-1.0, bias=1.0)
 
         def pick(s, window):
             b, t = divmod(s, PACK)
-            nc.vector.tensor_tensor(out=diff[b][:, t, :], in0=window[:].indirect(pos2_sb[:]), in1=share[s][:], op=ALU.mult)
-            nc.vector.tensor_tensor(out=prev[b][:, t, :], in0=window[:].indirect(pos3_sb[:]), in1=rest[s][:], op=ALU.mult)
+            nc.vector.tensor_copy(out=prev[b][:, t, :], in_=window[:].indirect(pos3_sb[:]))
+            nc.vector.tensor_copy(out=diff[b][:, t, :], in_=window[:].indirect(pos2_sb[:]))
+            nc.gpsimd.tensor_tensor(out=diff[b][:, t, :], in0=diff[b][:, t, :], in1=prev[b][:, t, :], op=ALU.subtract)
+            nc.gpsimd.tensor_tensor(out=diff[b][:, t, :], in0=diff[b][:, t, :], in1=share[s][:], op=ALU.mult)
+
+        def pick_last(s, window):
+            b, t = divmod(s, PACK)
+            halves = [(slice(HALF * h, HALF * (h + 1)), slice(16 * h, 16 * (h + 1))) for h in range(2)]
+            for cols, entries in halves:
+                nc.vector.tensor_copy(out=prev[b][:, t, cols], in_=window[:].indirect(pos3_sb[:, entries]))
+            for cols, entries in halves:
+                nc.vector.tensor_tensor(
+                    out=diff[b][:, t, cols], in0=window[:].indirect(pos2_sb[:, entries]), in1=prev[b][:, t, cols], op=ALU.subtract
+                )
+            for cols, entries in halves:
+                nc.vector.tensor_tensor(out=diff[b][:, t, cols], in0=diff[b][:, t, cols], in1=share[s][:, cols], op=ALU.mult)
 
         def blend(b, h):
             cols = slice(HALF * h, HALF * (h + 1))
@@ -175,26 +197,43 @@ def tile_list_sourdough_order_blend_kernel(
                 out=zq[b][:, cols].bitcast(FP8X4), scales=zq_sc[b][:, cols], in_=z_bf[b][:, cols, :].rearrange("p m t -> p (m t)")
             )
 
-        activity(0, nc.scalar.copy)
-        prepare_wd(0, 0, nc.vector.tensor_copy)
-        activity(1, nc.scalar.copy)
-        prepare_wd(1, 0, nc.vector.tensor_copy)
-        window = first_stage(0, False, nc.scalar.copy)
+        for h in range(2):
+            v[1, h] = keep.tile([P, BANK], U32, name="v1%d" % h, align_bytes=64)
+            nc.vector.tensor_copy(out=v[1, h][:], in_=tab1[:].indirect(offs_sb[:, 32 * h : 32 * h + 32]))
+        w8 = keep.tile([P, 2, N], U32, name="w8", tag="early_table", align_bytes=64)
+        nc.sync.dma_start(out=w8[:].bitcast(I32), in_=w8_words.rearrange("a p n t -> p a (n t)").bitcast(I32))
+        late_raw = keep.tile([P, 2 * PACK * PASS], F32, name="late_raw", tag="late_table", align_bytes=64)
+        for a in range(2):
+            wd_raw[a, 1] = late_raw[:, a * PACK * PASS : (a + 1) * PACK * PASS].rearrange("p (j c) -> p j c", j=PACK)
+            load_wd(wd_raw[a, 1], a, 1)
+        w8_sc = keep.tile([P, 2, N], U8, name="w8_sc", tag="picked_sc", align_bytes=64)
+        nc.gpsimd.memset(w8_sc[:].bitcast(I32), 0)
+        load_scale_rows(nc.sync, w8_sc, w8_scales)
+        bias = keep.tile([P, N // P], F32, name="bias", tag="w4_sc_raw", align_bytes=64)
+        with nc.allow_non_contiguous_dma(reason="one bias value a partition and output tile"):
+            nc.sync.dma_start(out=bias[:], in_=crumb0.rearrange("(c p) -> p c", p=P))
+        on_scalar = (nc.scalar.copy, nc.scalar.copy)
+        for s in range(2):
+            share_of(s, first_stage(s, True, on_scalar))
+            prepare_wd(s, 0, nc.vector.tensor_copy)
+        dough = {0: first_stage(0, False, (nc.vector.tensor_copy, nc.vector.tensor_copy)), 1: first_stage(1, False, on_scalar)}
         for s in range(8):
-            if s + 1 < 8:
-                following = first_stage(s + 1, False, nc.scalar.copy)
-            pick(s, window)
+            if s < 7:
+                pick(s, dough[s])
+            else:
+                pick_last(s, dough[s])
             if s + 2 < 8:
-                activity(s + 2, nc.scalar.copy)
-            if s < 2:
-                prepare_wd(s, 1, nc.vector.tensor_copy)
+                dough[s + 2] = first_stage(s + 2, False, on_scalar)
+            if s == 0:
+                prepare_wd(0, 1, nc.scalar.copy)
+                prepare_wd(1, 1, nc.scalar.copy)
+            if s + 2 < 8:
+                share_of(s + 2, first_stage(s + 2, True, on_scalar))
             if s == 4:
                 for h in range(2):
                     blend(0, h)
-            if s == 5:
                 for h in range(2):
                     quantize_z(0, h)
-            window = following
         blend(1, 0)
         blend(1, 1)
         for h in range(2):
@@ -202,7 +241,7 @@ def tile_list_sourdough_order_blend_kernel(
             cols = slice(HALF * h, HALF * (h + 1))
             result = ring.tile([P, N // P, HALF], F32, name="result")
             for c in range(N // P):
-                acc = psum.tile([P, BANK], F32, name="acc")
+                acc = bank(h == 0)
                 for b in range(2):
                     nc.tensor.matmul_mx(
                         out=acc[:, :HALF], lhsT=w8[:, b, P * c : P * (c + 1)].bitcast(FP8X4), lhsT_scale=w8_sc[:, b, P * c : P * (c + 1)],

@@ -39,7 +39,7 @@ def tile_list_sourdough_order_blend_kernel(
         lists = ctx.enter_context(tc.tile_pool(name="lists", bufs=1))
         keep = ctx.enter_context(tc.tile_pool(name="keep", bufs=1))
         ring = ctx.enter_context(tc.tile_pool(name="ring", bufs=2))
-        psum = ctx.enter_context(tc.psum_pool(name="psum", bufs=2))
+        psum = ctx.enter_context(tc.psum_pool(name="psum", bufs=1))
 
         offs_sb = lists.tile([P, S // 16], U16, name="offs_sb")
         pos1_sb = lists.tile([P, M // 16], U16, name="pos1_sb")
@@ -94,8 +94,8 @@ def tile_list_sourdough_order_blend_kernel(
         w4_sc = keep.tile([P, 2, H], U8, name="w4_sc", align_bytes=64)
         for a in range(2):
             nc.vector.tensor_copy(
-                out=w4[:, a, :].bitcast(U16).rearrange("p (b t m) -> p b m t", b=2, t=PACK),
-                in_=w4_raw[:, a, :].bitcast(U16).rearrange("p (b m t) -> p b m t", b=2, t=PACK),
+                out=w4[:, a, :].bitcast(U16).rearrange("p (b t m) -> p b t m", b=2, t=PACK),
+                in_=w4_raw[:, a, :].bitcast(U16).rearrange("p (b m t) -> p b t m", b=2, t=PACK),
             )
         early_raw = keep.tile([P, 2 * PACK * PASS], F32, name="early_raw", tag="wd_raw1", align_bytes=64)
         for a in range(2):
@@ -107,17 +107,21 @@ def tile_list_sourdough_order_blend_kernel(
             nc.vector.tensor_copy(out=v[0, h][:], in_=tab0[:].indirect(offs_sb[:, 32 * h : 32 * h + 32]))
         for a in range(2):
             nc.vector.tensor_copy(
-                out=w4_sc[:, a, :].rearrange("p (b t m) -> p b m t", b=2, t=PACK),
-                in_=w4_sc_raw[:, a, :].rearrange("p (b m t) -> p b m t", b=2, t=PACK),
+                out=w4_sc[:, a, :].rearrange("p (b t m) -> p b t m", b=2, t=PACK),
+                in_=w4_sc_raw[:, a, :].rearrange("p (b m t) -> p b t m", b=2, t=PACK),
             )
 
         wq = {}
         wq_sc = {}
 
         def prepare_wd(a, b, copy):
-            pieces = [(slice(0, P), slice(0, 1)), (slice(P, 2 * P), slice(1, 2)), (slice(2 * P, PASS), slice(2, 4))] if (a, b) == (1, 0) else [(slice(0, PASS), slice(0, 4))]
+            pieces = [(slice(0, 2 * P), slice(0, 2)), (slice(2 * P, PASS), slice(2, 4))] if (a, b) == (1, 0) else [(slice(0, PASS), slice(0, 4))]
             grouped = keep.tile([P, PACK, P, PACK], BF16, name="wd_bf", tag="wd_bf%d%d" % (a, b), align_bytes=64)
-            copy(out=grouped[:].rearrange("p t m j -> p m j t"), in_=wd_raw[a, b].rearrange("p j (m t) -> p m j t", t=PACK))
+            for pair in (slice(0, 2), slice(2, 4)):
+                copy(
+                    out=grouped[:, pair, :, :].rearrange("p t m j -> p m j t"),
+                    in_=wd_raw[a, b].rearrange("p j (m t) -> p m j t", t=PACK)[:, :, :, pair],
+                )
             wq[a, b] = keep.tile([P, PASS], U32, name="wq%d%d" % (a, b), align_bytes=64)
             wq_sc[a, b] = keep.tile([P, PASS], U8, name="wq_sc%d%d" % (a, b), align_bytes=64)
             for cols, ts in pieces:
@@ -125,19 +129,20 @@ def tile_list_sourdough_order_blend_kernel(
                     out=wq[a, b][:, cols].bitcast(FP8X4), scales=wq_sc[a, b][:, cols], in_=grouped[:, ts, :, :].rearrange("p t m j -> p (t m j)")
                 )
 
-        def bank(is_act):
-            return psum.tile([P, BANK], F32, name="act_acc" if is_act else "dough_acc", bufs=4)
+        banks_taken = []
+
+        def bank():
+            banks_taken.append(psum.tile([P, BANK], F32, name="acc%d" % (len(banks_taken) % 8)))
+            return banks_taken[-1]
 
         def first_stage(s, is_act, copies):
             b, t = divmod(s, PACK)
-            if is_act and s in (2, 3):
-                window = keep.tile([P, S], F32, name="held_act_w", tag="wd_bf10" if s == 2 else "wd_raw1", align_bytes=64)
-            elif is_act or s > 1:
+            if is_act or s > 1:
                 window = ring.tile([P, S], F32, name="act_w" if is_act else "dough_w", bufs=2 if is_act else 3)
             else:
                 window = keep.tile([P, S], F32, name="first_dough_w", tag="wd_bf%d1" % s, align_bytes=64)
             for h in range(2):
-                acc = bank(is_act)
+                acc = bank()
                 for a in range(2):
                     if is_act:
                         lhs = w4[:, a, 2 * P * s : 2 * P * (s + 1)].bitcast(FP4X4)
@@ -160,7 +165,7 @@ def tile_list_sourdough_order_blend_kernel(
         zq_sc = [keep.tile([P, M], U8, name="zq_sc%d" % b, align_bytes=64) for b in range(2)]
 
         def share_of(s, window):
-            share[s] = ring.tile([P, M], F32, name="share", bufs=4)
+            share[s] = ring.tile([P, M], F32, name="share", bufs=6)
             nc.scalar.activation(out=share[s][:], in_=window[:].indirect(pos1_sb[:]), func=ACT.Sigmoid)
 
         def pick(s, window):
@@ -182,12 +187,11 @@ def tile_list_sourdough_order_blend_kernel(
             for cols, entries in halves:
                 nc.vector.tensor_tensor(out=diff[b][:, t, cols], in0=diff[b][:, t, cols], in1=share[s][:, cols], op=ALU.mult)
 
-        def blend(b, h):
-            cols = slice(HALF * h, HALF * (h + 1))
+        def blend(b, cols):
             nc.vector.tensor_tensor(
-                out=z_bf[b][:, cols, :].rearrange("p (c i) t -> p c t i", i=4),
-                in0=diff[b][:, :, cols].rearrange("p t (c i) -> p c t i", i=4),
-                in1=prev[b][:, :, cols].rearrange("p t (c i) -> p c t i", i=4),
+                out=z_bf[b][:, cols, :].rearrange("p (c i) t -> p c t i", i=2),
+                in0=diff[b][:, :, cols].rearrange("p t (c i) -> p c t i", i=2),
+                in1=prev[b][:, :, cols].rearrange("p t (c i) -> p c t i", i=2),
                 op=ALU.add,
             )
 
@@ -216,32 +220,35 @@ def tile_list_sourdough_order_blend_kernel(
         for s in range(2):
             share_of(s, first_stage(s, True, on_scalar))
             prepare_wd(s, 0, nc.vector.tensor_copy)
-        dough = {0: first_stage(0, False, (nc.vector.tensor_copy, nc.vector.tensor_copy)), 1: first_stage(1, False, on_scalar)}
+        dough = {0: first_stage(0, False, (nc.vector.tensor_copy, nc.vector.tensor_copy))}
+        for s in range(1, PACK):
+            dough[s] = first_stage(s, False, on_scalar)
         for s in range(8):
             if s < 7:
                 pick(s, dough[s])
             else:
                 pick_last(s, dough[s])
-            if s + 2 < 8:
+            if s < 2:
+                prepare_wd(s, 1, nc.scalar.copy)
+            if PACK <= s + 2 < 8:
                 dough[s + 2] = first_stage(s + 2, False, on_scalar)
-            if s == 0:
-                prepare_wd(0, 1, nc.scalar.copy)
-                prepare_wd(1, 1, nc.scalar.copy)
             if s + 2 < 8:
                 share_of(s + 2, first_stage(s + 2, True, on_scalar))
             if s == 4:
                 for h in range(2):
-                    blend(0, h)
+                    blend(0, slice(HALF * h, HALF * (h + 1)))
                 for h in range(2):
                     quantize_z(0, h)
-        blend(1, 0)
-        blend(1, 1)
+        blend(1, slice(0, HALF))
+        blend(1, slice(HALF, HALF + P))
+        quantize_z(1, 0)
+        blend(1, slice(HALF + P, M))
+        quantize_z(1, 1)
         for h in range(2):
-            quantize_z(1, h)
             cols = slice(HALF * h, HALF * (h + 1))
             result = ring.tile([P, N // P, HALF], F32, name="result")
             for c in range(N // P):
-                acc = bank(h == 0)
+                acc = bank()
                 for b in range(2):
                     nc.tensor.matmul_mx(
                         out=acc[:, :HALF], lhsT=w8[:, b, P * c : P * (c + 1)].bitcast(FP8X4), lhsT_scale=w8_sc[:, b, P * c : P * (c + 1)],

@@ -94,8 +94,8 @@ def tile_list_sourdough_order_blend_kernel(
         w4_sc = keep.tile([P, 2, H], U8, name="w4_sc", align_bytes=64)
         for a in range(2):
             nc.vector.tensor_copy(
-                out=w4[:, a, :].bitcast(U16).rearrange("p (b t m) -> p b t m", b=2, t=PACK),
-                in_=w4_raw[:, a, :].bitcast(U16).rearrange("p (b m t) -> p b t m", b=2, t=PACK),
+                out=w4[:, a, :].bitcast(U16).rearrange("p (b t m) -> p b m t", b=2, t=PACK),
+                in_=w4_raw[:, a, :].bitcast(U16).rearrange("p (b m t) -> p b m t", b=2, t=PACK),
             )
         early_raw = keep.tile([P, 2 * PACK * PASS], F32, name="early_raw", tag="wd_raw1", align_bytes=64)
         for a in range(2):
@@ -107,8 +107,8 @@ def tile_list_sourdough_order_blend_kernel(
             nc.vector.tensor_copy(out=v[0, h][:], in_=tab0[:].indirect(offs_sb[:, 32 * h : 32 * h + 32]))
         for a in range(2):
             nc.vector.tensor_copy(
-                out=w4_sc[:, a, :].rearrange("p (b t m) -> p b t m", b=2, t=PACK),
-                in_=w4_sc_raw[:, a, :].rearrange("p (b m t) -> p b t m", b=2, t=PACK),
+                out=w4_sc[:, a, :].rearrange("p (b t m) -> p b m t", b=2, t=PACK),
+                in_=w4_sc_raw[:, a, :].rearrange("p (b m t) -> p b m t", b=2, t=PACK),
             )
 
         wq = {}
@@ -117,11 +117,7 @@ def tile_list_sourdough_order_blend_kernel(
         def prepare_wd(a, b, copy):
             pieces = [(slice(0, 2 * P), slice(0, 2)), (slice(2 * P, PASS), slice(2, 4))] if (a, b) == (1, 0) else [(slice(0, PASS), slice(0, 4))]
             grouped = keep.tile([P, PACK, P, PACK], BF16, name="wd_bf", tag="wd_bf%d%d" % (a, b), align_bytes=64)
-            for pair in (slice(0, 2), slice(2, 4)):
-                copy(
-                    out=grouped[:, pair, :, :].rearrange("p t m j -> p m j t"),
-                    in_=wd_raw[a, b].rearrange("p j (m t) -> p m j t", t=PACK)[:, :, :, pair],
-                )
+            copy(out=grouped[:].rearrange("p t m j -> p m j t"), in_=wd_raw[a, b].rearrange("p j (m t) -> p m j t", t=PACK))
             wq[a, b] = keep.tile([P, PASS], U32, name="wq%d%d" % (a, b), align_bytes=64)
             wq_sc[a, b] = keep.tile([P, PASS], U8, name="wq_sc%d%d" % (a, b), align_bytes=64)
             for cols, ts in pieces:
@@ -160,7 +156,7 @@ def tile_list_sourdough_order_blend_kernel(
         share = {}
         prev = [keep.tile([P, PACK, M], F32, name="prev%d" % b) for b in range(2)]
         diff = [keep.tile([P, PACK, M], F32, name="diff%d" % b) for b in range(2)]
-        z_bf = [keep.tile([P, M, PACK], BF16, name="z_bf%d" % b, align_bytes=64) for b in range(2)]
+        z_bf = {}
         zq = [keep.tile([P, M], U32, name="zq%d" % b, align_bytes=64) for b in range(2)]
         zq_sc = [keep.tile([P, M], U8, name="zq_sc%d" % b, align_bytes=64) for b in range(2)]
 
@@ -169,13 +165,6 @@ def tile_list_sourdough_order_blend_kernel(
             nc.scalar.activation(out=share[s][:], in_=window[:].indirect(pos1_sb[:]), func=ACT.Sigmoid)
 
         def pick(s, window):
-            b, t = divmod(s, PACK)
-            nc.vector.tensor_copy(out=prev[b][:, t, :], in_=window[:].indirect(pos3_sb[:]))
-            nc.vector.tensor_copy(out=diff[b][:, t, :], in_=window[:].indirect(pos2_sb[:]))
-            nc.gpsimd.tensor_tensor(out=diff[b][:, t, :], in0=diff[b][:, t, :], in1=prev[b][:, t, :], op=ALU.subtract)
-            nc.gpsimd.tensor_tensor(out=diff[b][:, t, :], in0=diff[b][:, t, :], in1=share[s][:], op=ALU.mult)
-
-        def pick_last(s, window):
             b, t = divmod(s, PACK)
             halves = [(slice(HALF * h, HALF * (h + 1)), slice(16 * h, 16 * (h + 1))) for h in range(2)]
             for cols, entries in halves:
@@ -189,9 +178,9 @@ def tile_list_sourdough_order_blend_kernel(
 
         def blend(b, cols):
             nc.vector.tensor_tensor(
-                out=z_bf[b][:, cols, :].rearrange("p (c i) t -> p c t i", i=2),
-                in0=diff[b][:, :, cols].rearrange("p t (c i) -> p c t i", i=2),
-                in1=prev[b][:, :, cols].rearrange("p t (c i) -> p c t i", i=2),
+                out=z_bf[b][:, cols, :].rearrange("p (c i) t -> p c t i", i=4),
+                in0=diff[b][:, :, cols].rearrange("p t (c i) -> p c t i", i=4),
+                in1=prev[b][:, :, cols].rearrange("p t (c i) -> p c t i", i=4),
                 op=ALU.add,
             )
 
@@ -224,21 +213,21 @@ def tile_list_sourdough_order_blend_kernel(
         for s in range(1, PACK):
             dough[s] = first_stage(s, False, on_scalar)
         for s in range(8):
-            if s < 7:
-                pick(s, dough[s])
-            else:
-                pick_last(s, dough[s])
-            if s < 2:
-                prepare_wd(s, 1, nc.scalar.copy)
+            pick(s, dough[s])
             if PACK <= s + 2 < 8:
                 dough[s + 2] = first_stage(s + 2, False, on_scalar)
             if s + 2 < 8:
                 share_of(s + 2, first_stage(s + 2, True, on_scalar))
-            if s == 4:
+            if s == 1:
+                for a in range(2):
+                    prepare_wd(a, 1, nc.scalar.copy)
+            if s == 3:
+                z_bf[0] = keep.tile([P, M, PACK], BF16, name="z_bf0", tag="wd_bf11", align_bytes=64)
                 for h in range(2):
                     blend(0, slice(HALF * h, HALF * (h + 1)))
                 for h in range(2):
                     quantize_z(0, h)
+        z_bf[1] = keep.tile([P, M, PACK], BF16, name="z_bf1", tag="wd_bf01", align_bytes=64)
         blend(1, slice(0, HALF))
         blend(1, slice(HALF, HALF + P))
         quantize_z(1, 0)

@@ -1,6 +1,7 @@
 from contextlib import ExitStack
 
 import concourse.mybir as mybir
+from concourse.masks import make_identity
 
 K, H, N, T, S, M = 1024, 1024, 512, 4096, 1024, 512
 FLOPS = 2 * (2 * K * H * S + H * N * M)
@@ -54,16 +55,19 @@ def tile_list_sourdough_order_blend_kernel(
         nc.vector.memset(w4_sc_raw[:].bitcast(I32), 0)
         nc.vector.memset(v_sc[:].bitcast(I32), 0)
 
-        warm = keep.tile([P, 2], F32, name="warm")
-        nc.vector.memset(warm[:, 0:1], 0.0)
-        nc.scalar.activation(out=warm[:, 1:2], in_=warm[:, 0:1], func=ACT.Sigmoid)
-
         load_scale_rows(nc.gpsimd, w4_sc_raw, w4_scales)
 
-        def load_wd(dst, a, b):
-            nc.sync.dma_start(
-                out=dst, in_=wd[a * PASS : (a + 1) * PASS, b * PASS : (b + 1) * PASS].rearrange("(p j) c -> p j c", j=PACK)
-            )
+        wd_raw = {}
+
+        def load_wd(staging, a, b, parts):
+            width = PASS // parts
+            wd_raw[a, b] = []
+            for i in range(parts):
+                first = PACK * (a * PASS + i * width)
+                raw = staging[:, first : first + PACK * width].rearrange("p (j c) -> p j c", j=PACK)
+                cols = slice(b * PASS + i * width, b * PASS + (i + 1) * width)
+                nc.sync.dma_start(out=raw, in_=wd[a * PASS : (a + 1) * PASS, cols].rearrange("(p j) c -> p j c", j=PACK))
+                wd_raw[a, b].append(raw)
 
         def load_table(dst, a):
             nc.sync.dma_start(out=dst[:].bitcast(I32), in_=tab_words[a].rearrange("p n t -> p (n t)").bitcast(I32))
@@ -77,7 +81,6 @@ def tile_list_sourdough_order_blend_kernel(
         nc.sync.dma_start(pos3_sb[:], pos3)
         tab0 = keep.tile([P, T], U32, name="tab0", tag="early_table", align_bytes=64)
         load_table(tab0, 0)
-        wd_raw = {}
 
         picked_sc = keep.tile([P, S], U8, name="picked_sc", tag="picked_sc", align_bytes=64)
         nc.vector.tensor_copy(out=picked_sc[:], in_=tab_sc[:].indirect(offs_sb[:]))
@@ -99,8 +102,7 @@ def tile_list_sourdough_order_blend_kernel(
             )
         early_raw = keep.tile([P, 2 * PACK * PASS], F32, name="early_raw", tag="wd_raw1", align_bytes=64)
         for a in range(2):
-            wd_raw[a, 0] = early_raw[:, a * PACK * PASS : (a + 1) * PACK * PASS].rearrange("p (j c) -> p j c", j=PACK)
-            load_wd(wd_raw[a, 0], a, 0)
+            load_wd(early_raw, a, 0, 1 + a)
         v = {}
         for h in range(2):
             v[0, h] = keep.tile([P, BANK], U32, name="v0%d" % h, align_bytes=64)
@@ -117,7 +119,12 @@ def tile_list_sourdough_order_blend_kernel(
         def prepare_wd(a, b, copy):
             pieces = [(slice(0, 2 * P), slice(0, 2)), (slice(2 * P, PASS), slice(2, 4))] if (a, b) == (1, 0) else [(slice(0, PASS), slice(0, 4))]
             grouped = keep.tile([P, PACK, P, PACK], BF16, name="wd_bf", tag="wd_bf%d%d" % (a, b), align_bytes=64)
-            copy(out=grouped[:].rearrange("p t m j -> p m j t"), in_=wd_raw[a, b].rearrange("p j (m t) -> p m j t", t=PACK))
+            rows = P // len(wd_raw[a, b])
+            for i, raw in enumerate(wd_raw[a, b]):
+                copy(
+                    out=grouped[:, :, rows * i : rows * (i + 1), :].rearrange("p t m j -> p m j t"),
+                    in_=raw.rearrange("p j (m t) -> p m j t", t=PACK),
+                )
             wq[a, b] = keep.tile([P, PASS], U32, name="wq%d%d" % (a, b), align_bytes=64)
             wq_sc[a, b] = keep.tile([P, PASS], U8, name="wq_sc%d%d" % (a, b), align_bytes=64)
             for cols, ts in pieces:
@@ -154,9 +161,13 @@ def tile_list_sourdough_order_blend_kernel(
             return window
 
         share = {}
-        prev = [keep.tile([P, PACK, M], F32, name="prev%d" % b) for b in range(2)]
-        diff = [keep.tile([P, PACK, M], F32, name="diff%d" % b) for b in range(2)]
-        z_bf = {}
+        prev = {}
+        diff = {}
+        prev_last = keep.tile([P, PACK, M], F32, name="prev_last")
+        diff_last = keep.tile([P, PACK, M], F32, name="diff_last")
+        z_bf = [keep.tile([P, M, PACK], BF16, name="z_bf%d" % b, align_bytes=64) for b in range(2)]
+        ident = keep.tile([P, P], F32, name="ident", align_bytes=64)
+        make_identity(nc, ident[:])
         zq = [keep.tile([P, M], U32, name="zq%d" % b, align_bytes=64) for b in range(2)]
         zq_sc = [keep.tile([P, M], U8, name="zq_sc%d" % b, align_bytes=64) for b in range(2)]
 
@@ -166,23 +177,51 @@ def tile_list_sourdough_order_blend_kernel(
 
         def pick(s, window):
             b, t = divmod(s, PACK)
+            if b == 0:
+                pair = keep.tile([P, 2, M], F32, name="pair", tag="wd_bf11" if t == 3 else "pair%d" % t, align_bytes=64)
+                prev[s], diff[s] = pair[:, 0, :], pair[:, 1, :]
+            else:
+                prev[s], diff[s] = prev_last[:, t, :], diff_last[:, t, :]
             halves = [(slice(HALF * h, HALF * (h + 1)), slice(16 * h, 16 * (h + 1))) for h in range(2)]
             for cols, entries in halves:
-                nc.vector.tensor_copy(out=prev[b][:, t, cols], in_=window[:].indirect(pos3_sb[:, entries]))
+                nc.vector.tensor_copy(out=prev[s][:, cols], in_=window[:].indirect(pos3_sb[:, entries]))
             for cols, entries in halves:
                 nc.vector.tensor_tensor(
-                    out=diff[b][:, t, cols], in0=window[:].indirect(pos2_sb[:, entries]), in1=prev[b][:, t, cols], op=ALU.subtract
+                    out=diff[s][:, cols], in0=window[:].indirect(pos2_sb[:, entries]), in1=prev[s][:, cols], op=ALU.subtract
                 )
             for cols, entries in halves:
-                nc.vector.tensor_tensor(out=diff[b][:, t, cols], in0=diff[b][:, t, cols], in1=share[s][:, cols], op=ALU.mult)
+                nc.vector.tensor_tensor(out=diff[s][:, cols], in0=diff[s][:, cols], in1=share[s][:, cols], op=ALU.mult)
 
-        def blend(b, cols):
+        def blend_on_vector(cols):
             nc.vector.tensor_tensor(
-                out=z_bf[b][:, cols, :].rearrange("p (c i) t -> p c t i", i=4),
-                in0=diff[b][:, :, cols].rearrange("p t (c i) -> p c t i", i=4),
-                in1=prev[b][:, :, cols].rearrange("p t (c i) -> p c t i", i=4),
+                out=z_bf[1][:, cols, :].rearrange("p (c i) t -> p c t i", i=4),
+                in0=diff_last[:, :, cols].rearrange("p t (c i) -> p c t i", i=4),
+                in1=prev_last[:, :, cols].rearrange("p t (c i) -> p c t i", i=4),
                 op=ALU.add,
             )
+
+        def blend_on_tensor():
+            turned = []
+            for c in range(M // P):
+                acc = bank()
+                for t in range(PACK):
+                    for i, term in enumerate((prev[t], diff[t])):
+                        nc.tensor.matmul(
+                            out=acc[:, P * t : P * (t + 1)], lhsT=term[:, P * c : P * (c + 1)], rhs=ident[:],
+                            is_transpose=True, start=(i == 0), stop=(i == 1),
+                        )
+                turned.append(keep.tile([P, P, PACK], BF16, name="turned%d" % c, align_bytes=64))
+                nc.scalar.copy(out=turned[c][:], in_=acc[:].rearrange("m (t p) -> m p t", t=PACK))
+            for h in range(2):
+                acc = bank()
+                for i in range(2):
+                    words = turned[2 * h + i][:].rearrange("m p t -> m (p t)").bitcast(F32)
+                    for u in range(2):
+                        nc.tensor.transpose(acc[:, P * (2 * i + u) : P * (2 * i + u + 1)], words[:, u : 2 * P : 2], ident[:])
+                nc.scalar.copy(
+                    out=z_bf[0][:, HALF * h : HALF * (h + 1), :].rearrange("p m t -> p (m t)").bitcast(F32).rearrange("p (i m u) -> p i m u", i=2, u=2),
+                    in_=acc[:].rearrange("p (i u m) -> p i m u", i=2, u=2),
+                )
 
         def quantize_z(b, h):
             cols = slice(HALF * h, HALF * (h + 1))
@@ -197,8 +236,7 @@ def tile_list_sourdough_order_blend_kernel(
         nc.sync.dma_start(out=w8[:].bitcast(I32), in_=w8_words.rearrange("a p n t -> p a (n t)").bitcast(I32))
         late_raw = keep.tile([P, 2 * PACK * PASS], F32, name="late_raw", tag="late_table", align_bytes=64)
         for a in range(2):
-            wd_raw[a, 1] = late_raw[:, a * PACK * PASS : (a + 1) * PACK * PASS].rearrange("p (j c) -> p j c", j=PACK)
-            load_wd(wd_raw[a, 1], a, 1)
+            load_wd(late_raw, a, 1, 1)
         w8_sc = keep.tile([P, 2, N], U8, name="w8_sc", tag="picked_sc", align_bytes=64)
         nc.gpsimd.memset(w8_sc[:].bitcast(I32), 0)
         load_scale_rows(nc.sync, w8_sc, w8_scales)
@@ -214,24 +252,21 @@ def tile_list_sourdough_order_blend_kernel(
             dough[s] = first_stage(s, False, on_scalar)
         for s in range(8):
             pick(s, dough[s])
+            if s == 1:
+                prepare_wd(0, 1, nc.vector.tensor_copy)
+                prepare_wd(1, 1, nc.scalar.copy)
             if PACK <= s + 2 < 8:
                 dough[s + 2] = first_stage(s + 2, False, on_scalar)
             if s + 2 < 8:
                 share_of(s + 2, first_stage(s + 2, True, on_scalar))
-            if s == 1:
-                for a in range(2):
-                    prepare_wd(a, 1, nc.scalar.copy)
-            if s == 3:
-                z_bf[0] = keep.tile([P, M, PACK], BF16, name="z_bf0", tag="wd_bf11", align_bytes=64)
-                for h in range(2):
-                    blend(0, slice(HALF * h, HALF * (h + 1)))
+            if s == 5:
+                blend_on_tensor()
                 for h in range(2):
                     quantize_z(0, h)
-        z_bf[1] = keep.tile([P, M, PACK], BF16, name="z_bf1", tag="wd_bf01", align_bytes=64)
-        blend(1, slice(0, HALF))
-        blend(1, slice(HALF, HALF + P))
+        blend_on_vector(slice(0, HALF))
+        blend_on_vector(slice(HALF, HALF + P))
         quantize_z(1, 0)
-        blend(1, slice(HALF + P, M))
+        blend_on_vector(slice(HALF + P, M))
         quantize_z(1, 1)
         for h in range(2):
             cols = slice(HALF * h, HALF * (h + 1))
@@ -243,7 +278,7 @@ def tile_list_sourdough_order_blend_kernel(
                         out=acc[:, :HALF], lhsT=w8[:, b, P * c : P * (c + 1)].bitcast(FP8X4), lhsT_scale=w8_sc[:, b, P * c : P * (c + 1)],
                         rhs=zq[b][:, cols].bitcast(FP8X4), rhs_scale=zq_sc[b][:, cols], start=(b == 0), stop=(b == 1),
                     )
-                if h == 1 and c % 2 == 1:
+                if h == 1 and c > 0:
                     nc.vector.tensor_scalar(out=result[:, c, :], in0=acc[:, :HALF], scalar1=bias[:, c : c + 1], scalar2=None, op0=ALU.add)
                 else:
                     nc.scalar.activation(out=result[:, c, :], in_=acc[:, :HALF], func=ACT.Identity, bias=bias[:, c : c + 1])

@@ -21,7 +21,9 @@ P = 128
 PACK = 4
 PASS = P * PACK
 BANK = 512
-HALF = M // 2
+SLICES = H // P
+WD_PIECES = (128, 128, 256, 512)
+LAST_PIECES = (256, 128, 128)
 
 
 def load_scale_rows(queue, plane, scales):
@@ -39,6 +41,7 @@ def tile_list_sourdough_order_blend_kernel(
     with ExitStack() as ctx:
         lists = ctx.enter_context(tc.tile_pool(name="lists", bufs=1))
         keep = ctx.enter_context(tc.tile_pool(name="keep", bufs=1))
+        arena = ctx.enter_context(tc.tile_pool(name="arena", bufs=1))
         ring = ctx.enter_context(tc.tile_pool(name="ring", bufs=2))
         psum = ctx.enter_context(tc.psum_pool(name="psum", bufs=1))
 
@@ -47,90 +50,110 @@ def tile_list_sourdough_order_blend_kernel(
         pos2_sb = lists.tile([P, M // 16], U16, name="pos2_sb")
         pos3_sb = lists.tile([P, M // 16], U16, name="pos3_sb")
 
-        tab_sc = keep.tile([P, T], U8, name="tab_sc", tag="late_table", align_bytes=64)
-        w4_sc_raw = keep.tile([P, 2, H], U8, name="w4_sc_raw", tag="w4_sc_raw", align_bytes=64)
+        arena_bytes = 64 * 1024
+        tab_sc = arena.tile([P, arena_bytes], U8, name="tab_sc", align_bytes=64, offset=0)
+        placed = [0]
+
+        def late_tile(shape, dtype, size, name):
+            tile = arena.tile(shape, dtype, name=name, align_bytes=64, offset=placed[-1])
+            placed.append(placed[-1] + size)
+            return tile
+
+        w4_sc = keep.tile([P, 2, H], U8, name="w4_sc", align_bytes=64)
         v_sc = keep.tile([P, 2, S], U8, name="v_sc", align_bytes=64)
-        nc.gpsimd.memset(tab_sc[:, : T // 2].bitcast(I32), 0)
-        nc.vector.memset(tab_sc[:, T // 2 :].bitcast(I32), 0)
-        nc.vector.memset(w4_sc_raw[:].bitcast(I32), 0)
+        nc.vector.memset(tab_sc[32:64, :T].bitcast(I32), 0)
+        nc.vector.memset(tab_sc[64:P, :T].bitcast(I32), 0)
+        ident = keep.tile([P, P], F32, name="ident", align_bytes=64)
+        make_identity(nc, ident[:])
+        nc.vector.memset(w4_sc[:].bitcast(I32), 0)
+        load_scale_rows(nc.gpsimd, w4_sc, w4_scales)
         nc.vector.memset(v_sc[:].bitcast(I32), 0)
 
-        load_scale_rows(nc.gpsimd, w4_sc_raw, w4_scales)
-
-        wd_raw = {}
-
-        def load_wd(staging, a, b, parts):
-            width = PASS // parts
-            wd_raw[a, b] = []
-            for i in range(parts):
-                first = PACK * (a * PASS + i * width)
-                raw = staging[:, first : first + PACK * width].rearrange("p (j c) -> p j c", j=PACK)
-                cols = slice(b * PASS + i * width, b * PASS + (i + 1) * width)
-                nc.sync.dma_start(out=raw, in_=wd[a * PASS : (a + 1) * PASS, cols].rearrange("(p j) c -> p j c", j=PACK))
-                wd_raw[a, b].append(raw)
-
-        def load_table(dst, a):
-            nc.sync.dma_start(out=dst[:].bitcast(I32), in_=tab_words[a].rearrange("p n t -> p (n t)").bitcast(I32))
-
         nc.sync.dma_start(offs_sb[:], offs)
-        nc.sync.dma_start(out=tab_sc[0:P:4, :].bitcast(I32), in_=tab_scales.rearrange("a q t -> (a q) t").bitcast(I32))
-        w4_raw = keep.tile([P, 2, 2 * H], U8, name="w4_raw", tag="wd_raw1", align_bytes=64)
-        nc.sync.dma_start(out=w4_raw[:].bitcast(I32), in_=w4_words.rearrange("a p c -> p a c").bitcast(I32))
+        nc.sync.dma_start(out=tab_sc[0:32, :T].bitcast(I32), in_=tab_scales.rearrange("a q t -> (a q) t").bitcast(I32))
         nc.sync.dma_start(pos1_sb[:], pos1)
-        nc.sync.dma_start(pos2_sb[:], pos2)
         nc.sync.dma_start(pos3_sb[:], pos3)
-        tab0 = keep.tile([P, T], U32, name="tab0", tag="early_table", align_bytes=64)
-        load_table(tab0, 0)
+        nc.sync.dma_start(pos2_sb[:], pos2)
+        tab = {}
 
-        picked_sc = keep.tile([P, S], U8, name="picked_sc", tag="picked_sc", align_bytes=64)
-        nc.vector.tensor_copy(out=picked_sc[:], in_=tab_sc[:].indirect(offs_sb[:]))
-        tab1 = keep.tile([P, T], U32, name="tab1", tag="late_table", align_bytes=64)
+        def load_table(a):
+            nc.sync.dma_start(out=tab[a][:].bitcast(I32), in_=tab_words[a].rearrange("p n t -> p (n t)").bitcast(I32))
+
+        tab[0] = keep.tile([P, T], U32, name="tab0", align_bytes=64)
+        load_table(0)
+        w4 = {0: keep.tile([P, 2, 2 * PASS], U8, name="w4_0", align_bytes=64)}
+
+        def load_w4(b):
+            nc.sync.dma_start(
+                out=w4[b][:].bitcast(I32), in_=w4_words[:, :, 2 * PASS * b : 2 * PASS * (b + 1)].rearrange("a p c -> p a c").bitcast(I32)
+            )
+
+        load_w4(0)
+        warm = keep.tile([P, 1], F32, name="warm")
+        nc.scalar.activation(out=warm[:], in_=ident[:, 0:1], func=ACT.Sigmoid)
+
+        picked_sc = keep.tile([P, S], U8, name="picked_sc", align_bytes=64)
+        nc.vector.tensor_copy(out=picked_sc[:], in_=tab_sc[:, :T].indirect(offs_sb[:]))
         for a in range(2):
-            for r in range(4):
-                if (a, r) == (1, 0):
-                    load_table(tab1, 1)
+            for q in range(4):
+                if (a, q) == (1, 0):
+                    tab[1] = late_tile([P, T], U32, 4 * T, "tab1")
+                    load_table(1)
                 nc.sync.dma_start(
-                    out=v_sc[r:P:32, a, :].bitcast(I32), in_=picked_sc[64 * a + 4 * r : 64 * a + 64 : 16, :].bitcast(I32)
+                    out=v_sc[32 * q : 32 * q + 4, a, :].bitcast(I32), in_=picked_sc[16 * a + 4 * q : 16 * a + 4 * q + 4, :].bitcast(I32)
                 )
 
-        w4 = keep.tile([P, 2, 2 * H], U8, name="w4", align_bytes=64)
-        w4_sc = keep.tile([P, 2, H], U8, name="w4_sc", align_bytes=64)
-        for a in range(2):
-            nc.vector.tensor_copy(
-                out=w4[:, a, :].bitcast(U16).rearrange("p (b t m) -> p b m t", b=2, t=PACK),
-                in_=w4_raw[:, a, :].bitcast(U16).rearrange("p (b m t) -> p b m t", b=2, t=PACK),
-            )
-        early_raw = keep.tile([P, 2 * PACK * PASS], F32, name="early_raw", tag="wd_raw1", align_bytes=64)
-        for a in range(2):
-            load_wd(early_raw, a, 0, 1 + a)
+        wd_raw = {}
+        starts = [sum(WD_PIECES[:i]) for i in range(len(WD_PIECES))]
+
+        def load_wd(i):
+            width = WD_PIECES[i]
+            for a in range(2):
+                wd_raw[i, a] = late_tile([P, PACK, width], F32, 4 * PACK * width, "wd_raw%d%d" % (i, a))
+                nc.sync.dma_start(
+                    out=wd_raw[i, a][:],
+                    in_=wd[a * PASS : (a + 1) * PASS, starts[i] : starts[i] + width].rearrange("(p j) c -> p j c", j=PACK),
+                )
+
+        load_wd(0)
+        load_wd(1)
+        load_wd(2)
+        w4[1] = late_tile([P, 2, 2 * PASS], U8, 4 * PASS, "w4_1")
+        load_w4(1)
+        load_wd(3)
+        w8 = late_tile([P, 2, N], U32, 8 * N, "w8")
+        nc.sync.dma_start(out=w8[:].bitcast(I32), in_=w8_words.rearrange("a p n t -> p a (n t)").bitcast(I32))
+        w8_sc = late_tile([P, 2, N], U8, 2 * N, "w8_sc")
+        nc.vector.memset(w8_sc[:].bitcast(I32), 0)
+        load_scale_rows(nc.sync, w8_sc, w8_scales)
+        bias = late_tile([P, N // P], F32, 64, "bias")
+        with nc.allow_non_contiguous_dma(reason="one bias value a partition and output tile"):
+            nc.sync.dma_start(out=bias[:], in_=crumb0.rearrange("(c p) -> p c", p=P))
+
         v = {}
-        for h in range(2):
-            v[0, h] = keep.tile([P, BANK], U32, name="v0%d" % h, align_bytes=64)
-            nc.vector.tensor_copy(out=v[0, h][:], in_=tab0[:].indirect(offs_sb[:, 32 * h : 32 * h + 32]))
         for a in range(2):
-            nc.vector.tensor_copy(
-                out=w4_sc[:, a, :].rearrange("p (b t m) -> p b m t", b=2, t=PACK),
-                in_=w4_sc_raw[:, a, :].rearrange("p (b m t) -> p b m t", b=2, t=PACK),
-            )
+            for h in range(2):
+                v[a, h] = keep.tile([P, BANK], U32, name="v%d%d" % (a, h), align_bytes=64)
+                nc.vector.tensor_copy(out=v[a, h][:], in_=tab[a][:].indirect(offs_sb[:, 32 * h : 32 * h + 32]))
 
         wq = {}
         wq_sc = {}
 
-        def prepare_wd(a, b, copy):
-            pieces = [(slice(0, 2 * P), slice(0, 2)), (slice(2 * P, PASS), slice(2, 4))] if (a, b) == (1, 0) else [(slice(0, PASS), slice(0, 4))]
-            grouped = keep.tile([P, PACK, P, PACK], BF16, name="wd_bf", tag="wd_bf%d%d" % (a, b), align_bytes=64)
-            rows = P // len(wd_raw[a, b])
-            for i, raw in enumerate(wd_raw[a, b]):
-                copy(
-                    out=grouped[:, :, rows * i : rows * (i + 1), :].rearrange("p t m j -> p m j t"),
-                    in_=raw.rearrange("p j (m t) -> p m j t", t=PACK),
+        def prepare_wd(s):
+            i = max(n for n in range(len(starts)) if starts[n] <= P * s)
+            cols = slice(P * s - starts[i], P * (s + 1) - starts[i])
+            grouped = keep.tile([P, 2, P, PACK], BF16, name="wd_bf%d" % s, tag="dough%d" % (s - 2), align_bytes=64)
+            for a in range(2):
+                nc.vector.tensor_copy(
+                    out=grouped[:, a, :, :].rearrange("p (c i) j -> p c j i", i=4),
+                    in_=wd_raw[i, a][:, :, cols].rearrange("p j (c i) -> p c j i", i=4),
                 )
-            wq[a, b] = keep.tile([P, PASS], U32, name="wq%d%d" % (a, b), align_bytes=64)
-            wq_sc[a, b] = keep.tile([P, PASS], U8, name="wq_sc%d%d" % (a, b), align_bytes=64)
-            for cols, ts in pieces:
-                nc.vector.quantize_mx(
-                    out=wq[a, b][:, cols].bitcast(FP8X4), scales=wq_sc[a, b][:, cols], in_=grouped[:, ts, :, :].rearrange("p t m j -> p (t m j)")
-                )
+            for a in range(2):
+                codes = keep.tile([P, P], U32, name="wq%d%d" % (s, a), align_bytes=64)
+                plane = keep.tile([P, P], U8, name="wq_sc%d%d" % (s, a), align_bytes=64)
+                nc.vector.quantize_mx(out=codes[:].bitcast(FP8X4), scales=plane[:], in_=grouped[:, a, :, :].rearrange("p c j -> p (c j)"))
+                wq[a, s] = codes[:]
+                wq_sc[a, s] = plane[:]
 
         banks_taken = []
 
@@ -138,151 +161,165 @@ def tile_list_sourdough_order_blend_kernel(
             banks_taken.append(psum.tile([P, BANK], F32, name="acc%d" % (len(banks_taken) % 8)))
             return banks_taken[-1]
 
-        def first_stage(s, is_act, copies):
+        def first_stage(s, is_act, copy):
             b, t = divmod(s, PACK)
-            if is_act or s > 1:
-                window = ring.tile([P, S], F32, name="act_w" if is_act else "dough_w", bufs=2 if is_act else 3)
+            if is_act:
+                window = ring.tile([P, S], F32, name="act_w", bufs=2)
             else:
-                window = keep.tile([P, S], F32, name="first_dough_w", tag="wd_bf%d1" % s, align_bytes=64)
+                window = keep.tile([P, S], F32, name="dough_w%d" % s, tag="dough%d" % s, align_bytes=64)
             for h in range(2):
                 acc = bank()
                 for a in range(2):
                     if is_act:
-                        lhs = w4[:, a, 2 * P * s : 2 * P * (s + 1)].bitcast(FP4X4)
+                        lhs = w4[b][:, a, 2 * P * t : 2 * P * (t + 1)].bitcast(FP4X4)
                         lhs_sc = w4_sc[:, a, P * s : P * (s + 1)]
                     else:
-                        lhs = wq[a, b][:, P * t : P * (t + 1)].bitcast(FP8X4)
-                        lhs_sc = wq_sc[a, b][:, P * t : P * (t + 1)]
+                        lhs = wq[a, s].bitcast(FP8X4)
+                        lhs_sc = wq_sc[a, s]
                     nc.tensor.matmul_mx(
                         out=acc[:], lhsT=lhs, lhsT_scale=lhs_sc, rhs=v[a, h][:].bitcast(FP8X4),
                         rhs_scale=v_sc[:, a, BANK * h : BANK * (h + 1)], start=(a == 0), stop=(a == 1),
                     )
-                copies[h](out=window[:, BANK * h : BANK * (h + 1)], in_=acc[:])
+                copy[h](out=window[:, BANK * h : BANK * (h + 1)], in_=acc[:])
             return window
 
+        on_scalar = (nc.scalar.copy, nc.scalar.copy)
         share = {}
+        dough = {}
         prev = {}
         diff = {}
-        prev_last = keep.tile([P, PACK, M], F32, name="prev_last")
-        diff_last = keep.tile([P, PACK, M], F32, name="diff_last")
+        tiles = M // P
+        turned = [keep.tile([P, 2, tiles, P, 2], BF16, name="turned%d" % b, align_bytes=64) for b in range(2)]
         z_bf = [keep.tile([P, M, PACK], BF16, name="z_bf%d" % b, align_bytes=64) for b in range(2)]
-        ident = keep.tile([P, P], F32, name="ident", align_bytes=64)
-        make_identity(nc, ident[:])
         zq = [keep.tile([P, M], U32, name="zq%d" % b, align_bytes=64) for b in range(2)]
         zq_sc = [keep.tile([P, M], U8, name="zq_sc%d" % b, align_bytes=64) for b in range(2)]
 
-        def share_of(s, window):
-            share[s] = ring.tile([P, M], F32, name="share", bufs=6)
+        def make_share(s):
+            window = first_stage(s, True, on_scalar)
+            share[s] = ring.tile([P, M], F32, name="share", bufs=4)
             nc.scalar.activation(out=share[s][:], in_=window[:].indirect(pos1_sb[:]), func=ACT.Sigmoid)
 
-        def pick(s, window):
-            b, t = divmod(s, PACK)
-            if b == 0:
-                pair = keep.tile([P, 2, M], F32, name="pair", tag="wd_bf11" if t == 3 else "pair%d" % t, align_bytes=64)
-                prev[s], diff[s] = pair[:, 0, :], pair[:, 1, :]
-            else:
-                prev[s], diff[s] = prev_last[:, t, :], diff_last[:, t, :]
-            halves = [(slice(HALF * h, HALF * (h + 1)), slice(16 * h, 16 * (h + 1))) for h in range(2)]
-            for cols, entries in halves:
-                nc.vector.tensor_copy(out=prev[s][:, cols], in_=window[:].indirect(pos3_sb[:, entries]))
-            for cols, entries in halves:
-                nc.vector.tensor_tensor(
-                    out=diff[s][:, cols], in0=window[:].indirect(pos2_sb[:, entries]), in1=prev[s][:, cols], op=ALU.subtract
-                )
-            for cols, entries in halves:
-                nc.vector.tensor_tensor(out=diff[s][:, cols], in0=diff[s][:, cols], in1=share[s][:, cols], op=ALU.mult)
+        def make_dough(s, copy):
+            dough[s] = first_stage(s, False, copy)
+            prev[s] = ring.tile([P, M], F32, name="prev", bufs=3)
+            diff[s] = ring.tile([P, M], F32, name="diff", bufs=3)
 
-        def blend_on_vector(cols):
+        def entries(cols):
+            return slice(cols.start // 16, cols.stop // 16)
+
+        def pick_prev(s, cols):
+            nc.vector.tensor_copy(out=prev[s][:, cols], in_=dough[s][:].indirect(pos3_sb[:, entries(cols)]))
+
+        def pick_diff(s, cols):
             nc.vector.tensor_tensor(
-                out=z_bf[1][:, cols, :].rearrange("p (c i) t -> p c t i", i=4),
-                in0=diff_last[:, :, cols].rearrange("p t (c i) -> p c t i", i=4),
-                in1=prev_last[:, :, cols].rearrange("p t (c i) -> p c t i", i=4),
-                op=ALU.add,
+                out=diff[s][:, cols], in0=dough[s][:].indirect(pos2_sb[:, entries(cols)]), in1=prev[s][:, cols], op=ALU.subtract
             )
 
-        def blend_on_tensor():
-            turned = []
-            for c in range(M // P):
-                acc = bank()
-                for t in range(PACK):
-                    for i, term in enumerate((prev[t], diff[t])):
-                        nc.tensor.matmul(
-                            out=acc[:, P * t : P * (t + 1)], lhsT=term[:, P * c : P * (c + 1)], rhs=ident[:],
-                            is_transpose=True, start=(i == 0), stop=(i == 1),
-                        )
-                turned.append(keep.tile([P, P, PACK], BF16, name="turned%d" % c, align_bytes=64))
-                nc.scalar.copy(out=turned[c][:], in_=acc[:].rearrange("m (t p) -> m p t", t=PACK))
-            for h in range(2):
-                acc = bank()
-                for i in range(2):
-                    words = turned[2 * h + i][:].rearrange("m p t -> m (p t)").bitcast(F32)
-                    for u in range(2):
-                        nc.tensor.transpose(acc[:, P * (2 * i + u) : P * (2 * i + u + 1)], words[:, u : 2 * P : 2], ident[:])
-                nc.scalar.copy(
-                    out=z_bf[0][:, HALF * h : HALF * (h + 1), :].rearrange("p m t -> p (m t)").bitcast(F32).rearrange("p (i m u) -> p i m u", i=2, u=2),
-                    in_=acc[:].rearrange("p (i u m) -> p i m u", i=2, u=2),
-                )
+        def weigh(s, cols):
+            nc.vector.tensor_tensor(out=diff[s][:, cols], in0=diff[s][:, cols], in1=share[s][:, cols], op=ALU.mult)
 
-        def quantize_z(b, h):
-            cols = slice(HALF * h, HALF * (h + 1))
+        def turn(s, cols):
+            b, t = divmod(s, PACK)
+            first, last = cols.start // P, cols.stop // P
+            acc = bank()
+            for c in range(first, last):
+                for i, term in enumerate((prev[s], diff[s])):
+                    nc.tensor.matmul(
+                        out=acc[:, P * (c - first) : P * (c - first + 1)], lhsT=term[:, P * c : P * (c + 1)], rhs=ident[:],
+                        is_transpose=True, start=(i == 0), stop=(i == 1),
+                    )
+            nc.scalar.copy(
+                out=turned[b][:, :, first:last, 32 * t : 32 * (t + 1), :],
+                in_=acc[:, : P * (last - first)].rearrange("m (c q u e) -> m u c q e", q=32, u=2, e=2),
+            )
+
+        def turn_back(b, cols):
+            first, last = cols.start // P, cols.stop // P
+            acc = bank()
+            for c in range(first, last):
+                for u in range(2):
+                    words = turned[b][:, u, c, :, :].rearrange("m p e -> m (p e)").bitcast(F32)
+                    k = 2 * (c - first) + u
+                    nc.tensor.transpose(acc[:, P * k : P * (k + 1)], words, ident[:])
+            nc.scalar.copy(
+                out=z_bf[b][:, cols, :].rearrange("p m t -> p (m t)").bitcast(F32).rearrange("p (c m u) -> p c m u", m=P, u=2),
+                in_=acc[:, : 2 * P * (last - first)].rearrange("p (c u m) -> p c m u", u=2, m=P),
+            )
+
+        def quantize_z(b, cols):
             nc.vector.quantize_mx(
                 out=zq[b][:, cols].bitcast(FP8X4), scales=zq_sc[b][:, cols], in_=z_bf[b][:, cols, :].rearrange("p m t -> p (m t)")
             )
 
-        for h in range(2):
-            v[1, h] = keep.tile([P, BANK], U32, name="v1%d" % h, align_bytes=64)
-            nc.vector.tensor_copy(out=v[1, h][:], in_=tab1[:].indirect(offs_sb[:, 32 * h : 32 * h + 32]))
-        w8 = keep.tile([P, 2, N], U32, name="w8", tag="early_table", align_bytes=64)
-        nc.sync.dma_start(out=w8[:].bitcast(I32), in_=w8_words.rearrange("a p n t -> p a (n t)").bitcast(I32))
-        late_raw = keep.tile([P, 2 * PACK * PASS], F32, name="late_raw", tag="late_table", align_bytes=64)
-        for a in range(2):
-            load_wd(late_raw, a, 1, 1)
-        w8_sc = keep.tile([P, 2, N], U8, name="w8_sc", tag="picked_sc", align_bytes=64)
-        nc.gpsimd.memset(w8_sc[:].bitcast(I32), 0)
-        load_scale_rows(nc.sync, w8_sc, w8_scales)
-        bias = keep.tile([P, N // P], F32, name="bias", tag="w4_sc_raw", align_bytes=64)
-        with nc.allow_non_contiguous_dma(reason="one bias value a partition and output tile"):
-            nc.sync.dma_start(out=bias[:], in_=crumb0.rearrange("(c p) -> p c", p=P))
-        on_scalar = (nc.scalar.copy, nc.scalar.copy)
-        for s in range(2):
-            share_of(s, first_stage(s, True, on_scalar))
-            prepare_wd(s, 0, nc.vector.tensor_copy)
-        dough = {0: first_stage(0, False, (nc.vector.tensor_copy, nc.vector.tensor_copy))}
-        for s in range(1, PACK):
-            dough[s] = first_stage(s, False, on_scalar)
-        for s in range(8):
-            pick(s, dough[s])
-            if s == 1:
-                prepare_wd(0, 1, nc.vector.tensor_copy)
-                prepare_wd(1, 1, nc.scalar.copy)
-            if PACK <= s + 2 < 8:
-                dough[s + 2] = first_stage(s + 2, False, on_scalar)
-            if s + 2 < 8:
-                share_of(s + 2, first_stage(s + 2, True, on_scalar))
-            if s == 5:
-                blend_on_tensor()
-                for h in range(2):
-                    quantize_z(0, h)
-        blend_on_vector(slice(0, HALF))
-        blend_on_vector(slice(HALF, HALF + P))
-        quantize_z(1, 0)
-        blend_on_vector(slice(HALF + P, M))
-        quantize_z(1, 1)
-        for h in range(2):
-            cols = slice(HALF * h, HALF * (h + 1))
-            result = ring.tile([P, N // P, HALF], F32, name="result")
-            for c in range(N // P):
+        def finish(cols):
+            width = cols.stop - cols.start
+            result = ring.tile([P, N // P, width], F32, name="result%d" % cols.start, bufs=1)
+            for pair in range(2):
                 acc = bank()
-                for b in range(2):
-                    nc.tensor.matmul_mx(
-                        out=acc[:, :HALF], lhsT=w8[:, b, P * c : P * (c + 1)].bitcast(FP8X4), lhsT_scale=w8_sc[:, b, P * c : P * (c + 1)],
-                        rhs=zq[b][:, cols].bitcast(FP8X4), rhs_scale=zq_sc[b][:, cols], start=(b == 0), stop=(b == 1),
+                for i in range(2):
+                    c = 2 * pair + i
+                    for b in range(2):
+                        nc.tensor.matmul_mx(
+                            out=acc[:, width * i : width * (i + 1)], lhsT=w8[:, b, P * c : P * (c + 1)].bitcast(FP8X4),
+                            lhsT_scale=w8_sc[:, b, P * c : P * (c + 1)],
+                            rhs=zq[b][:, cols].bitcast(FP8X4), rhs_scale=zq_sc[b][:, cols], start=(b == 0), stop=(b == 1),
+                        )
+                if pair == 1:
+                    nc.vector.tensor_tensor(
+                        out=result[:, 2:4, :], in0=acc[:, : 2 * width].rearrange("p (c m) -> p c m", c=2),
+                        in1=bias[:, 2:4].unsqueeze(2).to_broadcast([P, 2, width]), op=ALU.add,
                     )
-                if h == 1 and c > 0:
-                    nc.vector.tensor_scalar(out=result[:, c, :], in0=acc[:, :HALF], scalar1=bias[:, c : c + 1], scalar2=None, op0=ALU.add)
                 else:
-                    nc.scalar.activation(out=result[:, c, :], in_=acc[:, :HALF], func=ACT.Identity, bias=bias[:, c : c + 1])
-                if c % 2 == 1:
-                    nc.sync.dma_start(
-                        out=out[P * (c - 1) : P * (c + 1), cols].rearrange("(c p) m -> p c m", p=P), in_=result[:, c - 1 : c + 1, :]
-                    )
+                    for c in range(2):
+                        nc.scalar.activation(
+                            out=result[:, c, :], in_=acc[:, width * c : width * (c + 1)], func=ACT.Identity, bias=bias[:, c : c + 1]
+                        )
+            nc.sync.dma_start(out=out[:, cols].rearrange("(c p) m -> p c m", p=P), in_=result[:])
+
+        whole = slice(0, M)
+        halves = [slice(0, M // 2), slice(M // 2, M)]
+        make_share(0)
+        prepare_wd(0)
+        prepare_wd(1)
+        make_dough(0, (nc.vector.tensor_copy, nc.scalar.copy))
+        make_share(1)
+        for s in range(SLICES - 1):
+            make_dough(s + 1, on_scalar)
+            for step in (pick_prev, pick_diff, weigh):
+                for cols in halves:
+                    step(s, cols)
+            if s + 2 < SLICES:
+                prepare_wd(s + 2)
+            if s > 0:
+                turn(s - 1, whole)
+            if s + 2 < SLICES:
+                make_share(s + 2)
+            if s == PACK + 1:
+                for cols in halves:
+                    turn_back(0, cols)
+        quantize_z(0, whole)
+        edges = [sum(LAST_PIECES[:i]) for i in range(len(LAST_PIECES) + 1)]
+        pieces = [slice(edges[i], edges[i + 1]) for i in range(len(LAST_PIECES))]
+        last = SLICES - 1
+        pick_prev(last, pieces[0])
+        turn(last - 1, whole)
+        pick_prev(last, pieces[1])
+        pick_diff(last, pieces[0])
+        pick_prev(last, pieces[2])
+        weigh(last, pieces[0])
+        pick_diff(last, pieces[1])
+        turn(last, pieces[0])
+        pick_diff(last, pieces[2])
+        weigh(last, pieces[1])
+        turn(last, pieces[1])
+        turn_back(1, pieces[0])
+        weigh(last, pieces[2])
+        turn(last, pieces[2])
+        turn_back(1, pieces[1])
+        quantize_z(1, pieces[0])
+        turn_back(1, pieces[2])
+        quantize_z(1, pieces[1])
+        finish(pieces[0])
+        quantize_z(1, pieces[2])
+        finish(pieces[1])
+        finish(pieces[2])

@@ -26,8 +26,8 @@ WD_PIECES = (128, 128, 256, 512)
 LAST_PIECES = (256, 128, 128)
 
 
-def load_scale_rows(queue, plane, scales):
-    for q in range(4):
+def load_scale_rows(queue, plane, scales, quadrants):
+    for q in quadrants:
         queue.dma_start(
             out=plane[32 * q : 32 * q + 4, :, :].bitcast(I32),
             in_=scales[:, 4 * q : 4 * q + 4, :].rearrange("a r c -> r a c").bitcast(I32),
@@ -60,14 +60,15 @@ def tile_list_sourdough_order_blend_kernel(
             return tile
 
         w4_sc = keep.tile([P, 2, H], U8, name="w4_sc", align_bytes=64)
-        v_sc = keep.tile([P, 2, S], U8, name="v_sc", align_bytes=64)
+        v_sc = [keep.tile([P, S], U8, name="v_sc%d" % a, align_bytes=64) for a in range(2)]
+        nc.vector.memset(w4_sc[:].bitcast(I32), 0)
         nc.vector.memset(tab_sc[32:64, :T].bitcast(I32), 0)
         nc.vector.memset(tab_sc[64:P, :T].bitcast(I32), 0)
+        load_scale_rows(nc.gpsimd, w4_sc, w4_scales, range(4))
+        for a in range(2):
+            nc.vector.memset(v_sc[a][:].bitcast(I32), 0)
         ident = keep.tile([P, P], F32, name="ident", align_bytes=64)
         make_identity(nc, ident[:])
-        nc.vector.memset(w4_sc[:].bitcast(I32), 0)
-        load_scale_rows(nc.gpsimd, w4_sc, w4_scales)
-        nc.vector.memset(v_sc[:].bitcast(I32), 0)
 
         nc.sync.dma_start(offs_sb[:], offs)
         nc.sync.dma_start(out=tab_sc[0:32, :T].bitcast(I32), in_=tab_scales.rearrange("a q t -> (a q) t").bitcast(I32))
@@ -81,16 +82,32 @@ def tile_list_sourdough_order_blend_kernel(
 
         tab[0] = keep.tile([P, T], U32, name="tab0", align_bytes=64)
         load_table(0)
-        w4 = {0: keep.tile([P, 2, 2 * PASS], U8, name="w4_0", align_bytes=64)}
+        w4 = {}
+        wd_raw = {}
+        starts = [sum(WD_PIECES[:i]) for i in range(len(WD_PIECES))]
+
+        def early_tile(shape, dtype, size, name):
+            return keep.tile(shape, dtype, name=name, align_bytes=64)
 
         def load_w4(b):
+            w4[b] = late_tile([P, 2, 2 * PASS], U8, 4 * PASS, "w4_%d" % b)
             nc.sync.dma_start(
                 out=w4[b][:].bitcast(I32), in_=w4_words[:, :, 2 * PASS * b : 2 * PASS * (b + 1)].rearrange("a p c -> p a c").bitcast(I32)
             )
 
-        load_w4(0)
+        def load_wd(i, place):
+            width = WD_PIECES[i]
+            for a in range(2):
+                wd_raw[i, a] = place([P, PACK, width], F32, 4 * PACK * width, "wd_raw%d%d" % (i, a))
+                nc.sync.dma_start(
+                    out=wd_raw[i, a][:],
+                    in_=wd[a * PASS : (a + 1) * PASS, starts[i] : starts[i] + width].rearrange("(p j) c -> p j c", j=PACK),
+                )
+
+        load_wd(0, early_tile)
         warm = keep.tile([P, 1], F32, name="warm")
-        nc.scalar.activation(out=warm[:], in_=ident[:, 0:1], func=ACT.Sigmoid)
+        nc.vector.memset(warm[:], 0.0)
+        nc.scalar.activation(out=warm[:], in_=warm[:], func=ACT.Sigmoid)
 
         picked_sc = keep.tile([P, S], U8, name="picked_sc", align_bytes=64)
         nc.vector.tensor_copy(out=picked_sc[:], in_=tab_sc[:, :T].indirect(offs_sb[:]))
@@ -100,53 +117,46 @@ def tile_list_sourdough_order_blend_kernel(
                     tab[1] = late_tile([P, T], U32, 4 * T, "tab1")
                     load_table(1)
                 nc.sync.dma_start(
-                    out=v_sc[32 * q : 32 * q + 4, a, :].bitcast(I32), in_=picked_sc[16 * a + 4 * q : 16 * a + 4 * q + 4, :].bitcast(I32)
+                    out=v_sc[a][32 * q : 32 * q + 4, :].bitcast(I32), in_=picked_sc[16 * a + 4 * q : 16 * a + 4 * q + 4, :].bitcast(I32)
                 )
 
-        wd_raw = {}
-        starts = [sum(WD_PIECES[:i]) for i in range(len(WD_PIECES))]
-
-        def load_wd(i):
-            width = WD_PIECES[i]
-            for a in range(2):
-                wd_raw[i, a] = late_tile([P, PACK, width], F32, 4 * PACK * width, "wd_raw%d%d" % (i, a))
-                nc.sync.dma_start(
-                    out=wd_raw[i, a][:],
-                    in_=wd[a * PASS : (a + 1) * PASS, starts[i] : starts[i] + width].rearrange("(p j) c -> p j c", j=PACK),
-                )
-
-        load_wd(0)
-        load_wd(1)
-        load_wd(2)
-        w4[1] = late_tile([P, 2, 2 * PASS], U8, 4 * PASS, "w4_1")
+        load_w4(0)
+        load_wd(1, late_tile)
+        load_wd(2, late_tile)
         load_w4(1)
-        load_wd(3)
+        load_wd(3, late_tile)
         w8 = late_tile([P, 2, N], U32, 8 * N, "w8")
         nc.sync.dma_start(out=w8[:].bitcast(I32), in_=w8_words.rearrange("a p n t -> p a (n t)").bitcast(I32))
         w8_sc = late_tile([P, 2, N], U8, 2 * N, "w8_sc")
         nc.vector.memset(w8_sc[:].bitcast(I32), 0)
-        load_scale_rows(nc.sync, w8_sc, w8_scales)
+        load_scale_rows(nc.sync, w8_sc, w8_scales, range(4))
         bias = late_tile([P, N // P], F32, 64, "bias")
         with nc.allow_non_contiguous_dma(reason="one bias value a partition and output tile"):
             nc.sync.dma_start(out=bias[:], in_=crumb0.rearrange("(c p) -> p c", p=P))
 
         v = {}
-        for a in range(2):
+
+        def gather_table(a):
             for h in range(2):
                 v[a, h] = keep.tile([P, BANK], U32, name="v%d%d" % (a, h), align_bytes=64)
                 nc.vector.tensor_copy(out=v[a, h][:], in_=tab[a][:].indirect(offs_sb[:, 32 * h : 32 * h + 32]))
 
         wq = {}
+        staged = {}
         wq_sc = {}
 
         def prepare_wd(s):
             i = max(n for n in range(len(starts)) if starts[n] <= P * s)
             cols = slice(P * s - starts[i], P * (s + 1) - starts[i])
-            grouped = keep.tile([P, 2, P, PACK], BF16, name="wd_bf%d" % s, tag="dough%d" % (s - 2), align_bytes=64)
+            if s == 3:
+                grouped = staged[2][:, 1]
+            else:
+                staged[s] = keep.tile([P, 2, 2, P, PACK], BF16, name="wd_bf%d" % s, tag="dough%d" % (0 if s == 2 else s - 3), align_bytes=64)
+                grouped = staged[s][:, 0]
             for a in range(2):
                 nc.vector.tensor_copy(
-                    out=grouped[:, a, :, :].rearrange("p (c i) j -> p c j i", i=4),
-                    in_=wd_raw[i, a][:, :, cols].rearrange("p j (c i) -> p c j i", i=4),
+                    out=grouped[:, a, :, :],
+                    in_=wd_raw[i, a][:, :, cols].rearrange("p j c -> p c j"),
                 )
             for a in range(2):
                 codes = keep.tile([P, P], U32, name="wq%d%d" % (s, a), align_bytes=64)
@@ -161,29 +171,36 @@ def tile_list_sourdough_order_blend_kernel(
             banks_taken.append(psum.tile([P, BANK], F32, name="acc%d" % (len(banks_taken) % 8)))
             return banks_taken[-1]
 
-        def first_stage(s, is_act, copy):
+        def one_pass(acc, s, is_act, h, a):
             b, t = divmod(s, PACK)
             if is_act:
-                window = ring.tile([P, S], F32, name="act_w", bufs=2)
+                lhs = w4[b][:, a, 2 * P * t : 2 * P * (t + 1)].bitcast(FP4X4)
+                lhs_sc = w4_sc[:, a, P * s : P * (s + 1)]
             else:
-                window = keep.tile([P, S], F32, name="dough_w%d" % s, tag="dough%d" % s, align_bytes=64)
+                lhs = wq[a, s].bitcast(FP8X4)
+                lhs_sc = wq_sc[a, s]
+            nc.tensor.matmul_mx(
+                out=acc[:], lhsT=lhs, lhsT_scale=lhs_sc, rhs=v[a, h][:].bitcast(FP8X4),
+                rhs_scale=v_sc[a][:, BANK * h : BANK * (h + 1)], start=(a == 0), stop=(a == 1),
+            )
+
+        def new_window(s, is_act):
+            if is_act:
+                return ring.tile([P, S], F32, name="act_w", bufs=1)
+            return keep.tile([P, S], F32, name="dough_w%d" % s, tag="dough%d" % s, align_bytes=64)
+
+        def empty(window, h, acc):
+            nc.scalar.copy(out=window[:, BANK * h : BANK * (h + 1)], in_=acc[:])
+
+        def first_stage(s, is_act):
+            window = new_window(s, is_act)
             for h in range(2):
                 acc = bank()
                 for a in range(2):
-                    if is_act:
-                        lhs = w4[b][:, a, 2 * P * t : 2 * P * (t + 1)].bitcast(FP4X4)
-                        lhs_sc = w4_sc[:, a, P * s : P * (s + 1)]
-                    else:
-                        lhs = wq[a, s].bitcast(FP8X4)
-                        lhs_sc = wq_sc[a, s]
-                    nc.tensor.matmul_mx(
-                        out=acc[:], lhsT=lhs, lhsT_scale=lhs_sc, rhs=v[a, h][:].bitcast(FP8X4),
-                        rhs_scale=v_sc[:, a, BANK * h : BANK * (h + 1)], start=(a == 0), stop=(a == 1),
-                    )
-                copy[h](out=window[:, BANK * h : BANK * (h + 1)], in_=acc[:])
+                    one_pass(acc, s, is_act, h, a)
+                empty(window, h, acc)
             return window
 
-        on_scalar = (nc.scalar.copy, nc.scalar.copy)
         share = {}
         dough = {}
         prev = {}
@@ -194,15 +211,20 @@ def tile_list_sourdough_order_blend_kernel(
         zq = [keep.tile([P, M], U32, name="zq%d" % b, align_bytes=64) for b in range(2)]
         zq_sc = [keep.tile([P, M], U8, name="zq_sc%d" % b, align_bytes=64) for b in range(2)]
 
-        def make_share(s):
-            window = first_stage(s, True, on_scalar)
+        def share_of(s, window):
             share[s] = ring.tile([P, M], F32, name="share", bufs=4)
             nc.scalar.activation(out=share[s][:], in_=window[:].indirect(pos1_sb[:]), func=ACT.Sigmoid)
 
-        def make_dough(s, copy):
-            dough[s] = first_stage(s, False, copy)
+        def make_share(s):
+            share_of(s, first_stage(s, True))
+
+        def picks_of(s):
             prev[s] = ring.tile([P, M], F32, name="prev", bufs=3)
             diff[s] = ring.tile([P, M], F32, name="diff", bufs=3)
+
+        def make_dough(s):
+            dough[s] = first_stage(s, False)
+            picks_of(s)
 
         def entries(cols):
             return slice(cols.start // 16, cols.stop // 16)
@@ -274,52 +296,63 @@ def tile_list_sourdough_order_blend_kernel(
                         nc.scalar.activation(
                             out=result[:, c, :], in_=acc[:, width * c : width * (c + 1)], func=ACT.Identity, bias=bias[:, c : c + 1]
                         )
-            nc.sync.dma_start(out=out[:, cols].rearrange("(c p) m -> p c m", p=P), in_=result[:])
+                nc.sync.dma_start(
+                    out=out[2 * P * pair : 2 * P * (pair + 1), cols].rearrange("(c p) m -> p c m", p=P), in_=result[:, 2 * pair : 2 * pair + 2, :]
+                )
 
         whole = slice(0, M)
         halves = [slice(0, M // 2), slice(M // 2, M)]
-        make_share(0)
+        gather_table(0)
         prepare_wd(0)
+        gather_table(1)
         prepare_wd(1)
-        make_dough(0, (nc.vector.tensor_copy, nc.scalar.copy))
+        first_banks = [bank() for h in range(2)]
+        for h in range(2):
+            one_pass(first_banks[h], 0, False, h, 0)
+        dough[0] = new_window(0, False)
+        picks_of(0)
+        first_act = new_window(0, True)
+        act_banks = [bank() for h in range(2)]
+        for h in range(2):
+            one_pass(first_banks[h], 0, False, h, 1)
+            empty(dough[0], h, first_banks[h])
+            one_pass(act_banks[h], 0, True, h, 0)
+        for h in range(2):
+            one_pass(act_banks[h], 0, True, h, 1)
+            empty(first_act, h, act_banks[h])
+        share_of(0, first_act)
+        make_dough(1)
         make_share(1)
-        for s in range(SLICES - 1):
-            make_dough(s + 1, on_scalar)
+        for s in range(SLICES - 2):
             for step in (pick_prev, pick_diff, weigh):
                 for cols in halves:
                     step(s, cols)
-            if s + 2 < SLICES:
-                prepare_wd(s + 2)
-            if s > 0:
-                turn(s - 1, whole)
-            if s + 2 < SLICES:
+            if s == 0:
+                prepare_wd(2)
+            if s + 3 < SLICES:
+                prepare_wd(s + 3)
                 make_share(s + 2)
-            if s == PACK + 1:
-                for cols in halves:
-                    turn_back(0, cols)
-        quantize_z(0, whole)
+                make_dough(s + 2)
+            else:
+                make_dough(s + 2)
+                make_share(s + 2)
+            turn(s, whole)
+        for cols in halves:
+            turn_back(0, cols)
         edges = [sum(LAST_PIECES[:i]) for i in range(len(LAST_PIECES) + 1)]
         pieces = [slice(edges[i], edges[i + 1]) for i in range(len(LAST_PIECES))]
-        last = SLICES - 1
-        pick_prev(last, pieces[0])
-        turn(last - 1, whole)
-        pick_prev(last, pieces[1])
-        pick_diff(last, pieces[0])
-        pick_prev(last, pieces[2])
-        weigh(last, pieces[0])
-        pick_diff(last, pieces[1])
-        turn(last, pieces[0])
-        pick_diff(last, pieces[2])
-        weigh(last, pieces[1])
-        turn(last, pieces[1])
-        turn_back(1, pieces[0])
-        weigh(last, pieces[2])
-        turn(last, pieces[2])
-        turn_back(1, pieces[1])
-        quantize_z(1, pieces[0])
-        turn_back(1, pieces[2])
-        quantize_z(1, pieces[1])
-        finish(pieces[0])
-        quantize_z(1, pieces[2])
-        finish(pieces[1])
-        finish(pieces[2])
+        for i, cols in enumerate(pieces):
+            for step in (pick_prev, pick_diff, weigh):
+                for s in (SLICES - 2, SLICES - 1):
+                    step(s, cols)
+            if i == 0:
+                quantize_z(0, whole)
+            else:
+                quantize_z(1, pieces[i - 1])
+            for s in (SLICES - 2, SLICES - 1):
+                turn(s, cols)
+            if i > 0:
+                finish(pieces[i - 1])
+            turn_back(1, cols)
+        quantize_z(1, pieces[-1])
+        finish(pieces[-1])

@@ -155,8 +155,8 @@ def tile_list_sourdough_order_blend_kernel(
                 grouped = staged[s][:, 0]
             for a in range(2):
                 nc.vector.tensor_copy(
-                    out=grouped[:, a, :, :],
-                    in_=wd_raw[i, a][:, :, cols].rearrange("p j c -> p c j"),
+                    out=grouped[:, a, :, :].rearrange("p (c i) j -> p c j i", i=4),
+                    in_=wd_raw[i, a][:, :, cols].rearrange("p j (c i) -> p c j i", i=4),
                 )
             for a in range(2):
                 codes = keep.tile([P, P], U32, name="wq%d%d" % (s, a), align_bytes=64)

@@ -23,6 +23,7 @@ PASS = P * PACK
 BANK = 512
 SLICES = H // P
 WD_PIECES = (128, 128, 256, 512)
+EARLY_TURNS = 2
 LAST_PIECES = (256, 128, 128)
 
 
@@ -42,6 +43,7 @@ def tile_list_sourdough_order_blend_kernel(
         lists = ctx.enter_context(tc.tile_pool(name="lists", bufs=1))
         keep = ctx.enter_context(tc.tile_pool(name="keep", bufs=1))
         arena = ctx.enter_context(tc.tile_pool(name="arena", bufs=1))
+        regions = ctx.enter_context(tc.tile_pool(name="regions", bufs=1))
         ring = ctx.enter_context(tc.tile_pool(name="ring", bufs=2))
         psum = ctx.enter_context(tc.psum_pool(name="psum", bufs=1))
 
@@ -61,9 +63,9 @@ def tile_list_sourdough_order_blend_kernel(
 
         w4_sc = keep.tile([P, 2, H], U8, name="w4_sc", align_bytes=64)
         v_sc = [keep.tile([P, S], U8, name="v_sc%d" % a, align_bytes=64) for a in range(2)]
-        nc.vector.memset(w4_sc[:].bitcast(I32), 0)
-        nc.vector.memset(tab_sc[32:64, :T].bitcast(I32), 0)
         nc.vector.memset(tab_sc[64:P, :T].bitcast(I32), 0)
+        nc.gpsimd.memset(tab_sc[32:64, :T].bitcast(I32), 0)
+        nc.gpsimd.memset(w4_sc[:].bitcast(I32), 0)
         load_scale_rows(nc.gpsimd, w4_sc, w4_scales, range(4))
         for a in range(2):
             nc.vector.memset(v_sc[a][:].bitcast(I32), 0)
@@ -97,10 +99,10 @@ def tile_list_sourdough_order_blend_kernel(
 
         def load_wd(i, place):
             width = WD_PIECES[i]
+            wd_raw[i] = place([P, 2, PACK, width], F32, 8 * PACK * width, "wd_raw%d" % i)
             for a in range(2):
-                wd_raw[i, a] = place([P, PACK, width], F32, 4 * PACK * width, "wd_raw%d%d" % (i, a))
                 nc.sync.dma_start(
-                    out=wd_raw[i, a][:],
+                    out=wd_raw[i][:, a, :, :],
                     in_=wd[a * PASS : (a + 1) * PASS, starts[i] : starts[i] + width].rearrange("(p j) c -> p j c", j=PACK),
                 )
 
@@ -122,8 +124,8 @@ def tile_list_sourdough_order_blend_kernel(
 
         load_w4(0)
         load_wd(1, late_tile)
-        load_wd(2, late_tile)
         load_w4(1)
+        load_wd(2, late_tile)
         load_wd(3, late_tile)
         w8 = late_tile([P, 2, N], U32, 8 * N, "w8")
         nc.sync.dma_start(out=w8[:].bitcast(I32), in_=w8_words.rearrange("a p n t -> p a (n t)").bitcast(I32))
@@ -142,40 +144,79 @@ def tile_list_sourdough_order_blend_kernel(
                 nc.vector.tensor_copy(out=v[a, h][:], in_=tab[a][:].indirect(offs_sb[:, 32 * h : 32 * h + 32]))
 
         wq = {}
-        staged = {}
         wq_sc = {}
+        grouped = {}
+        region_bytes = 6 * 1024
 
-        def prepare_wd(s):
-            i = max(n for n in range(len(starts)) if starts[n] <= P * s)
-            cols = slice(P * s - starts[i], P * (s + 1) - starts[i])
-            if s == 3:
-                grouped = staged[2][:, 1]
-            else:
-                staged[s] = keep.tile([P, 2, 2, P, PACK], BF16, name="wd_bf%d" % s, tag="dough%d" % (0 if s == 2 else s - 3), align_bytes=64)
-                grouped = staged[s][:, 0]
+        def after_share(s, shape, dtype, offset, name):
+            if s < 0:
+                return keep.tile(shape, dtype, name=name, align_bytes=64)
+            return regions.tile(shape, dtype, name=name, align_bytes=64, offset=region_bytes * (s % 4) + offset)
+
+        def round_wd(i):
+            grouped[i] = keep.tile([P, 2, WD_PIECES[i], PACK], BF16, name="wd_bf%d" % i, align_bytes=64)
+            nc.vector.tensor_copy(
+                out=grouped[i][:].rearrange("p a (c i) j -> p a c j i", i=4),
+                in_=wd_raw[i][:].rearrange("p a j (c i) -> p a c j i", i=4),
+            )
+
+        def quantize_wd(i):
+            width = WD_PIECES[i]
+            codes = keep.tile([P, 2, width], U32, name="wq%d" % i, align_bytes=64)
+            plane = keep.tile([P, 2, width], U8, name="wq_sc%d" % i, align_bytes=64)
+            nc.vector.quantize_mx(
+                out=codes[:].rearrange("p a c -> p (a c)").bitcast(FP8X4), scales=plane[:].rearrange("p a c -> p (a c)"),
+                in_=grouped[i][:].rearrange("p a c j -> p (a c j)"),
+            )
             for a in range(2):
-                nc.vector.tensor_copy(
-                    out=grouped[:, a, :, :].rearrange("p (c i) j -> p c j i", i=4),
-                    in_=wd_raw[i, a][:, :, cols].rearrange("p j (c i) -> p c j i", i=4),
-                )
-            for a in range(2):
-                codes = keep.tile([P, P], U32, name="wq%d%d" % (s, a), align_bytes=64)
-                plane = keep.tile([P, P], U8, name="wq_sc%d%d" % (s, a), align_bytes=64)
-                nc.vector.quantize_mx(out=codes[:].bitcast(FP8X4), scales=plane[:], in_=grouped[:, a, :, :].rearrange("p c j -> p (c j)"))
-                wq[a, s] = codes[:]
-                wq_sc[a, s] = plane[:]
+                for s in range(starts[i] // P, (starts[i] + width) // P):
+                    cols = slice(P * s - starts[i], P * (s + 1) - starts[i])
+                    wq[a, s] = codes[:, a, cols]
+                    wq_sc[a, s] = plane[:, a, cols]
+
+        def round_dealt(a, held, copy=nc.vector.tensor_copy):
+            grouped["dealt", a] = after_share(held, [P, PACK, P, PACK], BF16, 2048, "wd_dealt%d" % a)
+            copy(
+                out=grouped["dealt", a][:].rearrange("p t m j -> p m j t"),
+                in_=wd_raw[3][:, a, :, :].rearrange("p j (m t) -> p m j t", t=PACK),
+            )
+
+        def quantize_dealt(a):
+            codes = keep.tile([P, PASS], U32, name="wq_dealt%d" % a, align_bytes=64)
+            plane = keep.tile([P, PASS], U8, name="wq_dealt_sc%d" % a, align_bytes=64)
+            nc.vector.quantize_mx(out=codes[:].bitcast(FP8X4), scales=plane[:], in_=grouped["dealt", a][:].rearrange("p t m j -> p (t m j)"))
+            for t in range(PACK):
+                wq[a, PACK + t] = codes[:, P * t : P * (t + 1)]
+                wq_sc[a, PACK + t] = plane[:, P * t : P * (t + 1)]
+
+        w4_dealt = arena.tile([P, 2, 2 * PASS], U8, name="w4_dealt", align_bytes=64, offset=0)
+        w4_dealt_sc = arena.tile([P, 2, PASS], U8, name="w4_dealt_sc", align_bytes=64, offset=4 * PASS)
+
+        def deal_w4_words():
+            nc.vector.tensor_copy(
+                out=w4_dealt[:].bitcast(U16).rearrange("p a (t m) -> p a m t", t=PACK),
+                in_=w4[1][:].bitcast(U16).rearrange("p a (m t) -> p a m t", t=PACK),
+            )
+
+        def deal_w4_scales():
+            nc.vector.tensor_copy(
+                out=w4_dealt_sc[:].rearrange("p a (t m) -> p a m t", t=PACK),
+                in_=w4_sc[:, :, PASS:].rearrange("p a (m t) -> p a m t", t=PACK),
+            )
 
         banks_taken = []
 
-        def bank():
-            banks_taken.append(psum.tile([P, BANK], F32, name="acc%d" % (len(banks_taken) % 8)))
-            return banks_taken[-1]
+        def bank(index=None):
+            if index is None:
+                index = len(banks_taken) % 8
+                banks_taken.append(index)
+            return psum.tile([P, BANK], F32, name="acc%d" % index)
 
         def one_pass(acc, s, is_act, h, a):
             b, t = divmod(s, PACK)
             if is_act:
-                lhs = w4[b][:, a, 2 * P * t : 2 * P * (t + 1)].bitcast(FP4X4)
-                lhs_sc = w4_sc[:, a, P * s : P * (s + 1)]
+                lhs = (w4[0], w4_dealt)[b][:, a, 2 * P * t : 2 * P * (t + 1)].bitcast(FP4X4)
+                lhs_sc = (w4_sc, w4_dealt_sc)[b][:, a, P * t : P * (t + 1)]
             else:
                 lhs = wq[a, s].bitcast(FP8X4)
                 lhs_sc = wq_sc[a, s]
@@ -186,8 +227,8 @@ def tile_list_sourdough_order_blend_kernel(
 
         def new_window(s, is_act):
             if is_act:
-                return ring.tile([P, S], F32, name="act_w", bufs=1)
-            return keep.tile([P, S], F32, name="dough_w%d" % s, tag="dough%d" % s, align_bytes=64)
+                return after_share(s, [P, S], F32, 0, "act_w%d" % s)
+            return ring.tile([P, S], F32, name="dough_w", bufs=3)
 
         def empty(window, h, acc):
             nc.scalar.copy(out=window[:, BANK * h : BANK * (h + 1)], in_=acc[:])
@@ -201,71 +242,82 @@ def tile_list_sourdough_order_blend_kernel(
                 empty(window, h, acc)
             return window
 
+        act = {}
         share = {}
         dough = {}
         prev = {}
         diff = {}
+        prod = {}
         tiles = M // P
-        turned = [keep.tile([P, 2, tiles, P, 2], BF16, name="turned%d" % b, align_bytes=64) for b in range(2)]
+        turned = keep.tile([P, 2, tiles, P, 2], BF16, name="turned", align_bytes=64)
+        prev_dealt = keep.tile([P, PACK, M], F32, name="prev_dealt", align_bytes=64)
+        prod_dealt = keep.tile([P, PACK, M], F32, name="prod_dealt", align_bytes=64)
         z_bf = [keep.tile([P, M, PACK], BF16, name="z_bf%d" % b, align_bytes=64) for b in range(2)]
         zq = [keep.tile([P, M], U32, name="zq%d" % b, align_bytes=64) for b in range(2)]
         zq_sc = [keep.tile([P, M], U8, name="zq_sc%d" % b, align_bytes=64) for b in range(2)]
 
-        def share_of(s, window):
-            share[s] = ring.tile([P, M], F32, name="share", bufs=4)
-            nc.scalar.activation(out=share[s][:], in_=window[:].indirect(pos1_sb[:]), func=ACT.Sigmoid)
-
         def make_share(s):
-            share_of(s, first_stage(s, True))
-
-        def picks_of(s):
-            prev[s] = ring.tile([P, M], F32, name="prev", bufs=3)
-            diff[s] = ring.tile([P, M], F32, name="diff", bufs=3)
-
-        def make_dough(s):
-            dough[s] = first_stage(s, False)
-            picks_of(s)
+            share[s] = ring.tile([P, M], F32, name="share", bufs=3)
+            nc.scalar.activation(out=share[s][:], in_=act[s][:].indirect(pos1_sb[:]), func=ACT.Sigmoid)
 
         def entries(cols):
             return slice(cols.start // 16, cols.stop // 16)
 
         def pick_prev(s, cols):
+            if s < PACK:
+                prev[s] = ring.tile([P, M], F32, name="prev", bufs=4)[:]
+                prod[s] = ring.tile([P, M], F32, name="prod", bufs=4)[:]
+            else:
+                prev[s] = prev_dealt[:, s - PACK, :]
+                prod[s] = prod_dealt[:, s - PACK, :]
             nc.vector.tensor_copy(out=prev[s][:, cols], in_=dough[s][:].indirect(pos3_sb[:, entries(cols)]))
 
         def pick_diff(s, cols):
+            if s not in diff:
+                diff[s] = after_share(s - 1, [P, M], F32, 0, "diff%d" % s)
             nc.vector.tensor_tensor(
                 out=diff[s][:, cols], in0=dough[s][:].indirect(pos2_sb[:, entries(cols)]), in1=prev[s][:, cols], op=ALU.subtract
             )
 
         def weigh(s, cols):
-            nc.vector.tensor_tensor(out=diff[s][:, cols], in0=diff[s][:, cols], in1=share[s][:, cols], op=ALU.mult)
+            nc.vector.tensor_tensor(out=prod[s][:, cols], in0=diff[s][:, cols], in1=share[s][:, cols], op=ALU.mult)
 
-        def turn(s, cols):
-            b, t = divmod(s, PACK)
+        def turn(rows, cols):
             first, last = cols.start // P, cols.stop // P
             acc = bank()
+            k = 0
             for c in range(first, last):
-                for i, term in enumerate((prev[s], diff[s])):
-                    nc.tensor.matmul(
-                        out=acc[:, P * (c - first) : P * (c - first + 1)], lhsT=term[:, P * c : P * (c + 1)], rhs=ident[:],
-                        is_transpose=True, start=(i == 0), stop=(i == 1),
-                    )
+                for t in rows:
+                    for i, term in enumerate((prod[t], prev[t])):
+                        nc.tensor.matmul(
+                            out=acc[:, P * k : P * (k + 1)], lhsT=term[:, P * c : P * (c + 1)], rhs=ident[:],
+                            is_transpose=True, start=(i == 0), stop=(i == 1),
+                        )
+                    k += 1
             nc.scalar.copy(
-                out=turned[b][:, :, first:last, 32 * t : 32 * (t + 1), :],
-                in_=acc[:, : P * (last - first)].rearrange("m (c q u e) -> m u c q e", q=32, u=2, e=2),
+                out=turned[:, :, first:last, 32 * rows[0] : 32 * (rows[-1] + 1), :],
+                in_=acc[:].rearrange("m (c q u e) -> m u c q e", c=last - first, u=2, e=2),
             )
 
-        def turn_back(b, cols):
+        def turn_back(cols):
             first, last = cols.start // P, cols.stop // P
             acc = bank()
             for c in range(first, last):
                 for u in range(2):
-                    words = turned[b][:, u, c, :, :].rearrange("m p e -> m (p e)").bitcast(F32)
+                    words = turned[:, u, c, :, :].rearrange("m p e -> m (p e)").bitcast(F32)
                     k = 2 * (c - first) + u
                     nc.tensor.transpose(acc[:, P * k : P * (k + 1)], words, ident[:])
             nc.scalar.copy(
-                out=z_bf[b][:, cols, :].rearrange("p m t -> p (m t)").bitcast(F32).rearrange("p (c m u) -> p c m u", m=P, u=2),
+                out=z_bf[0][:, cols, :].rearrange("p m t -> p (m t)").bitcast(F32).rearrange("p (c m u) -> p c m u", m=P, u=2),
                 in_=acc[:, : 2 * P * (last - first)].rearrange("p (c u m) -> p c m u", u=2, m=P),
+            )
+
+        def blend(cols):
+            nc.vector.tensor_tensor(
+                out=z_bf[1][:, cols, :].rearrange("p (c i) t -> p c t i", i=4),
+                in0=prod_dealt[:, :, cols].rearrange("p t (c i) -> p c t i", i=4),
+                in1=prev_dealt[:, :, cols].rearrange("p t (c i) -> p c t i", i=4),
+                op=ALU.add,
             )
 
         def quantize_z(b, cols):
@@ -273,45 +325,62 @@ def tile_list_sourdough_order_blend_kernel(
                 out=zq[b][:, cols].bitcast(FP8X4), scales=zq_sc[b][:, cols], in_=z_bf[b][:, cols, :].rearrange("p m t -> p (m t)")
             )
 
-        def finish(cols):
+        sums = {}
+
+        def last_pass(cols, b):
             width = cols.stop - cols.start
-            result = ring.tile([P, N // P, width], F32, name="result%d" % cols.start, bufs=1)
-            for pair in range(2):
-                acc = bank()
-                for i in range(2):
-                    c = 2 * pair + i
-                    for b in range(2):
-                        nc.tensor.matmul_mx(
-                            out=acc[:, width * i : width * (i + 1)], lhsT=w8[:, b, P * c : P * (c + 1)].bitcast(FP8X4),
-                            lhsT_scale=w8_sc[:, b, P * c : P * (c + 1)],
-                            rhs=zq[b][:, cols].bitcast(FP8X4), rhs_scale=zq_sc[b][:, cols], start=(b == 0), stop=(b == 1),
-                        )
-                if pair == 1:
+            per_bank = BANK // width
+            for c in range(N // P):
+                group, i = divmod(c, per_bank)
+                if (cols.start, group) not in sums:
+                    sums[cols.start, group] = bank()
+                nc.tensor.matmul_mx(
+                    out=sums[cols.start, group][:, width * i : width * (i + 1)], lhsT=w8[:, b, P * c : P * (c + 1)].bitcast(FP8X4),
+                    lhsT_scale=w8_sc[:, b, P * c : P * (c + 1)],
+                    rhs=zq[b][:, cols].bitcast(FP8X4), rhs_scale=zq_sc[b][:, cols],
+                    start=(b == 0 and i == 0), stop=(b == 1 and i == per_bank - 1),
+                )
+
+        def finish(cols, on_vector):
+            width = cols.stop - cols.start
+            per_bank = BANK // width
+            for group in range(N // P // per_bank):
+                result = keep.tile([P, per_bank, width], F32, name="result%d%d" % (cols.start, group), align_bytes=64)
+                acc = sums[cols.start, group]
+                tiles_of = slice(per_bank * group, per_bank * (group + 1))
+                if group in on_vector:
                     nc.vector.tensor_tensor(
-                        out=result[:, 2:4, :], in0=acc[:, : 2 * width].rearrange("p (c m) -> p c m", c=2),
-                        in1=bias[:, 2:4].unsqueeze(2).to_broadcast([P, 2, width]), op=ALU.add,
+                        out=result[:], in0=acc[:].rearrange("p (c m) -> p c m", c=per_bank),
+                        in1=bias[:, tiles_of].unsqueeze(2).to_broadcast([P, per_bank, width]), op=ALU.add,
                     )
                 else:
-                    for c in range(2):
+                    for i in range(per_bank):
+                        c = per_bank * group + i
                         nc.scalar.activation(
-                            out=result[:, c, :], in_=acc[:, width * c : width * (c + 1)], func=ACT.Identity, bias=bias[:, c : c + 1]
+                            out=result[:, i, :], in_=acc[:, width * i : width * (i + 1)], func=ACT.Identity, bias=bias[:, c : c + 1]
                         )
                 nc.sync.dma_start(
-                    out=out[2 * P * pair : 2 * P * (pair + 1), cols].rearrange("(c p) m -> p c m", p=P), in_=result[:, 2 * pair : 2 * pair + 2, :]
+                    out=out[P * tiles_of.start : P * tiles_of.stop, cols].rearrange("(c p) m -> p c m", p=P), in_=result[:]
                 )
 
         whole = slice(0, M)
         halves = [slice(0, M // 2), slice(M // 2, M)]
+        last = SLICES - 1
+        edges = [sum(LAST_PIECES[:i]) for i in range(len(LAST_PIECES) + 1)]
+        pieces = [slice(edges[i], edges[i + 1]) for i in range(len(LAST_PIECES))]
+
         gather_table(0)
-        prepare_wd(0)
+        round_wd(0)
+        quantize_wd(0)
         gather_table(1)
-        prepare_wd(1)
+        round_wd(1)
+        deal_w4_words()
+        quantize_wd(1)
         first_banks = [bank() for h in range(2)]
         for h in range(2):
             one_pass(first_banks[h], 0, False, h, 0)
         dough[0] = new_window(0, False)
-        picks_of(0)
-        first_act = new_window(0, True)
+        act[0] = new_window(0, True)
         act_banks = [bank() for h in range(2)]
         for h in range(2):
             one_pass(first_banks[h], 0, False, h, 1)
@@ -319,40 +388,58 @@ def tile_list_sourdough_order_blend_kernel(
             one_pass(act_banks[h], 0, True, h, 0)
         for h in range(2):
             one_pass(act_banks[h], 0, True, h, 1)
-            empty(first_act, h, act_banks[h])
-        share_of(0, first_act)
-        make_dough(1)
-        make_share(1)
-        for s in range(SLICES - 2):
-            for step in (pick_prev, pick_diff, weigh):
-                for cols in halves:
-                    step(s, cols)
+            empty(act[0], h, act_banks[h])
+        for s in range(last):
+            pick_prev(s, whole)
             if s == 0:
-                prepare_wd(2)
-            if s + 3 < SLICES:
-                prepare_wd(s + 3)
-                make_share(s + 2)
-                make_dough(s + 2)
-            else:
-                make_dough(s + 2)
-                make_share(s + 2)
-            turn(s, whole)
+                deal_w4_scales()
+            if s == 1:
+                quantize_wd(2)
+            if s == 2:
+                quantize_dealt(0)
+            if s > 0:
+                weigh(s - 1, whole)
+            if s == 2:
+                round_dealt(1, 1)
+            pick_diff(s, whole)
+            if s == 0:
+                round_wd(2)
+            if s == 1:
+                round_dealt(0, 0, nc.scalar.copy)
+            if s == 2:
+                quantize_dealt(1)
+            act[s + 1] = first_stage(s + 1, True)
+            dough[s + 1] = first_stage(s + 1, False)
+            make_share(s)
+            if 0 < s <= EARLY_TURNS:
+                turn([s - 1], whole)
+        make_share(last)
         for cols in halves:
-            turn_back(0, cols)
-        edges = [sum(LAST_PIECES[:i]) for i in range(len(LAST_PIECES) + 1)]
-        pieces = [slice(edges[i], edges[i + 1]) for i in range(len(LAST_PIECES))]
-        for i, cols in enumerate(pieces):
-            for step in (pick_prev, pick_diff, weigh):
-                for s in (SLICES - 2, SLICES - 1):
-                    step(s, cols)
-            if i == 0:
-                quantize_z(0, whole)
-            else:
-                quantize_z(1, pieces[i - 1])
-            for s in (SLICES - 2, SLICES - 1):
-                turn(s, cols)
-            if i > 0:
-                finish(pieces[i - 1])
-            turn_back(1, cols)
-        quantize_z(1, pieces[-1])
-        finish(pieces[-1])
+            turn([2, 3], cols)
+        for cols in halves:
+            turn_back(cols)
+        pick_prev(last, whole)
+        weigh(last - 1, whole)
+        pick_diff(last, pieces[0])
+        pick_diff(last, pieces[1])
+        weigh(last, pieces[0])
+        pick_diff(last, pieces[2])
+        blend(pieces[0])
+        weigh(last, pieces[1])
+        quantize_z(0, halves[0])
+        quantize_z(1, pieces[0])
+        last_pass(pieces[0], 0)
+        weigh(last, pieces[2])
+        blend(pieces[1])
+        quantize_z(0, halves[1])
+        blend(pieces[2])
+        last_pass(pieces[0], 1)
+        last_pass(pieces[1], 0)
+        last_pass(pieces[2], 0)
+        quantize_z(1, pieces[1])
+        quantize_z(1, pieces[2])
+        last_pass(pieces[1], 1)
+        last_pass(pieces[2], 1)
+        finish(pieces[0], (1,))
+        finish(pieces[1], ())
+        finish(pieces[2], (0,))

@@ -24,14 +24,15 @@ BANK = 512
 SLICES = H // P
 WD_PIECES = (128, 128, 256, 512)
 EARLY_TURNS = 2
+WARM_PASSES = 4
 LAST_PIECES = (256, 128, 128)
 
 
 def load_scale_rows(queue, plane, scales, quadrants):
     for q in quadrants:
         queue.dma_start(
-            out=plane[32 * q : 32 * q + 4, :, :].bitcast(I32),
-            in_=scales[:, 4 * q : 4 * q + 4, :].rearrange("a r c -> r a c").bitcast(I32),
+            out=plane[q:P:32, :, :].bitcast(I32),
+            in_=scales[:, q:16:4, :].rearrange("a r c -> r a c").bitcast(I32),
         )
 
 
@@ -44,6 +45,7 @@ def tile_list_sourdough_order_blend_kernel(
         keep = ctx.enter_context(tc.tile_pool(name="keep", bufs=1))
         arena = ctx.enter_context(tc.tile_pool(name="arena", bufs=1))
         regions = ctx.enter_context(tc.tile_pool(name="regions", bufs=1))
+        late_z = ctx.enter_context(tc.tile_pool(name="late_z", bufs=1))
         ring = ctx.enter_context(tc.tile_pool(name="ring", bufs=2))
         psum = ctx.enter_context(tc.psum_pool(name="psum", bufs=1))
 
@@ -86,6 +88,7 @@ def tile_list_sourdough_order_blend_kernel(
         load_table(0)
         w4 = {}
         wd_raw = {}
+        raw_at = {}
         starts = [sum(WD_PIECES[:i]) for i in range(len(WD_PIECES))]
 
         def early_tile(shape, dtype, size, name):
@@ -99,6 +102,7 @@ def tile_list_sourdough_order_blend_kernel(
 
         def load_wd(i, place):
             width = WD_PIECES[i]
+            raw_at[i] = placed[-1]
             wd_raw[i] = place([P, 2, PACK, width], F32, 8 * PACK * width, "wd_raw%d" % i)
             for a in range(2):
                 nc.sync.dma_start(
@@ -119,7 +123,7 @@ def tile_list_sourdough_order_blend_kernel(
                     tab[1] = late_tile([P, T], U32, 4 * T, "tab1")
                     load_table(1)
                 nc.sync.dma_start(
-                    out=v_sc[a][32 * q : 32 * q + 4, :].bitcast(I32), in_=picked_sc[16 * a + 4 * q : 16 * a + 4 * q + 4, :].bitcast(I32)
+                    out=v_sc[a][q:P:32, :].bitcast(I32), in_=picked_sc[16 * a + q : 16 * a + 16 : 4, :].bitcast(I32)
                 )
 
         load_w4(0)
@@ -154,7 +158,7 @@ def tile_list_sourdough_order_blend_kernel(
             return regions.tile(shape, dtype, name=name, align_bytes=64, offset=region_bytes * (s % 4) + offset)
 
         def round_wd(i):
-            grouped[i] = keep.tile([P, 2, WD_PIECES[i], PACK], BF16, name="wd_bf%d" % i, align_bytes=64)
+            grouped[i] = keep.tile([P, 2, WD_PIECES[i], PACK], BF16, name="wd_bf%d" % i, tag="wd_bf%d" % i, align_bytes=64)
             nc.vector.tensor_copy(
                 out=grouped[i][:].rearrange("p a (c i) j -> p a c j i", i=4),
                 in_=wd_raw[i][:].rearrange("p a j (c i) -> p a c j i", i=4),
@@ -190,7 +194,7 @@ def tile_list_sourdough_order_blend_kernel(
                 wq_sc[a, PACK + t] = plane[:, P * t : P * (t + 1)]
 
         w4_dealt = arena.tile([P, 2, 2 * PASS], U8, name="w4_dealt", align_bytes=64, offset=0)
-        w4_dealt_sc = arena.tile([P, 2, PASS], U8, name="w4_dealt_sc", align_bytes=64, offset=4 * PASS)
+        w4_dealt_sc = []
 
         def deal_w4_words():
             nc.vector.tensor_copy(
@@ -199,8 +203,9 @@ def tile_list_sourdough_order_blend_kernel(
             )
 
         def deal_w4_scales():
+            w4_dealt_sc.append(arena.tile([P, 2, PASS], U8, name="w4_dealt_sc", align_bytes=64, offset=raw_at[1]))
             nc.vector.tensor_copy(
-                out=w4_dealt_sc[:].rearrange("p a (t m) -> p a m t", t=PACK),
+                out=w4_dealt_sc[0][:].rearrange("p a (t m) -> p a m t", t=PACK),
                 in_=w4_sc[:, :, PASS:].rearrange("p a (m t) -> p a m t", t=PACK),
             )
 
@@ -216,7 +221,7 @@ def tile_list_sourdough_order_blend_kernel(
             b, t = divmod(s, PACK)
             if is_act:
                 lhs = (w4[0], w4_dealt)[b][:, a, 2 * P * t : 2 * P * (t + 1)].bitcast(FP4X4)
-                lhs_sc = (w4_sc, w4_dealt_sc)[b][:, a, P * t : P * (t + 1)]
+                lhs_sc = (w4_sc, w4_dealt_sc[0])[b][:, a, P * t : P * (t + 1)]
             else:
                 lhs = wq[a, s].bitcast(FP8X4)
                 lhs_sc = wq_sc[a, s]
@@ -252,7 +257,7 @@ def tile_list_sourdough_order_blend_kernel(
         turned = keep.tile([P, 2, tiles, P, 2], BF16, name="turned", align_bytes=64)
         prev_dealt = keep.tile([P, PACK, M], F32, name="prev_dealt", align_bytes=64)
         prod_dealt = keep.tile([P, PACK, M], F32, name="prod_dealt", align_bytes=64)
-        z_bf = [keep.tile([P, M, PACK], BF16, name="z_bf%d" % b, align_bytes=64) for b in range(2)]
+        z_bf = {0: late_z.tile([P, M, PACK], BF16, name="z_bf0", align_bytes=64, offset=0)}
         zq = [keep.tile([P, M], U32, name="zq%d" % b, align_bytes=64) for b in range(2)]
         zq_sc = [keep.tile([P, M], U8, name="zq_sc%d" % b, align_bytes=64) for b in range(2)]
 
@@ -265,7 +270,7 @@ def tile_list_sourdough_order_blend_kernel(
 
         def pick_prev(s, cols):
             if s < PACK:
-                prev[s] = ring.tile([P, M], F32, name="prev", bufs=4)[:]
+                prev[s] = keep.tile([P, M], F32, name="prev%d" % s, tag="wd_bf1" if s == 0 else "prev%d" % s, align_bytes=64)[:]
                 prod[s] = ring.tile([P, M], F32, name="prod", bufs=4)[:]
             else:
                 prev[s] = prev_dealt[:, s - PACK, :]
@@ -299,9 +304,12 @@ def tile_list_sourdough_order_blend_kernel(
                 in_=acc[:].rearrange("m (c q u e) -> m u c q e", c=last - first, u=2, e=2),
             )
 
+        back_banks = []
+
         def turn_back(cols):
             first, last = cols.start // P, cols.stop // P
             acc = bank()
+            back_banks.append(banks_taken[-1])
             for c in range(first, last):
                 for u in range(2):
                     words = turned[:, u, c, :, :].rearrange("m p e -> m (p e)").bitcast(F32)
@@ -313,8 +321,10 @@ def tile_list_sourdough_order_blend_kernel(
             )
 
         def blend(cols):
+            at = 8 * cols.start if cols.start else 8 * M
+            z_bf[1, cols.start] = late_z.tile([P, cols.stop - cols.start, PACK], BF16, name="z_piece%d" % cols.start, align_bytes=64, offset=at)
             nc.vector.tensor_tensor(
-                out=z_bf[1][:, cols, :].rearrange("p (c i) t -> p c t i", i=4),
+                out=z_bf[1, cols.start][:].rearrange("p (c i) t -> p c t i", i=4),
                 in0=prod_dealt[:, :, cols].rearrange("p t (c i) -> p c t i", i=4),
                 in1=prev_dealt[:, :, cols].rearrange("p t (c i) -> p c t i", i=4),
                 op=ALU.add,
@@ -322,23 +332,23 @@ def tile_list_sourdough_order_blend_kernel(
 
         def quantize_z(b, cols):
             nc.vector.quantize_mx(
-                out=zq[b][:, cols].bitcast(FP8X4), scales=zq_sc[b][:, cols], in_=z_bf[b][:, cols, :].rearrange("p m t -> p (m t)")
+                out=zq[b][:, cols].bitcast(FP8X4), scales=zq_sc[b][:, cols], in_=(z_bf[0][:, cols, :] if b == 0 else z_bf[1, cols.start][:]).rearrange("p m t -> p (m t)")
             )
 
         sums = {}
 
-        def last_pass(cols, b):
+        def last_pass(cols, b, opens):
             width = cols.stop - cols.start
             per_bank = BANK // width
             for c in range(N // P):
                 group, i = divmod(c, per_bank)
                 if (cols.start, group) not in sums:
-                    sums[cols.start, group] = bank()
+                    sums[cols.start, group] = bank(back_banks[1 - group] if cols.start == 0 else None)
                 nc.tensor.matmul_mx(
                     out=sums[cols.start, group][:, width * i : width * (i + 1)], lhsT=w8[:, b, P * c : P * (c + 1)].bitcast(FP8X4),
                     lhsT_scale=w8_sc[:, b, P * c : P * (c + 1)],
                     rhs=zq[b][:, cols].bitcast(FP8X4), rhs_scale=zq_sc[b][:, cols],
-                    start=(b == 0 and i == 0), stop=(b == 1 and i == per_bank - 1),
+                    start=(opens and i == 0), stop=(not opens and i == per_bank - 1),
                 )
 
         def finish(cols, on_vector):
@@ -374,7 +384,7 @@ def tile_list_sourdough_order_blend_kernel(
         quantize_wd(0)
         gather_table(1)
         round_wd(1)
-        deal_w4_words()
+        deal_w4_scales()
         quantize_wd(1)
         first_banks = [bank() for h in range(2)]
         for h in range(2):
@@ -392,7 +402,7 @@ def tile_list_sourdough_order_blend_kernel(
         for s in range(last):
             pick_prev(s, whole)
             if s == 0:
-                deal_w4_scales()
+                deal_w4_words()
             if s == 1:
                 quantize_wd(2)
             if s == 2:
@@ -411,13 +421,21 @@ def tile_list_sourdough_order_blend_kernel(
             act[s + 1] = first_stage(s + 1, True)
             dough[s + 1] = first_stage(s + 1, False)
             make_share(s)
-            if 0 < s <= EARLY_TURNS:
-                turn([s - 1], whole)
+            if last - 1 - EARLY_TURNS <= s < last - 1:
+                c = s - (last - 1 - EARLY_TURNS)
+                turn([0, 1, 2, 3], slice(P * c, P * (c + 1)))
         make_share(last)
-        for cols in halves:
-            turn([2, 3], cols)
+        for c in range(EARLY_TURNS, tiles):
+            turn([0, 1, 2, 3], slice(P * c, P * (c + 1)))
+        spare = banks_taken[-1]
         for cols in halves:
             turn_back(cols)
+        idle = bank(spare)
+        for i in range(WARM_PASSES):
+            nc.tensor.matmul_mx(
+                out=idle[:], lhsT=w8[:, 0, :P].bitcast(FP8X4), lhsT_scale=w8_sc[:, 0, :P], rhs=v[0, 0][:].bitcast(FP8X4),
+                rhs_scale=v_sc[0][:, :BANK], start=(i == 0), stop=(i == WARM_PASSES - 1),
+            )
         pick_prev(last, whole)
         weigh(last - 1, whole)
         pick_diff(last, pieces[0])
@@ -426,20 +444,19 @@ def tile_list_sourdough_order_blend_kernel(
         pick_diff(last, pieces[2])
         blend(pieces[0])
         weigh(last, pieces[1])
-        quantize_z(0, halves[0])
-        quantize_z(1, pieces[0])
-        last_pass(pieces[0], 0)
         weigh(last, pieces[2])
+        quantize_z(1, pieces[0])
+        last_pass(pieces[0], 1, True)
+        quantize_z(0, whole)
+        last_pass(pieces[0], 0, False)
+        last_pass(pieces[1], 0, True)
+        last_pass(pieces[2], 0, True)
         blend(pieces[1])
-        quantize_z(0, halves[1])
         blend(pieces[2])
-        last_pass(pieces[0], 1)
-        last_pass(pieces[1], 0)
-        last_pass(pieces[2], 0)
         quantize_z(1, pieces[1])
         quantize_z(1, pieces[2])
-        last_pass(pieces[1], 1)
-        last_pass(pieces[2], 1)
-        finish(pieces[0], (1,))
+        last_pass(pieces[1], 1, False)
+        last_pass(pieces[2], 1, False)
+        finish(pieces[0], ())
         finish(pieces[1], ())
         finish(pieces[2], (0,))

@@ -54,7 +54,7 @@ def tile_list_sourdough_order_blend_kernel(
         pos2_sb = lists.tile([P, M // 16], U16, name="pos2_sb")
         pos3_sb = lists.tile([P, M // 16], U16, name="pos3_sb")
 
-        arena_bytes = 64 * 1024
+        arena_bytes = 48 * 1024
         tab_sc = arena.tile([P, arena_bytes], U8, name="tab_sc", align_bytes=64, offset=0)
         placed = [0]
 
@@ -65,9 +65,9 @@ def tile_list_sourdough_order_blend_kernel(
 
         w4_sc = keep.tile([P, 2, H], U8, name="w4_sc", align_bytes=64)
         v_sc = [keep.tile([P, S], U8, name="v_sc%d" % a, align_bytes=64) for a in range(2)]
-        nc.vector.memset(tab_sc[64:P, :T].bitcast(I32), 0)
-        nc.gpsimd.memset(tab_sc[32:64, :T].bitcast(I32), 0)
         nc.gpsimd.memset(w4_sc[:].bitcast(I32), 0)
+        nc.vector.memset(tab_sc[64:P, :T].bitcast(I32), 0)
+        nc.vector.memset(tab_sc[32:64, :T].bitcast(I32), 0)
         load_scale_rows(nc.gpsimd, w4_sc, w4_scales, range(4))
         for a in range(2):
             nc.vector.memset(v_sc[a][:].bitcast(I32), 0)
@@ -75,10 +75,7 @@ def tile_list_sourdough_order_blend_kernel(
         make_identity(nc, ident[:])
 
         nc.sync.dma_start(offs_sb[:], offs)
-        nc.sync.dma_start(out=tab_sc[0:32, :T].bitcast(I32), in_=tab_scales.rearrange("a q t -> (a q) t").bitcast(I32))
-        nc.sync.dma_start(pos1_sb[:], pos1)
-        nc.sync.dma_start(pos3_sb[:], pos3)
-        nc.sync.dma_start(pos2_sb[:], pos2)
+        nc.scalar.dma_start(out=tab_sc[0:32, :T].bitcast(I32), in_=tab_scales.rearrange("a q t -> (a q) t").bitcast(I32))
         tab = {}
 
         def load_table(a):
@@ -111,6 +108,11 @@ def tile_list_sourdough_order_blend_kernel(
                 )
 
         load_wd(0, early_tile)
+        nc.sync.dma_start(pos1_sb[:], pos1)
+        nc.sync.dma_start(pos3_sb[:], pos3)
+        nc.sync.dma_start(pos2_sb[:], pos2)
+        tab[1] = arena.tile([P, T], U32, name="tab1", align_bytes=64, offset=arena_bytes)
+        load_table(1)
         warm = keep.tile([P, 1], F32, name="warm")
         nc.vector.memset(warm[:], 0.0)
         nc.scalar.activation(out=warm[:], in_=warm[:], func=ACT.Sigmoid)
@@ -119,10 +121,7 @@ def tile_list_sourdough_order_blend_kernel(
         nc.vector.tensor_copy(out=picked_sc[:], in_=tab_sc[:, :T].indirect(offs_sb[:]))
         for a in range(2):
             for q in range(4):
-                if (a, q) == (1, 0):
-                    tab[1] = late_tile([P, T], U32, 4 * T, "tab1")
-                    load_table(1)
-                nc.sync.dma_start(
+                (nc.gpsimd, nc.sync)[a].dma_start(
                     out=v_sc[a][q:P:32, :].bitcast(I32), in_=picked_sc[16 * a + q : 16 * a + 16 : 4, :].bitcast(I32)
                 )
 
@@ -193,7 +192,7 @@ def tile_list_sourdough_order_blend_kernel(
                 wq[a, PACK + t] = codes[:, P * t : P * (t + 1)]
                 wq_sc[a, PACK + t] = plane[:, P * t : P * (t + 1)]
 
-        w4_dealt = arena.tile([P, 2, 2 * PASS], U8, name="w4_dealt", align_bytes=64, offset=0)
+        w4_dealt = arena.tile([P, 2, 2 * PASS], U8, name="w4_dealt", align_bytes=64, offset=arena_bytes)
         w4_dealt_sc = []
 
         def deal_w4_words():

@@ -25,6 +25,7 @@ SLICES = H // P
 WD_PIECES = (128, 128, 256, 512)
 EARLY_TURNS = 2
 WARM_PASSES = 4
+MOVES_ON_GPSIMD = 6
 LAST_PIECES = (256, 128, 128)
 
 
@@ -121,7 +122,7 @@ def tile_list_sourdough_order_blend_kernel(
         nc.vector.tensor_copy(out=picked_sc[:], in_=tab_sc[:, :T].indirect(offs_sb[:]))
         for a in range(2):
             for q in range(4):
-                (nc.gpsimd, nc.sync)[a].dma_start(
+                (nc.gpsimd if 4 * a + q < MOVES_ON_GPSIMD else nc.sync).dma_start(
                     out=v_sc[a][q:P:32, :].bitcast(I32), in_=picked_sc[16 * a + q : 16 * a + 16 : 4, :].bitcast(I32)
                 )
 
@@ -202,7 +203,7 @@ def tile_list_sourdough_order_blend_kernel(
             )
 
         def deal_w4_scales():
-            w4_dealt_sc.append(arena.tile([P, 2, PASS], U8, name="w4_dealt_sc", align_bytes=64, offset=raw_at[1]))
+            w4_dealt_sc.append(keep.tile([P, 2, PASS], U8, name="w4_dealt_sc", tag="wd_bf0", align_bytes=64))
             nc.vector.tensor_copy(
                 out=w4_dealt_sc[0][:].rearrange("p a (t m) -> p a m t", t=PACK),
                 in_=w4_sc[:, :, PASS:].rearrange("p a (m t) -> p a m t", t=PACK),
@@ -232,6 +233,8 @@ def tile_list_sourdough_order_blend_kernel(
         def new_window(s, is_act):
             if is_act:
                 return after_share(s, [P, S], F32, 0, "act_w%d" % s)
+            if s == 0:
+                return keep.tile([P, S], F32, name="dough_w0", tag="first_dough", align_bytes=64)
             return ring.tile([P, S], F32, name="dough_w", bufs=3)
 
         def empty(window, h, acc):
@@ -381,9 +384,9 @@ def tile_list_sourdough_order_blend_kernel(
         gather_table(0)
         round_wd(0)
         quantize_wd(0)
+        deal_w4_scales()
         gather_table(1)
         round_wd(1)
-        deal_w4_scales()
         quantize_wd(1)
         first_banks = [bank() for h in range(2)]
         for h in range(2):
@@ -417,8 +420,11 @@ def tile_list_sourdough_order_blend_kernel(
                 round_dealt(0, 0, nc.scalar.copy)
             if s == 2:
                 quantize_dealt(1)
+            if s == 0:
+                dough[s + 1] = first_stage(s + 1, False)
             act[s + 1] = first_stage(s + 1, True)
-            dough[s + 1] = first_stage(s + 1, False)
+            if s > 0:
+                dough[s + 1] = first_stage(s + 1, False)
             make_share(s)
             if last - 1 - EARLY_TURNS <= s < last - 1:
                 c = s - (last - 1 - EARLY_TURNS)

@@ -24,7 +24,6 @@ BANK = 512
 SLICES = H // P
 WD_PIECES = (128, 128, 256, 512)
 EARLY_TURNS = 2
-WARM_PASSES = 4
 MOVES_ON_GPSIMD = 6
 LAST_PIECES = (256, 128, 128)
 
@@ -259,7 +258,7 @@ def tile_list_sourdough_order_blend_kernel(
         turned = keep.tile([P, 2, tiles, P, 2], BF16, name="turned", align_bytes=64)
         prev_dealt = keep.tile([P, PACK, M], F32, name="prev_dealt", align_bytes=64)
         prod_dealt = keep.tile([P, PACK, M], F32, name="prod_dealt", align_bytes=64)
-        z_bf = {0: late_z.tile([P, M, PACK], BF16, name="z_bf0", align_bytes=64, offset=0)}
+        z_bf = {(0, 2 * P * h): late_z.tile([P, 2 * P, PACK], BF16, name="z_half%d" % h, align_bytes=64, offset=16 * P * h) for h in range(2)}
         zq = [keep.tile([P, M], U32, name="zq%d" % b, align_bytes=64) for b in range(2)]
         zq_sc = [keep.tile([P, M], U8, name="zq_sc%d" % b, align_bytes=64) for b in range(2)]
 
@@ -318,12 +317,12 @@ def tile_list_sourdough_order_blend_kernel(
                     k = 2 * (c - first) + u
                     nc.tensor.transpose(acc[:, P * k : P * (k + 1)], words, ident[:])
             nc.scalar.copy(
-                out=z_bf[0][:, cols, :].rearrange("p m t -> p (m t)").bitcast(F32).rearrange("p (c m u) -> p c m u", m=P, u=2),
+                out=z_bf[0, cols.start][:].rearrange("p m t -> p (m t)").bitcast(F32).rearrange("p (c m u) -> p c m u", m=P, u=2),
                 in_=acc[:, : 2 * P * (last - first)].rearrange("p (c u m) -> p c m u", u=2, m=P),
             )
 
         def blend(cols):
-            at = 8 * cols.start if cols.start else 8 * M
+            at = 8 * M if cols.start == M // 2 else 8 * cols.start
             z_bf[1, cols.start] = late_z.tile([P, cols.stop - cols.start, PACK], BF16, name="z_piece%d" % cols.start, align_bytes=64, offset=at)
             nc.vector.tensor_tensor(
                 out=z_bf[1, cols.start][:].rearrange("p (c i) t -> p c t i", i=4),
@@ -334,18 +333,18 @@ def tile_list_sourdough_order_blend_kernel(
 
         def quantize_z(b, cols):
             nc.vector.quantize_mx(
-                out=zq[b][:, cols].bitcast(FP8X4), scales=zq_sc[b][:, cols], in_=(z_bf[0][:, cols, :] if b == 0 else z_bf[1, cols.start][:]).rearrange("p m t -> p (m t)")
+                out=zq[b][:, cols].bitcast(FP8X4), scales=zq_sc[b][:, cols], in_=z_bf[b, cols.start][:].rearrange("p m t -> p (m t)")
             )
 
         sums = {}
 
         def last_pass(cols, b, opens):
             width = cols.stop - cols.start
-            per_bank = BANK // width
+            per_bank = 2
             for c in range(N // P):
                 group, i = divmod(c, per_bank)
                 if (cols.start, group) not in sums:
-                    sums[cols.start, group] = bank(back_banks[1 - group] if cols.start == 0 else None)
+                    sums[cols.start, group] = bank(back_banks[1 + group] if cols.start == 0 else None)
                 nc.tensor.matmul_mx(
                     out=sums[cols.start, group][:, width * i : width * (i + 1)], lhsT=w8[:, b, P * c : P * (c + 1)].bitcast(FP8X4),
                     lhsT_scale=w8_sc[:, b, P * c : P * (c + 1)],
@@ -355,14 +354,14 @@ def tile_list_sourdough_order_blend_kernel(
 
         def finish(cols, on_vector):
             width = cols.stop - cols.start
-            per_bank = BANK // width
+            per_bank = 2
             for group in range(N // P // per_bank):
                 result = keep.tile([P, per_bank, width], F32, name="result%d%d" % (cols.start, group), align_bytes=64)
                 acc = sums[cols.start, group]
                 tiles_of = slice(per_bank * group, per_bank * (group + 1))
                 if group in on_vector:
                     nc.vector.tensor_tensor(
-                        out=result[:], in0=acc[:].rearrange("p (c m) -> p c m", c=per_bank),
+                        out=result[:], in0=acc[:, : per_bank * width].rearrange("p (c m) -> p c m", c=per_bank),
                         in1=bias[:, tiles_of].unsqueeze(2).to_broadcast([P, per_bank, width]), op=ALU.add,
                     )
                 else:
@@ -411,13 +410,11 @@ def tile_list_sourdough_order_blend_kernel(
                 quantize_dealt(0)
             if s > 0:
                 weigh(s - 1, whole)
-            if s == 2:
-                round_dealt(1, 1)
             pick_diff(s, whole)
             if s == 0:
                 round_wd(2)
             if s == 1:
-                round_dealt(0, 0, nc.scalar.copy)
+                round_dealt(0, 0)
             if s == 2:
                 quantize_dealt(1)
             if s == 0:
@@ -426,42 +423,39 @@ def tile_list_sourdough_order_blend_kernel(
             if s > 0:
                 dough[s + 1] = first_stage(s + 1, False)
             make_share(s)
+            if s == 1:
+                round_dealt(1, 1, nc.scalar.copy)
             if last - 1 - EARLY_TURNS <= s < last - 1:
                 c = s - (last - 1 - EARLY_TURNS)
                 turn([0, 1, 2, 3], slice(P * c, P * (c + 1)))
         make_share(last)
+        turn_back(halves[0])
         for c in range(EARLY_TURNS, tiles):
             turn([0, 1, 2, 3], slice(P * c, P * (c + 1)))
-        spare = banks_taken[-1]
-        for cols in halves:
-            turn_back(cols)
-        idle = bank(spare)
-        for i in range(WARM_PASSES):
-            nc.tensor.matmul_mx(
-                out=idle[:], lhsT=w8[:, 0, :P].bitcast(FP8X4), lhsT_scale=w8_sc[:, 0, :P], rhs=v[0, 0][:].bitcast(FP8X4),
-                rhs_scale=v_sc[0][:, :BANK], start=(i == 0), stop=(i == WARM_PASSES - 1),
-            )
+        back_banks.append(banks_taken[-1])
+        turn_back(halves[1])
         pick_prev(last, whole)
         weigh(last - 1, whole)
         pick_diff(last, pieces[0])
         pick_diff(last, pieces[1])
         weigh(last, pieces[0])
         pick_diff(last, pieces[2])
+        quantize_z(0, halves[0])
+        last_pass(pieces[0], 0, True)
         blend(pieces[0])
         weigh(last, pieces[1])
-        weigh(last, pieces[2])
         quantize_z(1, pieces[0])
-        last_pass(pieces[0], 1, True)
-        quantize_z(0, whole)
-        last_pass(pieces[0], 0, False)
-        last_pass(pieces[1], 0, True)
-        last_pass(pieces[2], 0, True)
+        last_pass(pieces[0], 1, False)
+        weigh(last, pieces[2])
         blend(pieces[1])
-        blend(pieces[2])
+        quantize_z(0, halves[1])
         quantize_z(1, pieces[1])
-        quantize_z(1, pieces[2])
+        last_pass(pieces[1], 0, True)
         last_pass(pieces[1], 1, False)
+        last_pass(pieces[2], 0, True)
+        blend(pieces[2])
+        quantize_z(1, pieces[2])
         last_pass(pieces[2], 1, False)
         finish(pieces[0], ())
         finish(pieces[1], ())
-        finish(pieces[2], (0,))
+        finish(pieces[2], (1,))

@@ -216,7 +216,7 @@ def tile_list_sourdough_order_blend_kernel(
                 banks_taken.append(index)
             return psum.tile([P, BANK], F32, name="acc%d" % index)
 
-        def one_pass(acc, s, is_act, h, a):
+        def one_pass(acc, s, is_act, h, a, opens):
             b, t = divmod(s, PACK)
             if is_act:
                 lhs = (w4[0], w4_dealt)[b][:, a, 2 * P * t : 2 * P * (t + 1)].bitcast(FP4X4)
@@ -226,7 +226,7 @@ def tile_list_sourdough_order_blend_kernel(
                 lhs_sc = wq_sc[a, s]
             nc.tensor.matmul_mx(
                 out=acc[:], lhsT=lhs, lhsT_scale=lhs_sc, rhs=v[a, h][:].bitcast(FP8X4),
-                rhs_scale=v_sc[a][:, BANK * h : BANK * (h + 1)], start=(a == 0), stop=(a == 1),
+                rhs_scale=v_sc[a][:, BANK * h : BANK * (h + 1)], start=opens, stop=not opens,
             )
 
         def new_window(s, is_act):
@@ -243,8 +243,9 @@ def tile_list_sourdough_order_blend_kernel(
             window = new_window(s, is_act)
             for h in range(2):
                 acc = bank()
-                for a in range(2):
-                    one_pass(acc, s, is_act, h, a)
+                order = (1, 0) if s < PACK or is_act else (0, 1)
+                for a in order:
+                    one_pass(acc, s, is_act, h, a, a == order[0])
                 empty(window, h, acc)
             return window
 
@@ -322,7 +323,7 @@ def tile_list_sourdough_order_blend_kernel(
             )
 
         def blend(cols):
-            at = 8 * M if cols.start == M // 2 else 8 * cols.start
+            at = 8 * (M + cols.start) if cols.start else 0
             z_bf[1, cols.start] = late_z.tile([P, cols.stop - cols.start, PACK], BF16, name="z_piece%d" % cols.start, align_bytes=64, offset=at)
             nc.vector.tensor_tensor(
                 out=z_bf[1, cols.start][:].rearrange("p (c i) t -> p c t i", i=4),
@@ -370,7 +371,7 @@ def tile_list_sourdough_order_blend_kernel(
                         nc.scalar.activation(
                             out=result[:, i, :], in_=acc[:, width * i : width * (i + 1)], func=ACT.Identity, bias=bias[:, c : c + 1]
                         )
-                nc.sync.dma_start(
+                (nc.sync if group in on_vector or cols.start == 0 else nc.scalar).dma_start(
                     out=out[P * tiles_of.start : P * tiles_of.stop, cols].rearrange("(c p) m -> p c m", p=P), in_=result[:]
                 )
 
@@ -389,16 +390,16 @@ def tile_list_sourdough_order_blend_kernel(
         quantize_wd(1)
         first_banks = [bank() for h in range(2)]
         for h in range(2):
-            one_pass(first_banks[h], 0, False, h, 0)
+            one_pass(first_banks[h], 0, False, h, 0, True)
         dough[0] = new_window(0, False)
         act[0] = new_window(0, True)
         act_banks = [bank() for h in range(2)]
         for h in range(2):
-            one_pass(first_banks[h], 0, False, h, 1)
+            one_pass(first_banks[h], 0, False, h, 1, False)
             empty(dough[0], h, first_banks[h])
-            one_pass(act_banks[h], 0, True, h, 0)
+            one_pass(act_banks[h], 0, True, h, 1, True)
         for h in range(2):
-            one_pass(act_banks[h], 0, True, h, 1)
+            one_pass(act_banks[h], 0, True, h, 0, False)
             empty(act[0], h, act_banks[h])
         for s in range(last):
             pick_prev(s, whole)
@@ -449,13 +450,13 @@ def tile_list_sourdough_order_blend_kernel(
         weigh(last, pieces[2])
         blend(pieces[1])
         quantize_z(0, halves[1])
-        quantize_z(1, pieces[1])
         last_pass(pieces[1], 0, True)
-        last_pass(pieces[1], 1, False)
         last_pass(pieces[2], 0, True)
         blend(pieces[2])
+        quantize_z(1, pieces[1])
         quantize_z(1, pieces[2])
+        last_pass(pieces[1], 1, False)
         last_pass(pieces[2], 1, False)
         finish(pieces[0], ())
-        finish(pieces[1], ())
+        finish(pieces[1], (1,))
         finish(pieces[2], (1,))

@@ -323,7 +323,7 @@ def tile_list_sourdough_order_blend_kernel(
             )
 
         def blend(cols):
-            at = 8 * (M + cols.start) if cols.start else 0
+            at = 8 * cols.start if cols.start > M // 2 else 0
             z_bf[1, cols.start] = late_z.tile([P, cols.stop - cols.start, PACK], BF16, name="z_piece%d" % cols.start, align_bytes=64, offset=at)
             nc.vector.tensor_tensor(
                 out=z_bf[1, cols.start][:].rearrange("p (c i) t -> p c t i", i=4),

@@ -21,18 +21,31 @@ P = 128
 PACK = 4
 PASS = P * PACK
 BANK = 512
+QUADRANT = 32
 SLICES = H // P
 WD_PIECES = (128, 128, 256, 512)
+EARLY_ACTS = 2
 EARLY_TURNS = 2
-MOVES_ON_GPSIMD = 6
 LAST_PIECES = (256, 128, 128)
 
 
-def load_scale_rows(queue, plane, scales, quadrants):
-    for q in quadrants:
+def load_plane(queue, plane, scales):
+    for r in range(4):
         queue.dma_start(
-            out=plane[q:P:32, :, :].bitcast(I32),
-            in_=scales[:, q:16:4, :].rearrange("a r c -> r a c").bitcast(I32),
+            out=plane[r:P:QUADRANT, :, :].bitcast(I32),
+            in_=scales[:, r:16:4, :].rearrange("a q c -> q a c").bitcast(I32),
+        )
+
+
+def load_spread(queue, spread, scales):
+    queue.dma_start(out=spread[0:P:4, :].bitcast(I32), in_=scales.rearrange("a q c -> q a c").bitcast(I32))
+
+
+def move_to_plane(queue, plane, spread):
+    for q in range(4):
+        queue.dma_start(
+            out=plane[QUADRANT * q : QUADRANT * q + 4, :, :].bitcast(I32),
+            in_=spread[QUADRANT * q : QUADRANT * (q + 1) : 4, :].bitcast(I32),
         )
 
 
@@ -46,7 +59,7 @@ def tile_list_sourdough_order_blend_kernel(
         arena = ctx.enter_context(tc.tile_pool(name="arena", bufs=1))
         regions = ctx.enter_context(tc.tile_pool(name="regions", bufs=1))
         late_z = ctx.enter_context(tc.tile_pool(name="late_z", bufs=1))
-        ring = ctx.enter_context(tc.tile_pool(name="ring", bufs=2))
+        ring = ctx.enter_context(tc.tile_pool(name="ring", bufs=3))
         psum = ctx.enter_context(tc.psum_pool(name="psum", bufs=1))
 
         offs_sb = lists.tile([P, S // 16], U16, name="offs_sb")
@@ -54,8 +67,69 @@ def tile_list_sourdough_order_blend_kernel(
         pos2_sb = lists.tile([P, M // 16], U16, name="pos2_sb")
         pos3_sb = lists.tile([P, M // 16], U16, name="pos3_sb")
 
-        arena_bytes = 48 * 1024
-        tab_sc = arena.tile([P, arena_bytes], U8, name="tab_sc", align_bytes=64, offset=0)
+        tab_sc = keep.tile([P, T], U8, name="tab_sc", align_bytes=64)
+        nc.vector.memset(tab_sc[:].bitcast(I32), 0)
+        load_spread(nc.scalar, tab_sc, tab_scales)
+
+        w4_sc = keep.tile([P, 2, PASS], U8, name="w4_sc", align_bytes=64)
+        w4_spread = keep.tile([P, PASS], U8, name="w4_spread", align_bytes=64)
+        v_sc = keep.tile([P, 2, S], U8, name="v_sc", align_bytes=64)
+        nc.gpsimd.memset(w4_sc[:].bitcast(I32), 0)
+        nc.gpsimd.memset(w4_spread[:].bitcast(I32), 0)
+        load_plane(nc.gpsimd, w4_sc, w4_scales[:, :, :PASS])
+        load_spread(nc.gpsimd, w4_spread, w4_scales[:, :, PASS:])
+        nc.vector.memset(v_sc[:].bitcast(I32), 0)
+        ident = keep.tile([P, P], F32, name="ident", align_bytes=64)
+        make_identity(nc, ident[:])
+
+        nc.sync.dma_start(offs_sb[:], offs)
+        nc.sync.dma_start(pos1_sb[:], pos1)
+        nc.sync.dma_start(pos3_sb[:], pos3)
+        nc.sync.dma_start(pos2_sb[:], pos2)
+
+        tab = [keep.tile([P, T], U32, name="tab%d" % a, align_bytes=64) for a in range(2)]
+
+        def load_table(a):
+            nc.sync.dma_start(out=tab[a][:].bitcast(I32), in_=tab_words[a].rearrange("p n t -> p (n t)").bitcast(I32))
+
+        def load_w4(tile, first, last):
+            nc.sync.dma_start(out=tile[:].bitcast(I32), in_=w4_words[:, :, 2 * first : 2 * last].rearrange("a p c -> p a c").bitcast(I32))
+
+        early_cols = P * EARLY_ACTS
+        w4_early = keep.tile([P, 2, 2 * early_cols], U8, name="w4_early", align_bytes=64)
+        load_table(0)
+        load_w4(w4_early, 0, early_cols)
+        load_table(1)
+
+        window_bytes = 4 * S
+        starts = [sum(WD_PIECES[:i]) for i in range(len(WD_PIECES))]
+        wd_raw = {}
+
+        def load_wd(i, a, tile):
+            width = WD_PIECES[i]
+            wd_raw[i, a] = tile[:, : PACK * width].rearrange("p (j c) -> p j c", j=PACK)
+            nc.sync.dma_start(
+                out=wd_raw[i, a],
+                in_=wd[a * PASS : (a + 1) * PASS, starts[i] : starts[i] + width].rearrange("(p j) c -> p j c", j=PACK),
+            )
+
+        load_wd(0, 0, regions.tile([P, EARLY_ACTS * S], F32, name="wd_raw00", align_bytes=64, offset=0))
+        load_wd(0, 1, keep.tile([P, PACK * WD_PIECES[0]], F32, name="wd_raw01", align_bytes=64))
+
+        warm = keep.tile([P, 1], F32, name="warm")
+        nc.vector.memset(warm[:], 0.0)
+        nc.scalar.activation(out=warm[:], in_=warm[:], func=ACT.Sigmoid)
+
+        arena_bytes = 40 * 1024
+        picked = arena.tile([P, arena_bytes], U8, name="picked", align_bytes=64, offset=0)
+        nc.vector.tensor_copy(out=picked[:, :S], in_=tab_sc[:].indirect(offs_sb[:]))
+        move_to_plane(nc.scalar, v_sc, picked[:, :S])
+
+        w4_dealt_spread = keep.tile([P, PASS], U8, name="w4_dealt_spread", align_bytes=64)
+        nc.vector.tensor_copy(
+            out=w4_dealt_spread[:].rearrange("p (t m) -> p m t", t=PACK), in_=w4_spread[:].rearrange("p (m t) -> p m t", t=PACK)
+        )
+
         placed = [0]
 
         def late_tile(shape, dtype, size, name):
@@ -63,78 +137,23 @@ def tile_list_sourdough_order_blend_kernel(
             placed.append(placed[-1] + size)
             return tile
 
-        w4_sc = keep.tile([P, 2, H], U8, name="w4_sc", align_bytes=64)
-        v_sc = [keep.tile([P, S], U8, name="v_sc%d" % a, align_bytes=64) for a in range(2)]
-        nc.gpsimd.memset(w4_sc[:].bitcast(I32), 0)
-        nc.vector.memset(tab_sc[64:P, :T].bitcast(I32), 0)
-        nc.vector.memset(tab_sc[32:64, :T].bitcast(I32), 0)
-        load_scale_rows(nc.gpsimd, w4_sc, w4_scales, range(4))
-        for a in range(2):
-            nc.vector.memset(v_sc[a][:].bitcast(I32), 0)
-        ident = keep.tile([P, P], F32, name="ident", align_bytes=64)
-        make_identity(nc, ident[:])
-
-        nc.sync.dma_start(offs_sb[:], offs)
-        nc.scalar.dma_start(out=tab_sc[0:32, :T].bitcast(I32), in_=tab_scales.rearrange("a q t -> (a q) t").bitcast(I32))
-        tab = {}
-
-        def load_table(a):
-            nc.sync.dma_start(out=tab[a][:].bitcast(I32), in_=tab_words[a].rearrange("p n t -> p (n t)").bitcast(I32))
-
-        tab[0] = keep.tile([P, T], U32, name="tab0", align_bytes=64)
-        load_table(0)
-        w4 = {}
-        wd_raw = {}
-        raw_at = {}
-        starts = [sum(WD_PIECES[:i]) for i in range(len(WD_PIECES))]
-
-        def early_tile(shape, dtype, size, name):
-            return keep.tile(shape, dtype, name=name, align_bytes=64)
-
-        def load_w4(b):
-            w4[b] = late_tile([P, 2, 2 * PASS], U8, 4 * PASS, "w4_%d" % b)
-            nc.sync.dma_start(
-                out=w4[b][:].bitcast(I32), in_=w4_words[:, :, 2 * PASS * b : 2 * PASS * (b + 1)].rearrange("a p c -> p a c").bitcast(I32)
-            )
-
-        def load_wd(i, place):
-            width = WD_PIECES[i]
-            raw_at[i] = placed[-1]
-            wd_raw[i] = place([P, 2, PACK, width], F32, 8 * PACK * width, "wd_raw%d" % i)
+        def load_late_wd(i):
             for a in range(2):
-                nc.sync.dma_start(
-                    out=wd_raw[i][:, a, :, :],
-                    in_=wd[a * PASS : (a + 1) * PASS, starts[i] : starts[i] + width].rearrange("(p j) c -> p j c", j=PACK),
-                )
+                load_wd(i, a, late_tile([P, PACK * WD_PIECES[i]], F32, 16 * WD_PIECES[i], "wd_raw%d%d" % (i, a)))
 
-        load_wd(0, early_tile)
-        nc.sync.dma_start(pos1_sb[:], pos1)
-        nc.sync.dma_start(pos3_sb[:], pos3)
-        nc.sync.dma_start(pos2_sb[:], pos2)
-        tab[1] = arena.tile([P, T], U32, name="tab1", align_bytes=64, offset=arena_bytes)
-        load_table(1)
-        warm = keep.tile([P, 1], F32, name="warm")
-        nc.vector.memset(warm[:], 0.0)
-        nc.scalar.activation(out=warm[:], in_=warm[:], func=ACT.Sigmoid)
-
-        picked_sc = keep.tile([P, S], U8, name="picked_sc", align_bytes=64)
-        nc.vector.tensor_copy(out=picked_sc[:], in_=tab_sc[:, :T].indirect(offs_sb[:]))
-        for a in range(2):
-            for q in range(4):
-                (nc.gpsimd if 4 * a + q < MOVES_ON_GPSIMD else nc.sync).dma_start(
-                    out=v_sc[a][q:P:32, :].bitcast(I32), in_=picked_sc[16 * a + q : 16 * a + 16 : 4, :].bitcast(I32)
-                )
-
-        load_w4(0)
-        load_wd(1, late_tile)
-        load_w4(1)
-        load_wd(2, late_tile)
-        load_wd(3, late_tile)
+        load_late_wd(1)
+        w4_late = late_tile([P, 2, 2 * (H - early_cols)], U8, 4 * (H - early_cols), "w4_late")
+        load_w4(w4_late, early_cols, H)
+        load_late_wd(2)
+        load_late_wd(3)
+        w4_dealt_sc = late_tile([P, 2, PASS], U8, 2 * PASS, "w4_dealt_sc")
+        nc.gpsimd.memset(w4_dealt_sc[:].bitcast(I32), 0)
+        move_to_plane(nc.sync, w4_dealt_sc, w4_dealt_spread)
         w8 = late_tile([P, 2, N], U32, 8 * N, "w8")
         nc.sync.dma_start(out=w8[:].bitcast(I32), in_=w8_words.rearrange("a p n t -> p a (n t)").bitcast(I32))
         w8_sc = late_tile([P, 2, N], U8, 2 * N, "w8_sc")
-        nc.vector.memset(w8_sc[:].bitcast(I32), 0)
-        load_scale_rows(nc.sync, w8_sc, w8_scales, range(4))
+        nc.gpsimd.memset(w8_sc[:].bitcast(I32), 0)
+        load_plane(nc.sync, w8_sc, w8_scales)
         bias = late_tile([P, N // P], F32, 64, "bias")
         with nc.allow_non_contiguous_dma(reason="one bias value a partition and output tile"):
             nc.sync.dma_start(out=bias[:], in_=crumb0.rearrange("(c p) -> p c", p=P))
@@ -146,66 +165,50 @@ def tile_list_sourdough_order_blend_kernel(
                 v[a, h] = keep.tile([P, BANK], U32, name="v%d%d" % (a, h), align_bytes=64)
                 nc.vector.tensor_copy(out=v[a, h][:], in_=tab[a][:].indirect(offs_sb[:, 32 * h : 32 * h + 32]))
 
+        rounded = {}
         wq = {}
         wq_sc = {}
-        grouped = {}
-        region_bytes = 6 * 1024
 
-        def after_share(s, shape, dtype, offset, name):
-            if s < 0:
-                return keep.tile(shape, dtype, name=name, align_bytes=64)
-            return regions.tile(shape, dtype, name=name, align_bytes=64, offset=region_bytes * (s % 4) + offset)
-
-        def round_wd(i):
-            grouped[i] = keep.tile([P, 2, WD_PIECES[i], PACK], BF16, name="wd_bf%d" % i, tag="wd_bf%d" % i, align_bytes=64)
-            nc.vector.tensor_copy(
-                out=grouped[i][:].rearrange("p a (c i) j -> p a c j i", i=4),
-                in_=wd_raw[i][:].rearrange("p a j (c i) -> p a c j i", i=4),
-            )
-
-        def quantize_wd(i):
+        def round_wd(i, a, copy):
             width = WD_PIECES[i]
-            codes = keep.tile([P, 2, width], U32, name="wq%d" % i, align_bytes=64)
-            plane = keep.tile([P, 2, width], U8, name="wq_sc%d" % i, align_bytes=64)
-            nc.vector.quantize_mx(
-                out=codes[:].rearrange("p a c -> p (a c)").bitcast(FP8X4), scales=plane[:].rearrange("p a c -> p (a c)"),
-                in_=grouped[i][:].rearrange("p a c j -> p (a c j)"),
-            )
-            for a in range(2):
-                for s in range(starts[i] // P, (starts[i] + width) // P):
-                    cols = slice(P * s - starts[i], P * (s + 1) - starts[i])
-                    wq[a, s] = codes[:, a, cols]
-                    wq_sc[a, s] = plane[:, a, cols]
+            if i == 0 or i == 3:
+                rounded[i, a] = keep.tile([P, PACK * width], BF16, name="wd_bf%d%d" % (i, a), align_bytes=64)[:]
+            else:
+                if (i, 0) not in rounded:
+                    both = keep.tile([P, 2 * PACK * width], BF16, name="wd_bf%d" % i, align_bytes=64)
+                    rounded[i] = both[:]
+                    for b in range(2):
+                        rounded[i, b] = both[:, PACK * width * b : PACK * width * (b + 1)]
+            if i == 3:
+                copy(
+                    out=rounded[i, a].rearrange("p (t m j) -> p m j t", t=PACK, j=PACK),
+                    in_=wd_raw[i, a].rearrange("p j (m t) -> p m j t", t=PACK),
+                )
+            else:
+                copy(
+                    out=rounded[i, a].rearrange("p (c i j) -> p c j i", i=4, j=PACK),
+                    in_=wd_raw[i, a].rearrange("p j (c i) -> p c j i", i=4),
+                )
 
-        def round_dealt(a, held, copy=nc.vector.tensor_copy):
-            grouped["dealt", a] = after_share(held, [P, PACK, P, PACK], BF16, 2048, "wd_dealt%d" % a)
-            copy(
-                out=grouped["dealt", a][:].rearrange("p t m j -> p m j t"),
-                in_=wd_raw[3][:, a, :, :].rearrange("p j (m t) -> p m j t", t=PACK),
-            )
+        def quantize_wd(i, passes):
+            width = WD_PIECES[i]
+            name = "%d%d" % (i, passes[0])
+            codes = keep.tile([P, len(passes) * width], U32, name="wq" + name, align_bytes=64)
+            plane = keep.tile([P, len(passes) * width], U8, name="wq_sc" + name, align_bytes=64)
+            source = rounded[i] if len(passes) == 2 else rounded[i, passes[0]]
+            nc.vector.quantize_mx(out=codes[:].bitcast(FP8X4), scales=plane[:], in_=source)
+            for k, a in enumerate(passes):
+                for t in range(width // P):
+                    cols = slice(width * k + P * t, width * k + P * (t + 1))
+                    wq[a, starts[i] // P + t] = codes[:, cols]
+                    wq_sc[a, starts[i] // P + t] = plane[:, cols]
 
-        def quantize_dealt(a):
-            codes = keep.tile([P, PASS], U32, name="wq_dealt%d" % a, align_bytes=64)
-            plane = keep.tile([P, PASS], U8, name="wq_dealt_sc%d" % a, align_bytes=64)
-            nc.vector.quantize_mx(out=codes[:].bitcast(FP8X4), scales=plane[:], in_=grouped["dealt", a][:].rearrange("p t m j -> p (t m j)"))
-            for t in range(PACK):
-                wq[a, PACK + t] = codes[:, P * t : P * (t + 1)]
-                wq_sc[a, PACK + t] = plane[:, P * t : P * (t + 1)]
-
-        w4_dealt = arena.tile([P, 2, 2 * PASS], U8, name="w4_dealt", align_bytes=64, offset=arena_bytes)
-        w4_dealt_sc = []
+        w4_dealt = keep.tile([P, 2, 2 * PASS], U8, name="w4_dealt", align_bytes=64)
 
         def deal_w4_words():
             nc.vector.tensor_copy(
                 out=w4_dealt[:].bitcast(U16).rearrange("p a (t m) -> p a m t", t=PACK),
-                in_=w4[1][:].bitcast(U16).rearrange("p a (m t) -> p a m t", t=PACK),
-            )
-
-        def deal_w4_scales():
-            w4_dealt_sc.append(keep.tile([P, 2, PASS], U8, name="w4_dealt_sc", tag="wd_bf0", align_bytes=64))
-            nc.vector.tensor_copy(
-                out=w4_dealt_sc[0][:].rearrange("p a (t m) -> p a m t", t=PACK),
-                in_=w4_sc[:, :, PASS:].rearrange("p a (m t) -> p a m t", t=PACK),
+                in_=w4_late[:, :, 2 * (PASS - early_cols) :].bitcast(U16).rearrange("p a (m t) -> p a m t", t=PACK),
             )
 
         banks_taken = []
@@ -217,44 +220,51 @@ def tile_list_sourdough_order_blend_kernel(
             return psum.tile([P, BANK], F32, name="acc%d" % index)
 
         def one_pass(acc, s, is_act, h, a, opens):
-            b, t = divmod(s, PACK)
-            if is_act:
-                lhs = (w4[0], w4_dealt)[b][:, a, 2 * P * t : 2 * P * (t + 1)].bitcast(FP4X4)
-                lhs_sc = (w4_sc, w4_dealt_sc[0])[b][:, a, P * t : P * (t + 1)]
-            else:
+            if not is_act:
                 lhs = wq[a, s].bitcast(FP8X4)
                 lhs_sc = wq_sc[a, s]
+            else:
+                if s < EARLY_ACTS:
+                    words, t = w4_early, s
+                elif s < PACK:
+                    words, t = w4_late, s - EARLY_ACTS
+                else:
+                    words, t = w4_dealt, s - PACK
+                lhs = words[:, a, 2 * P * t : 2 * P * (t + 1)].bitcast(FP4X4)
+                lhs_sc = (w4_sc, w4_dealt_sc)[s // PACK][:, a, P * (s % PACK) : P * (s % PACK + 1)]
             nc.tensor.matmul_mx(
                 out=acc[:], lhsT=lhs, lhsT_scale=lhs_sc, rhs=v[a, h][:].bitcast(FP8X4),
-                rhs_scale=v_sc[a][:, BANK * h : BANK * (h + 1)], start=opens, stop=not opens,
+                rhs_scale=v_sc[:, a, BANK * h : BANK * (h + 1)], start=opens, stop=not opens,
             )
 
-        def new_window(s, is_act):
-            if is_act:
-                return after_share(s, [P, S], F32, 0, "act_w%d" % s)
-            if s == 0:
-                return keep.tile([P, S], F32, name="dough_w0", tag="first_dough", align_bytes=64)
-            return ring.tile([P, S], F32, name="dough_w", bufs=3)
-
-        def empty(window, h, acc):
-            nc.scalar.copy(out=window[:, BANK * h : BANK * (h + 1)], in_=acc[:])
-
-        def first_stage(s, is_act):
-            window = new_window(s, is_act)
-            for h in range(2):
-                acc = bank()
-                order = (1, 0) if s < PACK or is_act else (0, 1)
-                for a in order:
-                    one_pass(acc, s, is_act, h, a, a == order[0])
-                empty(window, h, acc)
-            return window
+        def in_region(s, shape, name):
+            return regions.tile(shape, F32, name=name, align_bytes=64, offset=window_bytes * (s % 4))
 
         act = {}
-        share = {}
         dough = {}
+        share = {}
         prev = {}
         diff = {}
         prod = {}
+
+        def new_window(s, is_act):
+            if is_act:
+                act[s] = in_region(s, [P, S], "act_w%d" % s)
+                return act[s]
+            dough[s] = ring.tile([P, S], F32, name="dough_w", bufs=4)
+            return dough[s]
+
+        def empty(window, h, acc, copy=nc.scalar.copy):
+            copy(out=window[:, BANK * h : BANK * (h + 1)], in_=acc[:])
+
+        def first_stage(s, is_act, order=(0, 1)):
+            window = new_window(s, is_act)
+            for h in range(2):
+                acc = bank()
+                for a in order:
+                    one_pass(acc, s, is_act, h, a, a == order[0])
+                empty(window, h, acc)
+
         tiles = M // P
         turned = keep.tile([P, 2, tiles, P, 2], BF16, name="turned", align_bytes=64)
         prev_dealt = keep.tile([P, PACK, M], F32, name="prev_dealt", align_bytes=64)
@@ -271,17 +281,21 @@ def tile_list_sourdough_order_blend_kernel(
             return slice(cols.start // 16, cols.stop // 16)
 
         def pick_prev(s, cols):
-            if s < PACK:
-                prev[s] = keep.tile([P, M], F32, name="prev%d" % s, tag="wd_bf1" if s == 0 else "prev%d" % s, align_bytes=64)[:]
-                prod[s] = ring.tile([P, M], F32, name="prod", bufs=4)[:]
-            else:
-                prev[s] = prev_dealt[:, s - PACK, :]
-                prod[s] = prod_dealt[:, s - PACK, :]
+            if s not in prev:
+                if s < PACK:
+                    prev[s] = keep.tile([P, M], F32, name="prev%d" % s, align_bytes=64)[:]
+                    prod[s] = keep.tile([P, M], F32, name="prod%d" % s, align_bytes=64)[:]
+                else:
+                    prev[s] = prev_dealt[:, s - PACK, :]
+                    prod[s] = prod_dealt[:, s - PACK, :]
             nc.vector.tensor_copy(out=prev[s][:, cols], in_=dough[s][:].indirect(pos3_sb[:, entries(cols)]))
 
         def pick_diff(s, cols):
             if s not in diff:
-                diff[s] = after_share(s - 1, [P, M], F32, 0, "diff%d" % s)
+                if s == 0:
+                    diff[s] = keep.tile([P, M], F32, name="diff0", align_bytes=64)
+                else:
+                    diff[s] = in_region(s - 1, [P, M], "diff%d" % s)
             nc.vector.tensor_tensor(
                 out=diff[s][:, cols], in0=dough[s][:].indirect(pos2_sb[:, entries(cols)]), in1=prev[s][:, cols], op=ALU.subtract
             )
@@ -289,22 +303,14 @@ def tile_list_sourdough_order_blend_kernel(
         def weigh(s, cols):
             nc.vector.tensor_tensor(out=prod[s][:, cols], in0=diff[s][:, cols], in1=share[s][:, cols], op=ALU.mult)
 
-        def turn(rows, cols):
-            first, last = cols.start // P, cols.stop // P
+        def turn(cols):
             acc = bank()
-            k = 0
-            for c in range(first, last):
-                for t in rows:
-                    for i, term in enumerate((prod[t], prev[t])):
-                        nc.tensor.matmul(
-                            out=acc[:, P * k : P * (k + 1)], lhsT=term[:, P * c : P * (c + 1)], rhs=ident[:],
-                            is_transpose=True, start=(i == 0), stop=(i == 1),
-                        )
-                    k += 1
-            nc.scalar.copy(
-                out=turned[:, :, first:last, 32 * rows[0] : 32 * (rows[-1] + 1), :],
-                in_=acc[:].rearrange("m (c q u e) -> m u c q e", c=last - first, u=2, e=2),
-            )
+            for t in range(PACK):
+                for i, term in enumerate((prod[t], prev[t])):
+                    nc.tensor.matmul(
+                        out=acc[:, P * t : P * (t + 1)], lhsT=term[:, cols], rhs=ident[:], is_transpose=True, start=(i == 0), stop=(i == 1)
+                    )
+            nc.scalar.copy(out=turned[:, :, cols.start // P, :, :], in_=acc[:].rearrange("m (q u e) -> m u q e", u=2, e=2))
 
         back_banks = []
 
@@ -338,10 +344,10 @@ def tile_list_sourdough_order_blend_kernel(
             )
 
         sums = {}
+        per_bank = 2
 
         def last_pass(cols, b, opens):
             width = cols.stop - cols.start
-            per_bank = 2
             for c in range(N // P):
                 group, i = divmod(c, per_bank)
                 if (cols.start, group) not in sums:
@@ -355,7 +361,6 @@ def tile_list_sourdough_order_blend_kernel(
 
         def finish(cols, on_vector):
             width = cols.stop - cols.start
-            per_bank = 2
             for group in range(N // P // per_bank):
                 result = keep.tile([P, per_bank, width], F32, name="result%d%d" % (cols.start, group), align_bytes=64)
                 acc = sums[cols.start, group]
@@ -380,59 +385,81 @@ def tile_list_sourdough_order_blend_kernel(
         last = SLICES - 1
         edges = [sum(LAST_PIECES[:i]) for i in range(len(LAST_PIECES) + 1)]
         pieces = [slice(edges[i], edges[i + 1]) for i in range(len(LAST_PIECES))]
+        on_vector, on_scalar = nc.vector.tensor_copy, nc.scalar.copy
 
         gather_table(0)
-        round_wd(0)
-        quantize_wd(0)
-        deal_w4_scales()
+        act_banks = {(s, h): bank() for h in range(2) for s in range(EARLY_ACTS)}
+        for (s, h), acc in act_banks.items():
+            one_pass(acc, s, True, h, 0, True)
         gather_table(1)
-        round_wd(1)
-        quantize_wd(1)
-        first_banks = [bank() for h in range(2)]
+        round_wd(0, 0, on_scalar)
+        for s in range(EARLY_ACTS):
+            new_window(s, True)
+            one_pass(act_banks[s, 0], s, True, 0, 1, False)
+            empty(act[s], 0, act_banks[s, 0])
+        one_pass(act_banks[0, 1], 0, True, 1, 1, False)
+        empty(act[0], 1, act_banks[0, 1])
+        quantize_wd(0, (0,))
+        round_wd(0, 1, on_vector)
+        round_wd(1, 0, on_vector)
+        quantize_wd(0, (1,))
+        dough_banks = [bank() for h in range(2)]
         for h in range(2):
-            one_pass(first_banks[h], 0, False, h, 0, True)
-        dough[0] = new_window(0, False)
-        act[0] = new_window(0, True)
-        act_banks = [bank() for h in range(2)]
+            one_pass(dough_banks[h], 0, False, h, 0, True)
+        one_pass(act_banks[1, 1], 1, True, 1, 1, False)
+        empty(act[1], 1, act_banks[1, 1])
+        new_window(0, False)
         for h in range(2):
-            one_pass(first_banks[h], 0, False, h, 1, False)
-            empty(dough[0], h, first_banks[h])
-            one_pass(act_banks[h], 0, True, h, 1, True)
-        for h in range(2):
-            one_pass(act_banks[h], 0, True, h, 0, False)
-            empty(act[0], h, act_banks[h])
-        for s in range(last):
+            one_pass(dough_banks[h], 0, False, h, 1, False)
+        empty(dough[0], 0, dough_banks[0])
+        round_wd(1, 1, on_vector)
+        quantize_wd(1, (0, 1))
+        empty(dough[0], 1, dough_banks[1], on_vector)
+        first_stage(1, False)
+        for cols in halves:
+            pick_prev(0, cols)
+        for cols in halves:
+            pick_diff(0, cols)
+        deal_w4_words()
+        for a in range(2):
+            round_wd(2, a, on_scalar)
+        make_share(0)
+        pick_prev(1, whole)
+        quantize_wd(2, (0, 1))
+        weigh(0, whole)
+        pick_diff(1, whole)
+        first_stage(2, True)
+        first_stage(2, False)
+        make_share(1)
+        pick_prev(2, whole)
+        weigh(1, whole)
+        pick_diff(2, whole)
+        first_stage(3, False)
+        round_wd(3, 1, on_vector)
+        round_wd(3, 0, on_scalar)
+        make_share(2)
+        pick_prev(3, whole)
+        quantize_wd(3, (1,))
+        quantize_wd(3, (0,))
+        weigh(2, whole)
+        pick_diff(3, whole)
+        first_stage(3, True)
+        first_stage(4, True)
+        first_stage(4, False, (1, 0))
+        make_share(3)
+        for s in range(PACK, last):
             pick_prev(s, whole)
-            if s == 0:
-                deal_w4_words()
-            if s == 1:
-                quantize_wd(2)
-            if s == 2:
-                quantize_dealt(0)
-            if s > 0:
-                weigh(s - 1, whole)
+            weigh(s - 1, whole)
             pick_diff(s, whole)
-            if s == 0:
-                round_wd(2)
-            if s == 1:
-                round_dealt(0, 0)
-            if s == 2:
-                quantize_dealt(1)
-            if s == 0:
-                dough[s + 1] = first_stage(s + 1, False)
-            act[s + 1] = first_stage(s + 1, True)
-            if s > 0:
-                dough[s + 1] = first_stage(s + 1, False)
+            first_stage(s + 1, False)
             make_share(s)
-            if s == 1:
-                round_dealt(1, 1, nc.scalar.copy)
-            if last - 1 - EARLY_TURNS <= s < last - 1:
-                c = s - (last - 1 - EARLY_TURNS)
-                turn([0, 1, 2, 3], slice(P * c, P * (c + 1)))
+            first_stage(s + 1, True)
+            if s - PACK < EARLY_TURNS:
+                turn(slice(P * (s - PACK), P * (s - PACK + 1)))
         make_share(last)
         turn_back(halves[0])
         for c in range(EARLY_TURNS, tiles):
-            turn([0, 1, 2, 3], slice(P * c, P * (c + 1)))
+            turn(slice(P * c, P * (c + 1)))
         back_banks.append(banks_taken[-1])
         turn_back(halves[1])
         pick_prev(last, whole)

@@ -57,7 +57,8 @@ def tile_list_sourdough_order_blend_kernel(
         lists = ctx.enter_context(tc.tile_pool(name="lists", bufs=1))
         keep = ctx.enter_context(tc.tile_pool(name="keep", bufs=1))
         arena = ctx.enter_context(tc.tile_pool(name="arena", bufs=1))
-        regions = ctx.enter_context(tc.tile_pool(name="regions", bufs=1))
+        tables = ctx.enter_context(tc.tile_pool(name="tables", bufs=1))
+        codes_then = ctx.enter_context(tc.tile_pool(name="codes_then", bufs=1))
         late_z = ctx.enter_context(tc.tile_pool(name="late_z", bufs=1))
         ring = ctx.enter_context(tc.tile_pool(name="ring", bufs=3))
         psum = ctx.enter_context(tc.psum_pool(name="psum", bufs=1))
@@ -87,7 +88,8 @@ def tile_list_sourdough_order_blend_kernel(
         nc.sync.dma_start(pos3_sb[:], pos3)
         nc.sync.dma_start(pos2_sb[:], pos2)
 
-        tab = [keep.tile([P, T], U32, name="tab%d" % a, align_bytes=64) for a in range(2)]
+        table_bytes = 4 * T
+        tab = [tables.tile([P, T], U32, name="tab%d" % a, align_bytes=64, offset=table_bytes * a) for a in range(2)]
 
         def load_table(a):
             nc.sync.dma_start(out=tab[a][:].bitcast(I32), in_=tab_words[a].rearrange("p n t -> p (n t)").bitcast(I32))
@@ -101,7 +103,8 @@ def tile_list_sourdough_order_blend_kernel(
         load_w4(w4_early, 0, early_cols)
         load_table(1)
 
-        window_bytes = 4 * S
+        region_bytes = 6 * 1024
+        late_from = 2 * region_bytes
         starts = [sum(WD_PIECES[:i]) for i in range(len(WD_PIECES))]
         wd_raw = {}
 
@@ -113,24 +116,33 @@ def tile_list_sourdough_order_blend_kernel(
                 in_=wd[a * PASS : (a + 1) * PASS, starts[i] : starts[i] + width].rearrange("(p j) c -> p j c", j=PACK),
             )
 
-        load_wd(0, 0, regions.tile([P, EARLY_ACTS * S], F32, name="wd_raw00", align_bytes=64, offset=0))
+        load_wd(0, 0, arena.tile([P, region_bytes // 4 + S], F32, name="wd_raw00", align_bytes=64, offset=0))
         load_wd(0, 1, keep.tile([P, PACK * WD_PIECES[0]], F32, name="wd_raw01", align_bytes=64))
 
         warm = keep.tile([P, 1], F32, name="warm")
         nc.vector.memset(warm[:], 0.0)
         nc.scalar.activation(out=warm[:], in_=warm[:], func=ACT.Sigmoid)
 
-        arena_bytes = 40 * 1024
-        picked = arena.tile([P, arena_bytes], U8, name="picked", align_bytes=64, offset=0)
+        arena_bytes = 42 * 1024
+        picked = arena.tile([P, arena_bytes], U8, name="picked", align_bytes=64, offset=late_from)
         nc.vector.tensor_copy(out=picked[:, :S], in_=tab_sc[:].indirect(offs_sb[:]))
         move_to_plane(nc.scalar, v_sc, picked[:, :S])
 
-        w4_dealt_spread = keep.tile([P, PASS], U8, name="w4_dealt_spread", align_bytes=64)
+        v = {}
+
+        def gather_table(a):
+            for h in range(2):
+                v[a, h] = keep.tile([P, BANK], U32, name="v%d%d" % (a, h), align_bytes=64)
+                nc.vector.tensor_copy(out=v[a, h][:], in_=tab[a][:].indirect(offs_sb[:, 32 * h : 32 * h + 32]))
+
+        gather_table(0)
+        w4_dealt_spread = tables.tile([P, PASS], U8, name="w4_dealt_spread", align_bytes=64, offset=0)
         nc.vector.tensor_copy(
             out=w4_dealt_spread[:].rearrange("p (t m) -> p m t", t=PACK), in_=w4_spread[:].rearrange("p (m t) -> p m t", t=PACK)
         )
 
-        placed = [0]
+        placed = [3 * region_bytes + 16 * WD_PIECES[3]]
+        raw_at = {(2, 0): 2 * region_bytes, (3, 0): 3 * region_bytes}
 
         def late_tile(shape, dtype, size, name):
             tile = arena.tile(shape, dtype, name=name, align_bytes=64, offset=placed[-1])
@@ -139,7 +151,13 @@ def tile_list_sourdough_order_blend_kernel(
 
         def load_late_wd(i):
             for a in range(2):
-                load_wd(i, a, late_tile([P, PACK * WD_PIECES[i]], F32, 16 * WD_PIECES[i], "wd_raw%d%d" % (i, a)))
+                name = "wd_raw%d%d" % (i, a)
+                if (i, a) in raw_at:
+                    tile = arena.tile([P, PACK * WD_PIECES[i]], F32, name=name, align_bytes=64, offset=raw_at[i, a])
+                else:
+                    raw_at[i, a] = placed[-1]
+                    tile = late_tile([P, PACK * WD_PIECES[i]], F32, 16 * WD_PIECES[i], name)
+                load_wd(i, a, tile)
 
         load_late_wd(1)
         w4_late = late_tile([P, 2, 2 * (H - early_cols)], U8, 4 * (H - early_cols), "w4_late")
@@ -158,27 +176,27 @@ def tile_list_sourdough_order_blend_kernel(
         with nc.allow_non_contiguous_dma(reason="one bias value a partition and output tile"):
             nc.sync.dma_start(out=bias[:], in_=crumb0.rearrange("(c p) -> p c", p=P))
 
-        v = {}
-
-        def gather_table(a):
-            for h in range(2):
-                v[a, h] = keep.tile([P, BANK], U32, name="v%d%d" % (a, h), align_bytes=64)
-                nc.vector.tensor_copy(out=v[a, h][:], in_=tab[a][:].indirect(offs_sb[:, 32 * h : 32 * h + 32]))
-
         rounded = {}
         wq = {}
         wq_sc = {}
 
         def round_wd(i, a, copy):
             width = WD_PIECES[i]
-            if i == 0 or i == 3:
-                rounded[i, a] = keep.tile([P, PACK * width], BF16, name="wd_bf%d%d" % (i, a), align_bytes=64)[:]
-            else:
-                if (i, 0) not in rounded:
-                    both = keep.tile([P, 2 * PACK * width], BF16, name="wd_bf%d" % i, align_bytes=64)
-                    rounded[i] = both[:]
-                    for b in range(2):
-                        rounded[i, b] = both[:, PACK * width * b : PACK * width * (b + 1)]
+            name = "wd_bf%d%d" % (i, a)
+            if (i, a) == (0, 0):
+                rounded[i, a] = late_tile([P, PACK * width], BF16, 8 * width, name)[:]
+            elif i == 0:
+                rounded[i, a] = tables.tile([P, PACK * width], BF16, name=name, align_bytes=64, offset=table_bytes)[:]
+            elif i == 3:
+                rounded[i, a] = arena.tile([P, PACK * width], BF16, name=name, align_bytes=64, offset=(region_bytes + 4 * M) * a)[:]
+            elif (i, 0) not in rounded:
+                if i == 1:
+                    both = tables.tile([P, 2 * PACK * width], BF16, name=name, align_bytes=64, offset=table_bytes + 2048)
+                else:
+                    both = codes_then.tile([P, 2 * PACK * width], BF16, name=name, align_bytes=64, offset=4 * PASS)
+                rounded[i] = both[:]
+                for b in range(2):
+                    rounded[i, b] = both[:, PACK * width * b : PACK * width * (b + 1)]
             if i == 3:
                 copy(
                     out=rounded[i, a].rearrange("p (t m j) -> p m j t", t=PACK, j=PACK),
@@ -193,7 +211,14 @@ def tile_list_sourdough_order_blend_kernel(
         def quantize_wd(i, passes):
             width = WD_PIECES[i]
             name = "%d%d" % (i, passes[0])
-            codes = keep.tile([P, len(passes) * width], U32, name="wq" + name, align_bytes=64)
+            if (i, passes) == (0, (0,)):
+                codes = tables.tile([P, width], U32, name="wq" + name, align_bytes=64, offset=table_bytes + 1024)
+            elif (i, passes) == (0, (1,)):
+                codes = codes_then.tile([P, width], U32, name="wq" + name, align_bytes=64, offset=0)
+            elif i == 1:
+                codes = codes_then.tile([P, 2 * width], U32, name="wq" + name, align_bytes=64, offset=4 * PASS)
+            else:
+                codes = keep.tile([P, len(passes) * width], U32, name="wq" + name, align_bytes=64)
             plane = keep.tile([P, len(passes) * width], U8, name="wq_sc" + name, align_bytes=64)
             source = rounded[i] if len(passes) == 2 else rounded[i, passes[0]]
             nc.vector.quantize_mx(out=codes[:].bitcast(FP8X4), scales=plane[:], in_=source)
@@ -203,7 +228,7 @@ def tile_list_sourdough_order_blend_kernel(
                     wq[a, starts[i] // P + t] = codes[:, cols]
                     wq_sc[a, starts[i] // P + t] = plane[:, cols]
 
-        w4_dealt = keep.tile([P, 2, 2 * PASS], U8, name="w4_dealt", align_bytes=64)
+        w4_dealt = codes_then.tile([P, 2, 2 * PASS], U8, name="w4_dealt", align_bytes=64, offset=0)
 
         def deal_w4_words():
             nc.vector.tensor_copy(
@@ -212,10 +237,13 @@ def tile_list_sourdough_order_blend_kernel(
             )
 
         banks_taken = []
+        first_banks = (0, 2, 1, 3, 4, 5, 6, 7, 4, 5, 0, 1, 2, 3, 6, 7, 2, 3, 0, 1)
+        later_banks = (4, 5, 6, 7, 2, 3, 0, 1)
 
         def bank(index=None):
             if index is None:
-                index = len(banks_taken) % 8
+                taken = len(banks_taken)
+                index = first_banks[taken] if taken < len(first_banks) else later_banks[(taken - len(first_banks)) % 8]
                 banks_taken.append(index)
             return psum.tile([P, BANK], F32, name="acc%d" % index)
 
@@ -238,7 +266,7 @@ def tile_list_sourdough_order_blend_kernel(
             )
 
         def in_region(s, shape, name):
-            return regions.tile(shape, F32, name=name, align_bytes=64, offset=window_bytes * (s % 4))
+            return arena.tile(shape, F32, name=name, align_bytes=64, offset=region_bytes * (s % 4))
 
         act = {}
         dough = {}
@@ -274,7 +302,10 @@ def tile_list_sourdough_order_blend_kernel(
         zq_sc = [keep.tile([P, M], U8, name="zq_sc%d" % b, align_bytes=64) for b in range(2)]
 
         def make_share(s):
-            share[s] = ring.tile([P, M], F32, name="share", bufs=3)
+            if s < EARLY_ACTS:
+                share[s] = arena.tile([P, M], F32, name="share%d" % s, align_bytes=64, offset=raw_at[2, 1] + 4 * M * s)
+            else:
+                share[s] = ring.tile([P, M], F32, name="share", bufs=3)
             nc.scalar.activation(out=share[s][:], in_=act[s][:].indirect(pos1_sb[:]), func=ACT.Sigmoid)
 
         def entries(cols):
@@ -387,7 +418,6 @@ def tile_list_sourdough_order_blend_kernel(
         pieces = [slice(edges[i], edges[i + 1]) for i in range(len(LAST_PIECES))]
         on_vector, on_scalar = nc.vector.tensor_copy, nc.scalar.copy
 
-        gather_table(0)
         act_banks = {(s, h): bank() for h in range(2) for s in range(EARLY_ACTS)}
         for (s, h), acc in act_banks.items():
             one_pass(acc, s, True, h, 0, True)

@@ -37,15 +37,15 @@ def load_plane(queue, plane, scales):
         )
 
 
-def load_spread(queue, spread, scales):
-    queue.dma_start(out=spread[0:P:4, :].bitcast(I32), in_=scales.rearrange("a q c -> q a c").bitcast(I32))
+def load_spread(queue, spread, scales, step=4):
+    queue.dma_start(out=spread[0 : 32 * step : step, :].bitcast(I32), in_=scales.rearrange("a q c -> q a c").bitcast(I32))
 
 
-def move_to_plane(queue, plane, spread):
+def move_to_plane(queue, plane, spread, step=4):
     for q in range(4):
         queue.dma_start(
             out=plane[QUADRANT * q : QUADRANT * q + 4, :, :].bitcast(I32),
-            in_=spread[QUADRANT * q : QUADRANT * (q + 1) : 4, :].bitcast(I32),
+            in_=spread[8 * step * q : 8 * step * (q + 1) : step, :].bitcast(I32),
         )
 
 
@@ -69,24 +69,21 @@ def tile_list_sourdough_order_blend_kernel(
         pos3_sb = lists.tile([P, M // 16], U16, name="pos3_sb")
 
         tab_sc = keep.tile([P, T], U8, name="tab_sc", align_bytes=64)
-        nc.vector.memset(tab_sc[:].bitcast(I32), 0)
-        load_spread(nc.scalar, tab_sc, tab_scales)
+        load_spread(nc.scalar, tab_sc[P - 32 :, :], tab_scales, 1)
 
         w4_sc = keep.tile([P, 2, PASS], U8, name="w4_sc", align_bytes=64)
         w4_spread = keep.tile([P, PASS], U8, name="w4_spread", align_bytes=64)
         v_sc = keep.tile([P, 2, S], U8, name="v_sc", align_bytes=64)
-        nc.gpsimd.memset(w4_sc[:].bitcast(I32), 0)
+        nc.vector.memset(w4_sc[:].bitcast(I32), 0)
+        nc.vector.memset(tab_sc[: P - 32, :].bitcast(I32), 0)
         nc.gpsimd.memset(w4_spread[:].bitcast(I32), 0)
-        load_plane(nc.gpsimd, w4_sc, w4_scales[:, :, :PASS])
         load_spread(nc.gpsimd, w4_spread, w4_scales[:, :, PASS:])
         nc.vector.memset(v_sc[:].bitcast(I32), 0)
         ident = keep.tile([P, P], F32, name="ident", align_bytes=64)
         make_identity(nc, ident[:])
 
         nc.sync.dma_start(offs_sb[:], offs)
-        nc.sync.dma_start(pos1_sb[:], pos1)
-        nc.sync.dma_start(pos3_sb[:], pos3)
-        nc.sync.dma_start(pos2_sb[:], pos2)
+        load_plane(nc.sync, w4_sc, w4_scales[:, :, :PASS])
 
         table_bytes = 4 * T
         tab = [tables.tile([P, T], U32, name="tab%d" % a, align_bytes=64, offset=table_bytes * a) for a in range(2)]
@@ -99,12 +96,17 @@ def tile_list_sourdough_order_blend_kernel(
 
         early_cols = P * EARLY_ACTS
         w4_early = keep.tile([P, 2, 2 * early_cols], U8, name="w4_early", align_bytes=64)
-        load_table(0)
         load_w4(w4_early, 0, early_cols)
+        load_table(0)
+        nc.sync.dma_start(pos1_sb[:], pos1)
+        nc.sync.dma_start(pos3_sb[:], pos3)
+        picked = keep.tile([P, S], U8, name="picked", align_bytes=64)
+        nc.vector.tensor_copy(out=picked[:], in_=tab_sc[:].indirect(offs_sb[:]))
+        move_to_plane(nc.sync, v_sc, picked[P - 32 :, :], 1)
         load_table(1)
+        nc.sync.dma_start(pos2_sb[:], pos2)
 
         region_bytes = 6 * 1024
-        late_from = 2 * region_bytes
         starts = [sum(WD_PIECES[:i]) for i in range(len(WD_PIECES))]
         wd_raw = {}
 
@@ -123,11 +125,6 @@ def tile_list_sourdough_order_blend_kernel(
         nc.vector.memset(warm[:], 0.0)
         nc.scalar.activation(out=warm[:], in_=warm[:], func=ACT.Sigmoid)
 
-        arena_bytes = 42 * 1024
-        picked = arena.tile([P, arena_bytes], U8, name="picked", align_bytes=64, offset=late_from)
-        nc.vector.tensor_copy(out=picked[:, :S], in_=tab_sc[:].indirect(offs_sb[:]))
-        move_to_plane(nc.scalar, v_sc, picked[:, :S])
-
         v = {}
 
         def gather_table(a):
@@ -142,7 +139,7 @@ def tile_list_sourdough_order_blend_kernel(
         )
 
         placed = [3 * region_bytes + 16 * WD_PIECES[3]]
-        raw_at = {(2, 0): 2 * region_bytes, (3, 0): 3 * region_bytes}
+        raw_at = {(2, 1): 2 * region_bytes, (3, 0): 3 * region_bytes}
 
         def late_tile(shape, dtype, size, name):
             tile = arena.tile(shape, dtype, name=name, align_bytes=64, offset=placed[-1])
@@ -153,7 +150,8 @@ def tile_list_sourdough_order_blend_kernel(
             for a in range(2):
                 name = "wd_raw%d%d" % (i, a)
                 if (i, a) in raw_at:
-                    tile = arena.tile([P, PACK * WD_PIECES[i]], F32, name=name, align_bytes=64, offset=raw_at[i, a])
+                    columns = max(PACK * WD_PIECES[i], region_bytes // 4)
+                    tile = arena.tile([P, columns], F32, name=name, align_bytes=64, offset=raw_at[i, a])
                 else:
                     raw_at[i, a] = placed[-1]
                     tile = late_tile([P, PACK * WD_PIECES[i]], F32, 16 * WD_PIECES[i], name)
@@ -237,8 +235,8 @@ def tile_list_sourdough_order_blend_kernel(
             )
 
         banks_taken = []
-        first_banks = (0, 2, 1, 3, 4, 5, 6, 7, 4, 5, 0, 1, 2, 3, 6, 7, 2, 3, 0, 1)
-        later_banks = (4, 5, 6, 7, 2, 3, 0, 1)
+        first_banks = (0, 2, 1, 4, 5, 1, 6, 7, 4, 5, 0, 3, 2, 1, 6, 7, 2, 1, 0, 3)
+        later_banks = (4, 5, 6, 7, 2, 1, 0, 3)
 
         def bank(index=None):
             if index is None:
@@ -302,8 +300,10 @@ def tile_list_sourdough_order_blend_kernel(
         zq_sc = [keep.tile([P, M], U8, name="zq_sc%d" % b, align_bytes=64) for b in range(2)]
 
         def make_share(s):
-            if s < EARLY_ACTS:
-                share[s] = arena.tile([P, M], F32, name="share%d" % s, align_bytes=64, offset=raw_at[2, 1] + 4 * M * s)
+            if s == 0:
+                share[s] = arena.tile([P, M], F32, name="share0", align_bytes=64, offset=raw_at[2, 1] + 4 * S)
+            elif s == 1:
+                share[s] = codes_then.tile([P, M], F32, name="share1", align_bytes=64, offset=4 * PASS)
             else:
                 share[s] = ring.tile([P, M], F32, name="share", bufs=3)
             nc.scalar.activation(out=share[s][:], in_=act[s][:].indirect(pos1_sb[:]), func=ACT.Sigmoid)
@@ -418,7 +418,7 @@ def tile_list_sourdough_order_blend_kernel(
         pieces = [slice(edges[i], edges[i + 1]) for i in range(len(LAST_PIECES))]
         on_vector, on_scalar = nc.vector.tensor_copy, nc.scalar.copy
 
-        act_banks = {(s, h): bank() for h in range(2) for s in range(EARLY_ACTS)}
+        act_banks = {key: bank() for key in ((0, 0), (1, 0), (0, 1))}
         for (s, h), acc in act_banks.items():
             one_pass(acc, s, True, h, 0, True)
         gather_table(1)
@@ -436,8 +436,6 @@ def tile_list_sourdough_order_blend_kernel(
         dough_banks = [bank() for h in range(2)]
         for h in range(2):
             one_pass(dough_banks[h], 0, False, h, 0, True)
-        one_pass(act_banks[1, 1], 1, True, 1, 1, False)
-        empty(act[1], 1, act_banks[1, 1])
         new_window(0, False)
         for h in range(2):
             one_pass(dough_banks[h], 0, False, h, 1, False)
@@ -445,6 +443,10 @@ def tile_list_sourdough_order_blend_kernel(
         round_wd(1, 1, on_vector)
         quantize_wd(1, (0, 1))
         empty(dough[0], 1, dough_banks[1], on_vector)
+        acc = bank()
+        for a in range(2):
+            one_pass(acc, 1, True, 1, a, a == 0)
+        empty(act[1], 1, acc)
         first_stage(1, False)
         for cols in halves:
             pick_prev(0, cols)

@@ -186,7 +186,7 @@ def tile_list_sourdough_order_blend_kernel(
             elif i == 0:
                 rounded[i, a] = tables.tile([P, PACK * width], BF16, name=name, align_bytes=64, offset=table_bytes)[:]
             elif i == 3:
-                rounded[i, a] = arena.tile([P, PACK * width], BF16, name=name, align_bytes=64, offset=(region_bytes + 4 * M) * a)[:]
+                rounded[i, a] = arena.tile([P, PACK * width], BF16, name=name, align_bytes=64, offset=4 * M + region_bytes * a)[:]
             elif (i, 0) not in rounded:
                 if i == 1:
                     both = tables.tile([P, 2 * PACK * width], BF16, name=name, align_bytes=64, offset=table_bytes + 2048)
@@ -463,21 +463,21 @@ def tile_list_sourdough_order_blend_kernel(
         first_stage(2, True)
         first_stage(2, False)
         make_share(1)
+        round_wd(3, 0, on_vector)
         pick_prev(2, whole)
+        quantize_wd(3, (0,))
         weigh(1, whole)
         pick_diff(2, whole)
         first_stage(3, False)
         round_wd(3, 1, on_vector)
-        round_wd(3, 0, on_scalar)
         make_share(2)
         pick_prev(3, whole)
         quantize_wd(3, (1,))
-        quantize_wd(3, (0,))
         weigh(2, whole)
         pick_diff(3, whole)
         first_stage(3, True)
         first_stage(4, True)
-        first_stage(4, False, (1, 0))
+        first_stage(4, False)
         make_share(3)
         for s in range(PACK, last):
             pick_prev(s, whole)

@@ -23,9 +23,8 @@ PASS = P * PACK
 BANK = 512
 QUADRANT = 32
 SLICES = H // P
-WD_PIECES = (128, 128, 256, 512)
+WD_PIECES = (256, 256, 512)
 EARLY_ACTS = 2
-EARLY_TURNS = 2
 LAST_PIECES = (256, 128, 128)
 
 
@@ -37,15 +36,15 @@ def load_plane(queue, plane, scales):
         )
 
 
-def load_spread(queue, spread, scales, step=4):
-    queue.dma_start(out=spread[0 : 32 * step : step, :].bitcast(I32), in_=scales.rearrange("a q c -> q a c").bitcast(I32))
+def load_spread(queue, spread, scales):
+    queue.dma_start(out=spread[P - QUADRANT :, :].bitcast(I32), in_=scales.rearrange("a q c -> q a c").bitcast(I32))
 
 
-def move_to_plane(queue, plane, spread, step=4):
+def move_to_plane(queue, plane, spread):
     for q in range(4):
         queue.dma_start(
             out=plane[QUADRANT * q : QUADRANT * q + 4, :, :].bitcast(I32),
-            in_=spread[8 * step * q : 8 * step * (q + 1) : step, :].bitcast(I32),
+            in_=spread[P - QUADRANT + 8 * q : P - QUADRANT + 8 * (q + 1), :].bitcast(I32),
         )
 
 
@@ -69,57 +68,69 @@ def tile_list_sourdough_order_blend_kernel(
         pos3_sb = lists.tile([P, M // 16], U16, name="pos3_sb")
 
         tab_sc = keep.tile([P, T], U8, name="tab_sc", align_bytes=64)
-        load_spread(nc.scalar, tab_sc[P - 32 :, :], tab_scales, 1)
+        load_spread(nc.scalar, tab_sc, tab_scales)
 
         w4_sc = keep.tile([P, 2, PASS], U8, name="w4_sc", align_bytes=64)
         w4_spread = keep.tile([P, PASS], U8, name="w4_spread", align_bytes=64)
         v_sc = keep.tile([P, 2, S], U8, name="v_sc", align_bytes=64)
         nc.vector.memset(w4_sc[:].bitcast(I32), 0)
-        nc.vector.memset(tab_sc[: P - 32, :].bitcast(I32), 0)
-        nc.gpsimd.memset(w4_spread[:].bitcast(I32), 0)
-        load_spread(nc.gpsimd, w4_spread, w4_scales[:, :, PASS:])
+        nc.vector.memset(tab_sc[: P - QUADRANT, :].bitcast(I32), 0)
+        load_spread(nc.scalar, w4_spread, w4_scales[:, :, PASS:])
         nc.vector.memset(v_sc[:].bitcast(I32), 0)
+        nc.vector.memset(w4_spread[: P - QUADRANT, :].bitcast(I32), 0)
         ident = keep.tile([P, P], F32, name="ident", align_bytes=64)
         make_identity(nc, ident[:])
 
         nc.sync.dma_start(offs_sb[:], offs)
-        load_plane(nc.sync, w4_sc, w4_scales[:, :, :PASS])
 
         table_bytes = 4 * T
         tab = [tables.tile([P, T], U32, name="tab%d" % a, align_bytes=64, offset=table_bytes * a) for a in range(2)]
 
-        def load_table(a):
-            nc.sync.dma_start(out=tab[a][:].bitcast(I32), in_=tab_words[a].rearrange("p n t -> p (n t)").bitcast(I32))
+        def load_table(a, first, last):
+            nc.sync.dma_start(
+                out=tab[a][:, first:last].bitcast(I32), in_=tab_words[a, :, first:last, :].rearrange("p n t -> p (n t)").bitcast(I32)
+            )
 
         def load_w4(tile, first, last):
             nc.sync.dma_start(out=tile[:].bitcast(I32), in_=w4_words[:, :, 2 * first : 2 * last].rearrange("a p c -> p a c").bitcast(I32))
 
         early_cols = P * EARLY_ACTS
         w4_early = keep.tile([P, 2, 2 * early_cols], U8, name="w4_early", align_bytes=64)
-        load_w4(w4_early, 0, early_cols)
-        load_table(0)
-        nc.sync.dma_start(pos1_sb[:], pos1)
-        nc.sync.dma_start(pos3_sb[:], pos3)
+        load_table(0, 0, T // 2)
+        load_plane(nc.sync, w4_sc, w4_scales[:, :, :PASS])
+        load_table(0, T // 2, T)
+        load_table(1, 0, T // 4)
         picked = keep.tile([P, S], U8, name="picked", align_bytes=64)
         nc.vector.tensor_copy(out=picked[:], in_=tab_sc[:].indirect(offs_sb[:]))
-        move_to_plane(nc.sync, v_sc, picked[P - 32 :, :], 1)
-        load_table(1)
-        nc.sync.dma_start(pos2_sb[:], pos2)
+        move_to_plane(nc.sync, v_sc, picked)
+        load_table(1, T // 4, 5 * T // 8)
+        load_w4(w4_early, 0, early_cols)
+        load_table(1, 5 * T // 8, T)
 
         region_bytes = 6 * 1024
         starts = [sum(WD_PIECES[:i]) for i in range(len(WD_PIECES))]
+        dealt = len(WD_PIECES) - 1
+        after_regions = 3 * region_bytes + 16 * WD_PIECES[dealt]
+        raw_at = {(0, 0): 0, (1, 1): 2 * region_bytes, (dealt, 0): 3 * region_bytes, (dealt, 1): after_regions}
+        after_raw = after_regions + 16 * WD_PIECES[dealt]
+        raw_columns = {(0, 0): region_bytes // 4 + S, (1, 1): region_bytes // 4}
         wd_raw = {}
 
-        def load_wd(i, a, tile):
+        def load_wd(i):
             width = WD_PIECES[i]
-            wd_raw[i, a] = tile[:, : PACK * width].rearrange("p (j c) -> p j c", j=PACK)
-            nc.sync.dma_start(
-                out=wd_raw[i, a],
-                in_=wd[a * PASS : (a + 1) * PASS, starts[i] : starts[i] + width].rearrange("(p j) c -> p j c", j=PACK),
-            )
+            for a in range(2):
+                name = "wd_raw%d%d" % (i, a)
+                if (i, a) in raw_at:
+                    tile = arena.tile([P, raw_columns.get((i, a), PACK * width)], F32, name=name, align_bytes=64, offset=raw_at[i, a])
+                else:
+                    tile = keep.tile([P, PACK * width], F32, name=name, align_bytes=64)
+                wd_raw[i, a] = tile[:, : PACK * width].rearrange("p (j c) -> p j c", j=PACK)
+                nc.sync.dma_start(
+                    out=wd_raw[i, a],
+                    in_=wd[a * PASS : (a + 1) * PASS, starts[i] : starts[i] + width].rearrange("(p j) c -> p j c", j=PACK),
+                )
 
-        load_wd(0, 0, arena.tile([P, region_bytes // 4 + S], F32, name="wd_raw00", align_bytes=64, offset=0))
-        load_wd(0, 1, keep.tile([P, PACK * WD_PIECES[0]], F32, name="wd_raw01", align_bytes=64))
+        load_wd(0)
 
         warm = keep.tile([P, 1], F32, name="warm")
         nc.vector.memset(warm[:], 0.0)
@@ -132,111 +143,90 @@ def tile_list_sourdough_order_blend_kernel(
                 v[a, h] = keep.tile([P, BANK], U32, name="v%d%d" % (a, h), align_bytes=64)
                 nc.vector.tensor_copy(out=v[a, h][:], in_=tab[a][:].indirect(offs_sb[:, 32 * h : 32 * h + 32]))
 
-        gather_table(0)
-        w4_dealt_spread = tables.tile([P, PASS], U8, name="w4_dealt_spread", align_bytes=64, offset=0)
+        w4_dealt_spread = keep.tile([P, PASS], U8, name="w4_dealt_spread", align_bytes=64)
         nc.vector.tensor_copy(
             out=w4_dealt_spread[:].rearrange("p (t m) -> p m t", t=PACK), in_=w4_spread[:].rearrange("p (m t) -> p m t", t=PACK)
         )
 
-        placed = [3 * region_bytes + 16 * WD_PIECES[3]]
-        raw_at = {(2, 1): 2 * region_bytes, (3, 0): 3 * region_bytes}
-
-        def late_tile(shape, dtype, size, name):
-            tile = arena.tile(shape, dtype, name=name, align_bytes=64, offset=placed[-1])
-            placed.append(placed[-1] + size)
-            return tile
-
-        def load_late_wd(i):
-            for a in range(2):
-                name = "wd_raw%d%d" % (i, a)
-                if (i, a) in raw_at:
-                    columns = max(PACK * WD_PIECES[i], region_bytes // 4)
-                    tile = arena.tile([P, columns], F32, name=name, align_bytes=64, offset=raw_at[i, a])
-                else:
-                    raw_at[i, a] = placed[-1]
-                    tile = late_tile([P, PACK * WD_PIECES[i]], F32, 16 * WD_PIECES[i], name)
-                load_wd(i, a, tile)
-
-        load_late_wd(1)
-        w4_late = late_tile([P, 2, 2 * (H - early_cols)], U8, 4 * (H - early_cols), "w4_late")
-        load_w4(w4_late, early_cols, H)
-        load_late_wd(2)
-        load_late_wd(3)
-        w4_dealt_sc = late_tile([P, 2, PASS], U8, 2 * PASS, "w4_dealt_sc")
+        gather_table(0)
+        w4_second = keep.tile([P, 2, 2 * PASS], U8, name="w4_second", align_bytes=64)
+        load_w4(w4_second, PASS, H)
+        nc.sync.dma_start(pos3_sb[:], pos3)
+        nc.sync.dma_start(pos2_sb[:], pos2)
+        load_wd(1)
+        nc.sync.dma_start(pos1_sb[:], pos1)
+        w4_late = keep.tile([P, 2, 2 * (PASS - early_cols)], U8, name="w4_late", align_bytes=64)
+        load_w4(w4_late, early_cols, PASS)
+        load_wd(dealt)
+        w4_dealt_sc = keep.tile([P, 2, PASS], U8, name="w4_dealt_sc", align_bytes=64)
         nc.gpsimd.memset(w4_dealt_sc[:].bitcast(I32), 0)
-        move_to_plane(nc.sync, w4_dealt_sc, w4_dealt_spread)
-        w8 = late_tile([P, 2, N], U32, 8 * N, "w8")
+        move_to_plane(nc.gpsimd, w4_dealt_sc, w4_dealt_spread)
+        w8 = keep.tile([P, 2, N], U32, name="w8", align_bytes=64)
         nc.sync.dma_start(out=w8[:].bitcast(I32), in_=w8_words.rearrange("a p n t -> p a (n t)").bitcast(I32))
-        w8_sc = late_tile([P, 2, N], U8, 2 * N, "w8_sc")
+        w8_sc = keep.tile([P, 2, N], U8, name="w8_sc", align_bytes=64)
         nc.gpsimd.memset(w8_sc[:].bitcast(I32), 0)
         load_plane(nc.sync, w8_sc, w8_scales)
-        bias = late_tile([P, N // P], F32, 64, "bias")
+        bias = keep.tile([P, N // P], F32, name="bias", align_bytes=64)
         with nc.allow_non_contiguous_dma(reason="one bias value a partition and output tile"):
             nc.sync.dma_start(out=bias[:], in_=crumb0.rearrange("(c p) -> p c", p=P))
 
+        codes_at = {1: 0, 2: 8 * PASS}
         rounded = {}
         wq = {}
         wq_sc = {}
 
-        def round_wd(i, a, copy):
-            width = WD_PIECES[i]
-            name = "wd_bf%d%d" % (i, a)
-            if (i, a) == (0, 0):
-                rounded[i, a] = late_tile([P, PACK * width], BF16, 8 * width, name)[:]
-            elif i == 0:
-                rounded[i, a] = tables.tile([P, PACK * width], BF16, name=name, align_bytes=64, offset=table_bytes)[:]
-            elif i == 3:
-                rounded[i, a] = arena.tile([P, PACK * width], BF16, name=name, align_bytes=64, offset=4 * M + region_bytes * a)[:]
-            elif (i, 0) not in rounded:
-                if i == 1:
-                    both = tables.tile([P, 2 * PACK * width], BF16, name=name, align_bytes=64, offset=table_bytes + 2048)
+        def round_wd(i, a, parts, copy):
+            if i not in rounded:
+                if i == 0:
+                    rounded[i] = keep.tile([P, 2, 2, PASS], BF16, name="wd_bf0", align_bytes=64)
                 else:
-                    both = codes_then.tile([P, 2 * PACK * width], BF16, name=name, align_bytes=64, offset=4 * PASS)
-                rounded[i] = both[:]
-                for b in range(2):
-                    rounded[i, b] = both[:, PACK * width * b : PACK * width * (b + 1)]
-            if i == 3:
-                copy(
-                    out=rounded[i, a].rearrange("p (t m j) -> p m j t", t=PACK, j=PACK),
-                    in_=wd_raw[i, a].rearrange("p j (m t) -> p m j t", t=PACK),
-                )
-            else:
-                copy(
-                    out=rounded[i, a].rearrange("p (c i j) -> p c j i", i=4, j=PACK),
-                    in_=wd_raw[i, a].rearrange("p j (c i) -> p c j i", i=4),
-                )
+                    rounded[i] = codes_then.tile([P, 2, 2, PASS], BF16, name="wd_bf1", align_bytes=64, offset=codes_at[1])
+            copy(
+                out=rounded[i][:, parts, a, :].rearrange("p s (c i j) -> p s c j i", i=4, j=PACK),
+                in_=wd_raw[i, a].rearrange("p j (s c i) -> p s c j i", i=4, c=P // 4)[:, parts, :, :, :],
+            )
 
-        def quantize_wd(i, passes):
-            width = WD_PIECES[i]
-            name = "%d%d" % (i, passes[0])
-            if (i, passes) == (0, (0,)):
-                codes = tables.tile([P, width], U32, name="wq" + name, align_bytes=64, offset=table_bytes + 1024)
-            elif (i, passes) == (0, (1,)):
-                codes = codes_then.tile([P, width], U32, name="wq" + name, align_bytes=64, offset=0)
-            elif i == 1:
-                codes = codes_then.tile([P, 2 * width], U32, name="wq" + name, align_bytes=64, offset=4 * PASS)
+        def round_dealt(a, rows, copy):
+            if (dealt, a) not in rounded:
+                rounded[dealt, a] = arena.tile([P, PACK, P, PACK], BF16, name="wd_dealt%d" % a, align_bytes=64, offset=4 * M + region_bytes * a)
+            copy(
+                out=rounded[dealt, a][:].rearrange("p t m j -> p m j t")[:, rows, :, :],
+                in_=wd_raw[dealt, a].rearrange("p j (m t) -> p m j t", t=PACK)[:, rows, :, :],
+            )
+
+        def quantize_wd(source, keys):
+            name = "%d%d" % keys[0]
+            width = P * len(keys)
+            if keys[0][1] in codes_at:
+                codes = codes_then.tile([P, width], U32, name="wq" + name, align_bytes=64, offset=codes_at[keys[0][1]])
             else:
-                codes = keep.tile([P, len(passes) * width], U32, name="wq" + name, align_bytes=64)
-            plane = keep.tile([P, len(passes) * width], U8, name="wq_sc" + name, align_bytes=64)
-            source = rounded[i] if len(passes) == 2 else rounded[i, passes[0]]
+                codes = keep.tile([P, width], U32, name="wq" + name, align_bytes=64)
+            plane = keep.tile([P, width], U8, name="wq_sc" + name, align_bytes=64)
             nc.vector.quantize_mx(out=codes[:].bitcast(FP8X4), scales=plane[:], in_=source)
-            for k, a in enumerate(passes):
-                for t in range(width // P):
-                    cols = slice(width * k + P * t, width * k + P * (t + 1))
-                    wq[a, starts[i] // P + t] = codes[:, cols]
-                    wq_sc[a, starts[i] // P + t] = plane[:, cols]
+            for k, key in enumerate(keys):
+                wq[key] = codes[:, P * k : P * (k + 1)]
+                wq_sc[key] = plane[:, P * k : P * (k + 1)]
 
-        w4_dealt = codes_then.tile([P, 2, 2 * PASS], U8, name="w4_dealt", align_bytes=64, offset=0)
+        def quantize_slice(s):
+            quantize_wd(rounded[s // 2][:, s % 2, :, :].rearrange("p a x -> p (a x)"), [(0, s), (1, s)])
+
+        def quantize_first(a):
+            quantize_wd(rounded[0][:, 0, a, :], [(a, 0)])
+
+        def quantize_dealt(a):
+            quantize_wd(rounded[dealt, a][:].rearrange("p t m j -> p (t m j)"), [(a, PACK + t) for t in range(PACK)])
+
+        w4_dealt = keep.tile([P, 2, 2 * PASS], U8, name="w4_dealt", align_bytes=64)
 
         def deal_w4_words():
             nc.vector.tensor_copy(
                 out=w4_dealt[:].bitcast(U16).rearrange("p a (t m) -> p a m t", t=PACK),
-                in_=w4_late[:, :, 2 * (PASS - early_cols) :].bitcast(U16).rearrange("p a (m t) -> p a m t", t=PACK),
+                in_=w4_second[:].bitcast(U16).rearrange("p a (m t) -> p a m t", t=PACK),
             )
 
         banks_taken = []
-        first_banks = (0, 2, 1, 4, 5, 1, 6, 7, 4, 5, 0, 3, 2, 1, 6, 7, 2, 1, 0, 3)
-        later_banks = (4, 5, 6, 7, 2, 1, 0, 3)
+        first_banks = (0, 2, 3, 1, 4, 5, 6, 7, 4, 5, 0, 3, 2, 1, 6, 7, 2, 1, 6, 7, 0, 3)
+        later_banks = (4, 5, 2, 1, 6, 7, 0, 3)
 
         def bank(index=None):
             if index is None:
@@ -264,7 +254,7 @@ def tile_list_sourdough_order_blend_kernel(
             )
 
         def in_region(s, shape, name):
-            return arena.tile(shape, F32, name=name, align_bytes=64, offset=region_bytes * (s % 4))
+            return arena.tile(shape, F32, name=name, align_bytes=64, offset=region_bytes * s if s < PACK else after_raw + 4 * S * (s - PACK))
 
         act = {}
         dough = {}
@@ -301,9 +291,11 @@ def tile_list_sourdough_order_blend_kernel(
 
         def make_share(s):
             if s == 0:
-                share[s] = arena.tile([P, M], F32, name="share0", align_bytes=64, offset=raw_at[2, 1] + 4 * S)
+                share[s] = arena.tile([P, M], F32, name="share0", align_bytes=64, offset=raw_at[1, 1] + 4 * S)
             elif s == 1:
-                share[s] = codes_then.tile([P, M], F32, name="share1", align_bytes=64, offset=4 * PASS)
+                share[s] = codes_then.tile([P, M], F32, name="share1", align_bytes=64, offset=codes_at[2])
+            elif s == 2:
+                share[s] = arena.tile([P, M], F32, name="share2", align_bytes=64, offset=raw_at[dealt, 1])
             else:
                 share[s] = ring.tile([P, M], F32, name="share", bufs=3)
             nc.scalar.activation(out=share[s][:], in_=act[s][:].indirect(pos1_sb[:]), func=ACT.Sigmoid)
@@ -412,27 +404,28 @@ def tile_list_sourdough_order_blend_kernel(
                 )
 
         whole = slice(0, M)
+        both = slice(0, 2)
         halves = [slice(0, M // 2), slice(M // 2, M)]
         last = SLICES - 1
         edges = [sum(LAST_PIECES[:i]) for i in range(len(LAST_PIECES) + 1)]
         pieces = [slice(edges[i], edges[i + 1]) for i in range(len(LAST_PIECES))]
         on_vector, on_scalar = nc.vector.tensor_copy, nc.scalar.copy
 
-        act_banks = {key: bank() for key in ((0, 0), (1, 0), (0, 1))}
+        act_banks = {key: bank() for key in ((0, 0), (1, 0), (0, 1), (1, 1))}
         for (s, h), acc in act_banks.items():
             one_pass(acc, s, True, h, 0, True)
         gather_table(1)
-        round_wd(0, 0, on_scalar)
+        round_wd(0, 0, both, on_scalar)
         for s in range(EARLY_ACTS):
             new_window(s, True)
             one_pass(act_banks[s, 0], s, True, 0, 1, False)
             empty(act[s], 0, act_banks[s, 0])
         one_pass(act_banks[0, 1], 0, True, 1, 1, False)
         empty(act[0], 1, act_banks[0, 1])
-        quantize_wd(0, (0,))
-        round_wd(0, 1, on_vector)
-        round_wd(1, 0, on_vector)
-        quantize_wd(0, (1,))
+        quantize_first(0)
+        round_wd(0, 1, slice(0, 1), on_vector)
+        round_wd(0, 1, slice(1, 2), on_vector)
+        quantize_first(1)
         dough_banks = [bank() for h in range(2)]
         for h in range(2):
             one_pass(dough_banks[h], 0, False, h, 0, True)
@@ -440,43 +433,43 @@ def tile_list_sourdough_order_blend_kernel(
         for h in range(2):
             one_pass(dough_banks[h], 0, False, h, 1, False)
         empty(dough[0], 0, dough_banks[0])
-        round_wd(1, 1, on_vector)
-        quantize_wd(1, (0, 1))
+        quantize_slice(1)
+        deal_w4_words()
         empty(dough[0], 1, dough_banks[1], on_vector)
-        acc = bank()
-        for a in range(2):
-            one_pass(acc, 1, True, 1, a, a == 0)
-        empty(act[1], 1, acc)
+        one_pass(act_banks[1, 1], 1, True, 1, 1, False)
+        empty(act[1], 1, act_banks[1, 1])
         first_stage(1, False)
         for cols in halves:
             pick_prev(0, cols)
         for cols in halves:
             pick_diff(0, cols)
-        deal_w4_words()
         for a in range(2):
-            round_wd(2, a, on_scalar)
+            round_wd(1, a, both, on_scalar)
         make_share(0)
         pick_prev(1, whole)
-        quantize_wd(2, (0, 1))
+        quantize_slice(2)
+        quantize_slice(3)
         weigh(0, whole)
         pick_diff(1, whole)
         first_stage(2, True)
         first_stage(2, False)
         make_share(1)
-        round_wd(3, 0, on_vector)
+        round_dealt(0, slice(0, P), on_vector)
         pick_prev(2, whole)
-        quantize_wd(3, (0,))
+        quantize_dealt(0)
         weigh(1, whole)
         pick_diff(2, whole)
         first_stage(3, False)
-        round_wd(3, 1, on_vector)
+        round_dealt(1, slice(0, P // 2), on_vector)
+        round_dealt(1, slice(P // 2, P), on_scalar)
         make_share(2)
         pick_prev(3, whole)
-        quantize_wd(3, (1,))
+        quantize_dealt(1)
         weigh(2, whole)
         pick_diff(3, whole)
         first_stage(3, True)
         first_stage(4, True)
+        first_stage(5, True)
         first_stage(4, False)
         make_share(3)
         for s in range(PACK, last):
@@ -484,13 +477,15 @@ def tile_list_sourdough_order_blend_kernel(
             weigh(s - 1, whole)
             pick_diff(s, whole)
             first_stage(s + 1, False)
+            if s == last - 1:
+                first_stage(s, True)
             make_share(s)
-            first_stage(s + 1, True)
-            if s - PACK < EARLY_TURNS:
-                turn(slice(P * (s - PACK), P * (s - PACK + 1)))
-        make_share(last)
+        for c in range(tiles // 2):
+            turn(slice(P * c, P * (c + 1)))
+        first_stage(last, True)
         turn_back(halves[0])
-        for c in range(EARLY_TURNS, tiles):
+        make_share(last)
+        for c in range(tiles // 2, tiles):
             turn(slice(P * c, P * (c + 1)))
         back_banks.append(banks_taken[-1])
         turn_back(halves[1])

@@ -23,7 +23,7 @@ PASS = P * PACK
 BANK = 512
 QUADRANT = 32
 SLICES = H // P
-WD_PIECES = (256, 256, 512)
+WD_PIECES = (128, 128, 256, 512)
 EARLY_ACTS = 2
 LAST_PIECES = (256, 128, 128)
 
@@ -70,14 +70,11 @@ def tile_list_sourdough_order_blend_kernel(
         tab_sc = keep.tile([P, T], U8, name="tab_sc", align_bytes=64)
         load_spread(nc.scalar, tab_sc, tab_scales)
 
-        w4_sc = keep.tile([P, 2, PASS], U8, name="w4_sc", align_bytes=64)
-        w4_spread = keep.tile([P, PASS], U8, name="w4_spread", align_bytes=64)
+        w4_sc = keep.tile([P, 2, H], U8, name="w4_sc", align_bytes=64)
         v_sc = keep.tile([P, 2, S], U8, name="v_sc", align_bytes=64)
         nc.vector.memset(w4_sc[:].bitcast(I32), 0)
         nc.vector.memset(tab_sc[: P - QUADRANT, :].bitcast(I32), 0)
-        load_spread(nc.scalar, w4_spread, w4_scales[:, :, PASS:])
         nc.vector.memset(v_sc[:].bitcast(I32), 0)
-        nc.vector.memset(w4_spread[: P - QUADRANT, :].bitcast(I32), 0)
         ident = keep.tile([P, P], F32, name="ident", align_bytes=64)
         make_identity(nc, ident[:])
 
@@ -96,14 +93,12 @@ def tile_list_sourdough_order_blend_kernel(
 
         early_cols = P * EARLY_ACTS
         w4_early = keep.tile([P, 2, 2 * early_cols], U8, name="w4_early", align_bytes=64)
-        load_table(0, 0, T // 2)
-        load_plane(nc.sync, w4_sc, w4_scales[:, :, :PASS])
-        load_table(0, T // 2, T)
-        load_table(1, 0, T // 4)
+        load_table(0, 0, T)
+        load_plane(nc.sync, w4_sc, w4_scales)
+        load_table(1, 0, 5 * T // 8)
         picked = keep.tile([P, S], U8, name="picked", align_bytes=64)
         nc.vector.tensor_copy(out=picked[:], in_=tab_sc[:].indirect(offs_sb[:]))
         move_to_plane(nc.sync, v_sc, picked)
-        load_table(1, T // 4, 5 * T // 8)
         load_w4(w4_early, 0, early_cols)
         load_table(1, 5 * T // 8, T)
 
@@ -111,9 +106,9 @@ def tile_list_sourdough_order_blend_kernel(
         starts = [sum(WD_PIECES[:i]) for i in range(len(WD_PIECES))]
         dealt = len(WD_PIECES) - 1
         after_regions = 3 * region_bytes + 16 * WD_PIECES[dealt]
-        raw_at = {(0, 0): 0, (1, 1): 2 * region_bytes, (dealt, 0): 3 * region_bytes, (dealt, 1): after_regions}
+        raw_at = {(0, 0): 0, (2, 1): 2 * region_bytes, (dealt, 0): 52 * 1024, (dealt, 1): after_regions}
         after_raw = after_regions + 16 * WD_PIECES[dealt]
-        raw_columns = {(0, 0): region_bytes // 4 + S, (1, 1): region_bytes // 4}
+        raw_columns = {(0, 0): region_bytes // 4 + S, (2, 1): region_bytes // 4}
         wd_raw = {}
 
         def load_wd(i):
@@ -143,24 +138,22 @@ def tile_list_sourdough_order_blend_kernel(
                 v[a, h] = keep.tile([P, BANK], U32, name="v%d%d" % (a, h), align_bytes=64)
                 nc.vector.tensor_copy(out=v[a, h][:], in_=tab[a][:].indirect(offs_sb[:, 32 * h : 32 * h + 32]))
 
-        w4_dealt_spread = keep.tile([P, PASS], U8, name="w4_dealt_spread", align_bytes=64)
+        w4_dealt_sc = keep.tile([P, 2, PASS], U8, name="w4_dealt_sc", align_bytes=64)
         nc.vector.tensor_copy(
-            out=w4_dealt_spread[:].rearrange("p (t m) -> p m t", t=PACK), in_=w4_spread[:].rearrange("p (m t) -> p m t", t=PACK)
+            out=w4_dealt_sc[:].rearrange("p a (t m) -> p a m t", t=PACK), in_=w4_sc[:, :, PASS:].rearrange("p a (m t) -> p a m t", t=PACK)
         )
 
         gather_table(0)
+        load_wd(1)
         w4_second = keep.tile([P, 2, 2 * PASS], U8, name="w4_second", align_bytes=64)
         load_w4(w4_second, PASS, H)
         nc.sync.dma_start(pos3_sb[:], pos3)
         nc.sync.dma_start(pos2_sb[:], pos2)
-        load_wd(1)
+        load_wd(2)
         nc.sync.dma_start(pos1_sb[:], pos1)
         w4_late = keep.tile([P, 2, 2 * (PASS - early_cols)], U8, name="w4_late", align_bytes=64)
         load_w4(w4_late, early_cols, PASS)
         load_wd(dealt)
-        w4_dealt_sc = keep.tile([P, 2, PASS], U8, name="w4_dealt_sc", align_bytes=64)
-        nc.gpsimd.memset(w4_dealt_sc[:].bitcast(I32), 0)
-        move_to_plane(nc.gpsimd, w4_dealt_sc, w4_dealt_spread)
         w8 = keep.tile([P, 2, N], U32, name="w8", align_bytes=64)
         nc.sync.dma_start(out=w8[:].bitcast(I32), in_=w8_words.rearrange("a p n t -> p a (n t)").bitcast(I32))
         w8_sc = keep.tile([P, 2, N], U8, name="w8_sc", align_bytes=64)
@@ -170,34 +163,43 @@ def tile_list_sourdough_order_blend_kernel(
         with nc.allow_non_contiguous_dma(reason="one bias value a partition and output tile"):
             nc.sync.dma_start(out=bias[:], in_=crumb0.rearrange("(c p) -> p c", p=P))
 
-        codes_at = {1: 0, 2: 8 * PASS}
+        codes_at = {1: 0, 2: 8 * PASS, 3: 12 * PASS}
         rounded = {}
         wq = {}
         wq_sc = {}
 
-        def round_wd(i, a, parts, copy):
-            if i not in rounded:
-                if i == 0:
-                    rounded[i] = keep.tile([P, 2, 2, PASS], BF16, name="wd_bf0", align_bytes=64)
-                else:
-                    rounded[i] = codes_then.tile([P, 2, 2, PASS], BF16, name="wd_bf1", align_bytes=64, offset=codes_at[1])
+        rounded[0, 0] = keep.tile([P, 1, PASS], BF16, name="wd_bf00", align_bytes=64)[:]
+        rounded[0, 1] = tables.tile([P, 1, PASS], BF16, name="wd_bf01", align_bytes=64, offset=table_bytes)[:]
+        rounded[1] = tables.tile([P, 1, 2, PASS], BF16, name="wd_bf1", align_bytes=64, offset=table_bytes + 4 * PASS)
+        rounded[2] = codes_then.tile([P, 2, 2, PASS], BF16, name="wd_bf2", align_bytes=64, offset=codes_at[1])
+        for i in (1, 2):
+            for a in range(2):
+                rounded[i, a] = rounded[i][:, :, a, :]
+
+        def round_wd(i, a, copy, parts=slice(0, 2)):
             copy(
-                out=rounded[i][:, parts, a, :].rearrange("p s (c i j) -> p s c j i", i=4, j=PACK),
+                out=rounded[i, a].rearrange("p s (c i j) -> p s c j i", i=4, j=PACK)[:, parts, :, :, :],
                 in_=wd_raw[i, a].rearrange("p j (s c i) -> p s c j i", i=4, c=P // 4)[:, parts, :, :, :],
             )
 
-        def round_dealt(a, rows, copy):
-            if (dealt, a) not in rounded:
-                rounded[dealt, a] = arena.tile([P, PACK, P, PACK], BF16, name="wd_dealt%d" % a, align_bytes=64, offset=4 * M + region_bytes * a)
+        dealt_at = {(0, 0): 4 * M, (0, 2): 8 * M, (1, 0): region_bytes + 4 * M, (1, 2): 2 * region_bytes + 4 * M}
+
+        def round_dealt(a, ts, rows, copy):
+            if (dealt, a, ts.start) not in rounded:
+                rounded[dealt, a, ts.start] = arena.tile(
+                    [P, ts.stop - ts.start, P, PACK], BF16, name="wd_dealt%d%d" % (a, ts.start), align_bytes=64, offset=dealt_at[a, ts.start]
+                )
             copy(
-                out=rounded[dealt, a][:].rearrange("p t m j -> p m j t")[:, rows, :, :],
-                in_=wd_raw[dealt, a].rearrange("p j (m t) -> p m j t", t=PACK)[:, rows, :, :],
+                out=rounded[dealt, a, ts.start][:].rearrange("p t m j -> p m j t")[:, rows, :, :],
+                in_=wd_raw[dealt, a].rearrange("p j (m t) -> p m j t", t=PACK)[:, rows, :, ts],
             )
 
         def quantize_wd(source, keys):
             name = "%d%d" % keys[0]
             width = P * len(keys)
-            if keys[0][1] in codes_at:
+            if keys == [(0, 0)]:
+                codes = tables.tile([P, width], U32, name="wq" + name, align_bytes=64, offset=table_bytes + 2 * PASS)
+            elif keys[0][1] in codes_at:
                 codes = codes_then.tile([P, width], U32, name="wq" + name, align_bytes=64, offset=codes_at[keys[0][1]])
             else:
                 codes = keep.tile([P, width], U32, name="wq" + name, align_bytes=64)
@@ -208,13 +210,14 @@ def tile_list_sourdough_order_blend_kernel(
                 wq_sc[key] = plane[:, P * k : P * (k + 1)]
 
         def quantize_slice(s):
-            quantize_wd(rounded[s // 2][:, s % 2, :, :].rearrange("p a x -> p (a x)"), [(0, s), (1, s)])
+            quantize_wd(rounded[min(s, 2)][:, max(s - 2, 0), :, :].rearrange("p a x -> p (a x)"), [(0, s), (1, s)])
 
         def quantize_first(a):
-            quantize_wd(rounded[0][:, 0, a, :], [(a, 0)])
+            quantize_wd(rounded[0, a][:, 0, :], [(a, 0)])
 
-        def quantize_dealt(a):
-            quantize_wd(rounded[dealt, a][:].rearrange("p t m j -> p (t m j)"), [(a, PACK + t) for t in range(PACK)])
+        def quantize_dealt(a, ts):
+            source = rounded[dealt, a, ts.start][:].rearrange("p t m j -> p (t m j)")
+            quantize_wd(source, [(a, PACK + t) for t in range(ts.start, ts.stop)])
 
         w4_dealt = keep.tile([P, 2, 2 * PASS], U8, name="w4_dealt", align_bytes=64)
 
@@ -225,13 +228,13 @@ def tile_list_sourdough_order_blend_kernel(
             )
 
         banks_taken = []
-        first_banks = (0, 2, 3, 1, 4, 5, 6, 7, 4, 5, 0, 3, 2, 1, 6, 7, 2, 1, 6, 7, 0, 3)
-        later_banks = (4, 5, 2, 1, 6, 7, 0, 3)
+        first_banks = (0, 2, 3, 1, 4, 5, 6, 7, 4, 5, 6, 7, 0, 3, 2, 1, 4, 5, 6, 7, 0, 3)
+        later_banks = (2, 1, 4, 5, 6, 7, 0, 3, 0, 3, 2, 1, 6, 2, 1, 7, 4, 5, 0, 3, 6, 2)
 
         def bank(index=None):
             if index is None:
                 taken = len(banks_taken)
-                index = first_banks[taken] if taken < len(first_banks) else later_banks[(taken - len(first_banks)) % 8]
+                index = first_banks[taken] if taken < len(first_banks) else later_banks[taken - len(first_banks)]
                 banks_taken.append(index)
             return psum.tile([P, BANK], F32, name="acc%d" % index)
 
@@ -291,11 +294,11 @@ def tile_list_sourdough_order_blend_kernel(
 
         def make_share(s):
             if s == 0:
-                share[s] = arena.tile([P, M], F32, name="share0", align_bytes=64, offset=raw_at[1, 1] + 4 * S)
+                share[s] = arena.tile([P, M], F32, name="share0", align_bytes=64, offset=raw_at[2, 1] + 4 * S)
             elif s == 1:
                 share[s] = codes_then.tile([P, M], F32, name="share1", align_bytes=64, offset=codes_at[2])
             elif s == 2:
-                share[s] = arena.tile([P, M], F32, name="share2", align_bytes=64, offset=raw_at[dealt, 1])
+                share[s] = codes_then.tile([P, M], F32, name="share2", align_bytes=64, offset=codes_at[3])
             else:
                 share[s] = ring.tile([P, M], F32, name="share", bufs=3)
             nc.scalar.activation(out=share[s][:], in_=act[s][:].indirect(pos1_sb[:]), func=ACT.Sigmoid)
@@ -317,6 +320,8 @@ def tile_list_sourdough_order_blend_kernel(
             if s not in diff:
                 if s == 0:
                     diff[s] = keep.tile([P, M], F32, name="diff0", align_bytes=64)
+                elif s == 3:
+                    diff[s] = arena.tile([P, M], F32, name="diff3", align_bytes=64, offset=dealt_at[1, 0])
                 else:
                     diff[s] = in_region(s - 1, [P, M], "diff%d" % s)
             nc.vector.tensor_tensor(
@@ -335,12 +340,9 @@ def tile_list_sourdough_order_blend_kernel(
                     )
             nc.scalar.copy(out=turned[:, :, cols.start // P, :, :], in_=acc[:].rearrange("m (q u e) -> m u q e", u=2, e=2))
 
-        back_banks = []
-
         def turn_back(cols):
             first, last = cols.start // P, cols.stop // P
             acc = bank()
-            back_banks.append(banks_taken[-1])
             for c in range(first, last):
                 for u in range(2):
                     words = turned[:, u, c, :, :].rearrange("m p e -> m (p e)").bitcast(F32)
@@ -374,7 +376,7 @@ def tile_list_sourdough_order_blend_kernel(
             for c in range(N // P):
                 group, i = divmod(c, per_bank)
                 if (cols.start, group) not in sums:
-                    sums[cols.start, group] = bank(back_banks[1 + group] if cols.start == 0 else None)
+                    sums[cols.start, group] = bank()
                 nc.tensor.matmul_mx(
                     out=sums[cols.start, group][:, width * i : width * (i + 1)], lhsT=w8[:, b, P * c : P * (c + 1)].bitcast(FP8X4),
                     lhsT_scale=w8_sc[:, b, P * c : P * (c + 1)],
@@ -404,7 +406,6 @@ def tile_list_sourdough_order_blend_kernel(
                 )
 
         whole = slice(0, M)
-        both = slice(0, 2)
         halves = [slice(0, M // 2), slice(M // 2, M)]
         last = SLICES - 1
         edges = [sum(LAST_PIECES[:i]) for i in range(len(LAST_PIECES) + 1)]
@@ -415,7 +416,7 @@ def tile_list_sourdough_order_blend_kernel(
         for (s, h), acc in act_banks.items():
             one_pass(acc, s, True, h, 0, True)
         gather_table(1)
-        round_wd(0, 0, both, on_scalar)
+        round_wd(0, 0, on_scalar, slice(0, 1))
         for s in range(EARLY_ACTS):
             new_window(s, True)
             one_pass(act_banks[s, 0], s, True, 0, 1, False)
@@ -423,8 +424,8 @@ def tile_list_sourdough_order_blend_kernel(
         one_pass(act_banks[0, 1], 0, True, 1, 1, False)
         empty(act[0], 1, act_banks[0, 1])
         quantize_first(0)
-        round_wd(0, 1, slice(0, 1), on_vector)
-        round_wd(0, 1, slice(1, 2), on_vector)
+        round_wd(0, 1, on_vector, slice(0, 1))
+        round_wd(1, 0, on_vector, slice(0, 1))
         quantize_first(1)
         dough_banks = [bank() for h in range(2)]
         for h in range(2):
@@ -433,6 +434,7 @@ def tile_list_sourdough_order_blend_kernel(
         for h in range(2):
             one_pass(dough_banks[h], 0, False, h, 1, False)
         empty(dough[0], 0, dough_banks[0])
+        round_wd(1, 1, on_vector, slice(0, 1))
         quantize_slice(1)
         deal_w4_words()
         empty(dough[0], 1, dough_banks[1], on_vector)
@@ -443,8 +445,9 @@ def tile_list_sourdough_order_blend_kernel(
             pick_prev(0, cols)
         for cols in halves:
             pick_diff(0, cols)
-        for a in range(2):
-            round_wd(1, a, both, on_scalar)
+        round_wd(2, 0, on_scalar, slice(0, 1))
+        round_wd(2, 0, on_vector, slice(1, 2))
+        round_wd(2, 1, on_scalar)
         make_share(0)
         pick_prev(1, whole)
         quantize_slice(2)
@@ -452,29 +455,36 @@ def tile_list_sourdough_order_blend_kernel(
         weigh(0, whole)
         pick_diff(1, whole)
         first_stage(2, True)
+        first_stage(3, True)
         first_stage(2, False)
         make_share(1)
-        round_dealt(0, slice(0, P), on_vector)
+        round_dealt(0, slice(0, 2), slice(0, P), on_vector)
+        round_dealt(0, slice(2, PACK), slice(0, 3 * P // 4), on_vector)
         pick_prev(2, whole)
-        quantize_dealt(0)
+        quantize_dealt(0, slice(0, 2))
         weigh(1, whole)
         pick_diff(2, whole)
         first_stage(3, False)
-        round_dealt(1, slice(0, P // 2), on_vector)
-        round_dealt(1, slice(P // 2, P), on_scalar)
+        round_dealt(1, slice(0, 2), slice(0, P), on_vector)
         make_share(2)
         pick_prev(3, whole)
-        quantize_dealt(1)
+        quantize_dealt(1, slice(0, 2))
         weigh(2, whole)
         pick_diff(3, whole)
-        first_stage(3, True)
         first_stage(4, True)
+        round_dealt(0, slice(2, PACK), slice(3 * P // 4, P), on_scalar)
+        round_dealt(1, slice(2, PACK), slice(0, P), on_scalar)
         first_stage(5, True)
         first_stage(4, False)
         make_share(3)
         for s in range(PACK, last):
             pick_prev(s, whole)
-            weigh(s - 1, whole)
+            if s == PACK:
+                quantize_dealt(0, slice(2, PACK))
+                weigh(s - 1, whole)
+                quantize_dealt(1, slice(2, PACK))
+            else:
+                weigh(s - 1, whole)
             pick_diff(s, whole)
             first_stage(s + 1, False)
             if s == last - 1:
@@ -487,7 +497,6 @@ def tile_list_sourdough_order_blend_kernel(
         make_share(last)
         for c in range(tiles // 2, tiles):
             turn(slice(P * c, P * (c + 1)))
-        back_banks.append(banks_taken[-1])
         turn_back(halves[1])
         pick_prev(last, whole)
         weigh(last - 1, whole)

@@ -229,7 +229,7 @@ def tile_list_sourdough_order_blend_kernel(
 
         banks_taken = []
         first_banks = (0, 2, 3, 1, 4, 5, 6, 7, 4, 5, 6, 7, 0, 3, 2, 1, 4, 5, 6, 7, 0, 3)
-        later_banks = (2, 1, 4, 5, 6, 7, 0, 3, 0, 3, 2, 1, 6, 2, 1, 7, 4, 5, 0, 3, 6, 2)
+        later_banks = (2, 1, 4, 5, 6, 7, 0, 3, 2, 1, 1, 2, 0, 3, 6, 7, 4, 5, 1, 2, 0, 3, 6, 7)
 
         def bank(index=None):
             if index is None:
@@ -354,7 +354,7 @@ def tile_list_sourdough_order_blend_kernel(
             )
 
         def blend(cols):
-            at = 8 * cols.start if cols.start > M // 2 else 0
+            at = 8 * cols.start if cols.start > M // 2 else 8 * M + 8 * cols.start
             z_bf[1, cols.start] = late_z.tile([P, cols.stop - cols.start, PACK], BF16, name="z_piece%d" % cols.start, align_bytes=64, offset=at)
             nc.vector.tensor_tensor(
                 out=z_bf[1, cols.start][:].rearrange("p (c i) t -> p c t i", i=4),
@@ -369,10 +369,10 @@ def tile_list_sourdough_order_blend_kernel(
             )
 
         sums = {}
-        per_bank = 2
 
         def last_pass(cols, b, opens):
             width = cols.stop - cols.start
+            per_bank = 1 if cols.start == 0 else 2
             for c in range(N // P):
                 group, i = divmod(c, per_bank)
                 if (cols.start, group) not in sums:
@@ -386,6 +386,7 @@ def tile_list_sourdough_order_blend_kernel(
 
         def finish(cols, on_vector):
             width = cols.stop - cols.start
+            per_bank = 1 if cols.start == 0 else 2
             for group in range(N // P // per_bank):
                 result = keep.tile([P, per_bank, width], F32, name="result%d%d" % (cols.start, group), align_bytes=64)
                 acc = sums[cols.start, group]
@@ -401,9 +402,12 @@ def tile_list_sourdough_order_blend_kernel(
                         nc.scalar.activation(
                             out=result[:, i, :], in_=acc[:, width * i : width * (i + 1)], func=ACT.Identity, bias=bias[:, c : c + 1]
                         )
-                (nc.sync if group in on_vector or cols.start == 0 else nc.scalar).dma_start(
-                    out=out[P * tiles_of.start : P * tiles_of.stop, cols].rearrange("(c p) m -> p c m", p=P), in_=result[:]
-                )
+                        if cols.start == 0:
+                            nc.sync.dma_start(out=out[P * c : P * (c + 1), cols], in_=result[:, i, :])
+                if cols.start > 0:
+                    (nc.sync if group in on_vector else nc.scalar).dma_start(
+                        out=out[P * tiles_of.start : P * tiles_of.stop, cols].rearrange("(c p) m -> p c m", p=P), in_=result[:]
+                    )
 
         whole = slice(0, M)
         halves = [slice(0, M // 2), slice(M // 2, M)]
@@ -490,28 +494,26 @@ def tile_list_sourdough_order_blend_kernel(
             if s == last - 1:
                 first_stage(s, True)
             make_share(s)
-        for c in range(tiles // 2):
-            turn(slice(P * c, P * (c + 1)))
         first_stage(last, True)
-        turn_back(halves[0])
         make_share(last)
-        for c in range(tiles // 2, tiles):
+        for c in range(tiles):
             turn(slice(P * c, P * (c + 1)))
-        turn_back(halves[1])
+        for cols in halves:
+            turn_back(cols)
         pick_prev(last, whole)
         weigh(last - 1, whole)
         pick_diff(last, pieces[0])
         pick_diff(last, pieces[1])
         weigh(last, pieces[0])
         pick_diff(last, pieces[2])
-        quantize_z(0, halves[0])
-        last_pass(pieces[0], 0, True)
         blend(pieces[0])
         weigh(last, pieces[1])
-        quantize_z(1, pieces[0])
-        last_pass(pieces[0], 1, False)
         weigh(last, pieces[2])
+        quantize_z(1, pieces[0])
+        last_pass(pieces[0], 1, True)
         blend(pieces[1])
+        quantize_z(0, halves[0])
+        last_pass(pieces[0], 0, False)
         quantize_z(0, halves[1])
         last_pass(pieces[1], 0, True)
         last_pass(pieces[2], 0, True)

@@ -328,8 +328,8 @@ def tile_list_sourdough_order_blend_kernel(
                 out=diff[s][:, cols], in0=dough[s][:].indirect(pos2_sb[:, entries(cols)]), in1=prev[s][:, cols], op=ALU.subtract
             )
 
-        def weigh(s, cols):
-            nc.vector.tensor_tensor(out=prod[s][:, cols], in0=diff[s][:, cols], in1=share[s][:, cols], op=ALU.mult)
+        def weigh(s, cols, engine=nc.vector):
+            engine.tensor_tensor(out=prod[s][:, cols], in0=diff[s][:, cols], in1=share[s][:, cols], op=ALU.mult)
 
         def turn(cols):
             acc = bank()
@@ -473,7 +473,7 @@ def tile_list_sourdough_order_blend_kernel(
         make_share(2)
         pick_prev(3, whole)
         quantize_dealt(1, slice(0, 2))
-        weigh(2, whole)
+        weigh(2, whole, nc.gpsimd)
         pick_diff(3, whole)
         first_stage(4, True)
         round_dealt(0, slice(2, PACK), slice(3 * P // 4, P), on_scalar)
@@ -488,7 +488,7 @@ def tile_list_sourdough_order_blend_kernel(
                 weigh(s - 1, whole)
                 quantize_dealt(1, slice(2, PACK))
             else:
-                weigh(s - 1, whole)
+                weigh(s - 1, whole, nc.gpsimd)
             pick_diff(s, whole)
             first_stage(s + 1, False)
             if s == last - 1:
@@ -501,7 +501,7 @@ def tile_list_sourdough_order_blend_kernel(
         for cols in halves:
             turn_back(cols)
         pick_prev(last, whole)
-        weigh(last - 1, whole)
+        weigh(last - 1, whole, nc.gpsimd)
         pick_diff(last, pieces[0])
         pick_diff(last, pieces[1])
         weigh(last, pieces[0])

@@ -463,7 +463,7 @@ def tile_list_sourdough_order_blend_kernel(
         first_stage(2, False)
         make_share(1)
         round_dealt(0, slice(0, 2), slice(0, P), on_vector)
-        round_dealt(0, slice(2, PACK), slice(0, 3 * P // 4), on_vector)
+        round_dealt(0, slice(2, PACK), slice(0, P), on_vector)
         pick_prev(2, whole)
         quantize_dealt(0, slice(0, 2))
         weigh(1, whole)
@@ -473,19 +473,18 @@ def tile_list_sourdough_order_blend_kernel(
         make_share(2)
         pick_prev(3, whole)
         quantize_dealt(1, slice(0, 2))
+        round_dealt(1, slice(2, PACK), slice(0, P), on_vector)
         weigh(2, whole, nc.gpsimd)
         pick_diff(3, whole)
         first_stage(4, True)
-        round_dealt(0, slice(2, PACK), slice(3 * P // 4, P), on_scalar)
-        round_dealt(1, slice(2, PACK), slice(0, P), on_scalar)
+        make_share(3)
         first_stage(5, True)
         first_stage(4, False)
-        make_share(3)
         for s in range(PACK, last):
             pick_prev(s, whole)
             if s == PACK:
                 quantize_dealt(0, slice(2, PACK))
-                weigh(s - 1, whole)
+                weigh(s - 1, whole, nc.gpsimd)
                 quantize_dealt(1, slice(2, PACK))
             else:
                 weigh(s - 1, whole, nc.gpsimd)

@@ -229,7 +229,7 @@ def tile_list_sourdough_order_blend_kernel(
 
         banks_taken = []
         first_banks = (0, 2, 3, 1, 4, 5, 6, 7, 4, 5, 6, 7, 0, 3, 2, 1, 4, 5, 6, 7, 0, 3)
-        later_banks = (2, 1, 4, 5, 6, 7, 0, 3, 2, 1, 1, 2, 0, 3, 6, 7, 4, 5, 1, 2, 0, 3, 6, 7)
+        later_banks = (2, 1, 4, 5, 6, 7, 0, 3, 0, 3, 2, 1, 6, 2, 1, 7, 1, 5, 0, 3, 6, 4)
 
         def bank(index=None):
             if index is None:
@@ -354,7 +354,7 @@ def tile_list_sourdough_order_blend_kernel(
             )
 
         def blend(cols):
-            at = 8 * cols.start if cols.start > M // 2 else 8 * M + 8 * cols.start
+            at = 8 * cols.start if cols.start > M // 2 else 0
             z_bf[1, cols.start] = late_z.tile([P, cols.stop - cols.start, PACK], BF16, name="z_piece%d" % cols.start, align_bytes=64, offset=at)
             nc.vector.tensor_tensor(
                 out=z_bf[1, cols.start][:].rearrange("p (c i) t -> p c t i", i=4),
@@ -369,10 +369,10 @@ def tile_list_sourdough_order_blend_kernel(
             )
 
         sums = {}
+        per_bank = 2
 
         def last_pass(cols, b, opens):
             width = cols.stop - cols.start
-            per_bank = 1 if cols.start == 0 else 2
             for c in range(N // P):
                 group, i = divmod(c, per_bank)
                 if (cols.start, group) not in sums:
@@ -386,7 +386,6 @@ def tile_list_sourdough_order_blend_kernel(
 
         def finish(cols, on_vector):
             width = cols.stop - cols.start
-            per_bank = 1 if cols.start == 0 else 2
             for group in range(N // P // per_bank):
                 result = keep.tile([P, per_bank, width], F32, name="result%d%d" % (cols.start, group), align_bytes=64)
                 acc = sums[cols.start, group]
@@ -402,12 +401,9 @@ def tile_list_sourdough_order_blend_kernel(
                         nc.scalar.activation(
                             out=result[:, i, :], in_=acc[:, width * i : width * (i + 1)], func=ACT.Identity, bias=bias[:, c : c + 1]
                         )
-                        if cols.start == 0:
-                            nc.sync.dma_start(out=out[P * c : P * (c + 1), cols], in_=result[:, i, :])
-                if cols.start > 0:
-                    (nc.sync if group in on_vector else nc.scalar).dma_start(
-                        out=out[P * tiles_of.start : P * tiles_of.stop, cols].rearrange("(c p) m -> p c m", p=P), in_=result[:]
-                    )
+                (nc.sync if group in on_vector or cols.start == 0 else nc.scalar).dma_start(
+                    out=out[P * tiles_of.start : P * tiles_of.stop, cols].rearrange("(c p) m -> p c m", p=P), in_=result[:]
+                )
 
         whole = slice(0, M)
         halves = [slice(0, M // 2), slice(M // 2, M)]
@@ -493,26 +489,28 @@ def tile_list_sourdough_order_blend_kernel(
             if s == last - 1:
                 first_stage(s, True)
             make_share(s)
-        first_stage(last, True)
-        make_share(last)
-        for c in range(tiles):
+        for c in range(tiles // 2):
             turn(slice(P * c, P * (c + 1)))
-        for cols in halves:
-            turn_back(cols)
+        first_stage(last, True)
+        turn_back(halves[0])
+        make_share(last)
+        for c in range(tiles // 2, tiles):
+            turn(slice(P * c, P * (c + 1)))
+        turn_back(halves[1])
         pick_prev(last, whole)
-        weigh(last - 1, whole, nc.gpsimd)
+        weigh(last - 1, whole)
         pick_diff(last, pieces[0])
         pick_diff(last, pieces[1])
         weigh(last, pieces[0])
         pick_diff(last, pieces[2])
+        quantize_z(0, halves[0])
+        last_pass(pieces[0], 0, True)
         blend(pieces[0])
         weigh(last, pieces[1])
-        weigh(last, pieces[2])
         quantize_z(1, pieces[0])
-        last_pass(pieces[0], 1, True)
+        last_pass(pieces[0], 1, False)
+        weigh(last, pieces[2])
         blend(pieces[1])
-        quantize_z(0, halves[0])
-        last_pass(pieces[0], 0, False)
         quantize_z(0, halves[1])
         last_pass(pieces[1], 0, True)
         last_pass(pieces[2], 0, True)

from contextlib import ExitStack

import concourse.mybir as mybir
from concourse.masks import make_identity

K, H, N, T, S, M = 1024, 1024, 512, 4096, 1024, 512
FLOPS = 2 * (2 * K * H * S + H * N * M)

F32 = mybir.dt.float32
BF16 = mybir.dt.bfloat16
I32 = mybir.dt.int32
U32 = mybir.dt.uint32
U16 = mybir.dt.uint16
U8 = mybir.dt.uint8
FP8X4 = mybir.dt.float8_e4m3fn_x4
FP4X4 = mybir.dt.float4_e2m1fn_x4
ALU = mybir.AluOpType
ACT = mybir.ActivationFunctionType

P = 128
PACK = 4
PASS = P * PACK
BANK = 512
QUADRANT = 32
SLICES = H // P
WD_PIECES = (128, 128, 256, 512)
EARLY_ACTS = 2
LAST_PIECES = (256, 128, 128)


def load_plane(queue, plane, scales):
    for r in range(4):
        queue.dma_start(
            out=plane[r:P:QUADRANT, :, :].bitcast(I32),
            in_=scales[:, r:16:4, :].rearrange("a q c -> q a c").bitcast(I32),
        )


def load_spread(queue, spread, scales):
    queue.dma_start(out=spread[P - QUADRANT :, :].bitcast(I32), in_=scales.rearrange("a q c -> q a c").bitcast(I32))


def move_to_plane(queue, plane, spread):
    for q in range(4):
        queue.dma_start(
            out=plane[QUADRANT * q : QUADRANT * q + 4, :, :].bitcast(I32),
            in_=spread[P - QUADRANT + 8 * q : P - QUADRANT + 8 * (q + 1), :].bitcast(I32),
        )


def tile_list_sourdough_order_blend_kernel(
    tc, tab_words, tab_scales, offs, pos1, pos2, pos3, w4_words, w4_scales, wd, w8_words, w8_scales, crumb0, out
):
    nc = tc.nc
    with ExitStack() as ctx:
        lists = ctx.enter_context(tc.tile_pool(name="lists", bufs=1))
        keep = ctx.enter_context(tc.tile_pool(name="keep", bufs=1))
        arena = ctx.enter_context(tc.tile_pool(name="arena", bufs=1))
        tables = ctx.enter_context(tc.tile_pool(name="tables", bufs=1))
        codes_then = ctx.enter_context(tc.tile_pool(name="codes_then", bufs=1))
        late_z = ctx.enter_context(tc.tile_pool(name="late_z", bufs=1))
        ring = ctx.enter_context(tc.tile_pool(name="ring", bufs=3))
        psum = ctx.enter_context(tc.psum_pool(name="psum", bufs=1))

        offs_sb = lists.tile([P, S // 16], U16, name="offs_sb")
        pos1_sb = lists.tile([P, M // 16], U16, name="pos1_sb")
        pos2_sb = lists.tile([P, M // 16], U16, name="pos2_sb")
        pos3_sb = lists.tile([P, M // 16], U16, name="pos3_sb")

        tab_sc = keep.tile([P, T], U8, name="tab_sc", align_bytes=64)
        load_spread(nc.scalar, tab_sc, tab_scales)

        w4_sc = keep.tile([P, 2, H], U8, name="w4_sc", align_bytes=64)
        v_sc = keep.tile([P, 2, S], U8, name="v_sc", align_bytes=64)
        nc.vector.memset(w4_sc[:].bitcast(I32), 0)
        nc.vector.memset(tab_sc[: P - QUADRANT, :].bitcast(I32), 0)
        nc.vector.memset(v_sc[:].bitcast(I32), 0)
        ident = keep.tile([P, P], F32, name="ident", align_bytes=64)
        make_identity(nc, ident[:])

        nc.sync.dma_start(offs_sb[:], offs)

        table_bytes = 4 * T
        tab = [tables.tile([P, T], U32, name="tab%d" % a, align_bytes=64, offset=table_bytes * a) for a in range(2)]

        def load_table(a, first, last):
            nc.sync.dma_start(
                out=tab[a][:, first:last].bitcast(I32), in_=tab_words[a, :, first:last, :].rearrange("p n t -> p (n t)").bitcast(I32)
            )

        def load_w4(tile, first, last):
            nc.sync.dma_start(out=tile[:].bitcast(I32), in_=w4_words[:, :, 2 * first : 2 * last].rearrange("a p c -> p a c").bitcast(I32))

        early_cols = P * EARLY_ACTS
        w4_early = keep.tile([P, 2, 2 * early_cols], U8, name="w4_early", align_bytes=64)
        load_table(0, 0, T)
        load_plane(nc.sync, w4_sc, w4_scales)
        load_table(1, 0, 5 * T // 8)
        picked = keep.tile([P, S], U8, name="picked", align_bytes=64)
        nc.vector.tensor_copy(out=picked[:], in_=tab_sc[:].indirect(offs_sb[:]))
        move_to_plane(nc.sync, v_sc, picked)
        load_w4(w4_early, 0, early_cols)
        load_table(1, 5 * T // 8, T)

        region_bytes = 6 * 1024
        starts = [sum(WD_PIECES[:i]) for i in range(len(WD_PIECES))]
        dealt = len(WD_PIECES) - 1
        after_regions = 3 * region_bytes + 16 * WD_PIECES[dealt]
        raw_at = {(0, 0): 0, (2, 1): 2 * region_bytes, (dealt, 0): 52 * 1024, (dealt, 1): after_regions}
        after_raw = after_regions + 16 * WD_PIECES[dealt]
        raw_columns = {(0, 0): region_bytes // 4 + S, (2, 1): region_bytes // 4}
        wd_raw = {}

        def load_wd(i):
            width = WD_PIECES[i]
            for a in range(2):
                name = "wd_raw%d%d" % (i, a)
                if (i, a) in raw_at:
                    tile = arena.tile([P, raw_columns.get((i, a), PACK * width)], F32, name=name, align_bytes=64, offset=raw_at[i, a])
                else:
                    tile = keep.tile([P, PACK * width], F32, name=name, align_bytes=64)
                wd_raw[i, a] = tile[:, : PACK * width].rearrange("p (j c) -> p j c", j=PACK)
                nc.sync.dma_start(
                    out=wd_raw[i, a],
                    in_=wd[a * PASS : (a + 1) * PASS, starts[i] : starts[i] + width].rearrange("(p j) c -> p j c", j=PACK),
                )

        load_wd(0)

        warm = keep.tile([P, 1], F32, name="warm")
        nc.vector.memset(warm[:], 0.0)
        nc.scalar.activation(out=warm[:], in_=warm[:], func=ACT.Sigmoid)

        v = {}

        def gather_table(a):
            for h in range(2):
                v[a, h] = keep.tile([P, BANK], U32, name="v%d%d" % (a, h), align_bytes=64)
                nc.vector.tensor_copy(out=v[a, h][:], in_=tab[a][:].indirect(offs_sb[:, 32 * h : 32 * h + 32]))

        w4_dealt_sc = keep.tile([P, 2, PASS], U8, name="w4_dealt_sc", align_bytes=64)
        nc.vector.tensor_copy(
            out=w4_dealt_sc[:].rearrange("p a (t m) -> p a m t", t=PACK), in_=w4_sc[:, :, PASS:].rearrange("p a (m t) -> p a m t", t=PACK)
        )

        gather_table(0)
        load_wd(1)
        w4_second = keep.tile([P, 2, 2 * PASS], U8, name="w4_second", align_bytes=64)
        load_w4(w4_second, PASS, H)
        nc.sync.dma_start(pos3_sb[:], pos3)
        nc.sync.dma_start(pos2_sb[:], pos2)
        load_wd(2)
        nc.sync.dma_start(pos1_sb[:], pos1)
        w4_late = keep.tile([P, 2, 2 * (PASS - early_cols)], U8, name="w4_late", align_bytes=64)
        load_w4(w4_late, early_cols, PASS)
        load_wd(dealt)
        w8 = keep.tile([P, 2, N], U32, name="w8", align_bytes=64)
        nc.sync.dma_start(out=w8[:].bitcast(I32), in_=w8_words.rearrange("a p n t -> p a (n t)").bitcast(I32))
        w8_sc = keep.tile([P, 2, N], U8, name="w8_sc", align_bytes=64)
        nc.gpsimd.memset(w8_sc[:].bitcast(I32), 0)
        load_plane(nc.sync, w8_sc, w8_scales)
        bias = keep.tile([P, N // P], F32, name="bias", align_bytes=64)
        with nc.allow_non_contiguous_dma(reason="one bias value a partition and output tile"):
            nc.sync.dma_start(out=bias[:], in_=crumb0.rearrange("(c p) -> p c", p=P))

        codes_at = {1: 0, 2: 8 * PASS, 3: 12 * PASS}
        rounded = {}
        wq = {}
        wq_sc = {}

        rounded[0, 0] = keep.tile([P, 1, PASS], BF16, name="wd_bf00", align_bytes=64)[:]
        rounded[0, 1] = tables.tile([P, 1, PASS], BF16, name="wd_bf01", align_bytes=64, offset=table_bytes)[:]
        rounded[1] = tables.tile([P, 1, 2, PASS], BF16, name="wd_bf1", align_bytes=64, offset=table_bytes + 4 * PASS)
        rounded[2] = codes_then.tile([P, 2, 2, PASS], BF16, name="wd_bf2", align_bytes=64, offset=codes_at[1])
        for i in (1, 2):
            for a in range(2):
                rounded[i, a] = rounded[i][:, :, a, :]

        def round_wd(i, a, copy, parts=slice(0, 2)):
            copy(
                out=rounded[i, a].rearrange("p s (c i j) -> p s c j i", i=4, j=PACK)[:, parts, :, :, :],
                in_=wd_raw[i, a].rearrange("p j (s c i) -> p s c j i", i=4, c=P // 4)[:, parts, :, :, :],
            )

        dealt_at = {(0, 0): 4 * M, (0, 2): 8 * M, (1, 0): region_bytes + 4 * M, (1, 2): 2 * region_bytes + 4 * M}

        def round_dealt(a, ts, rows, copy):
            if (dealt, a, ts.start) not in rounded:
                rounded[dealt, a, ts.start] = arena.tile(
                    [P, ts.stop - ts.start, P, PACK], BF16, name="wd_dealt%d%d" % (a, ts.start), align_bytes=64, offset=dealt_at[a, ts.start]
                )
            copy(
                out=rounded[dealt, a, ts.start][:].rearrange("p t m j -> p m j t")[:, rows, :, :],
                in_=wd_raw[dealt, a].rearrange("p j (m t) -> p m j t", t=PACK)[:, rows, :, ts],
            )

        def quantize_wd(source, keys):
            name = "%d%d" % keys[0]
            width = P * len(keys)
            if keys == [(0, 0)]:
                codes = tables.tile([P, width], U32, name="wq" + name, align_bytes=64, offset=table_bytes + 2 * PASS)
            elif keys[0][1] in codes_at:
                codes = codes_then.tile([P, width], U32, name="wq" + name, align_bytes=64, offset=codes_at[keys[0][1]])
            else:
                codes = keep.tile([P, width], U32, name="wq" + name, align_bytes=64)
            plane = keep.tile([P, width], U8, name="wq_sc" + name, align_bytes=64)
            nc.vector.quantize_mx(out=codes[:].bitcast(FP8X4), scales=plane[:], in_=source)
            for k, key in enumerate(keys):
                wq[key] = codes[:, P * k : P * (k + 1)]
                wq_sc[key] = plane[:, P * k : P * (k + 1)]

        def quantize_slice(s):
            quantize_wd(rounded[min(s, 2)][:, max(s - 2, 0), :, :].rearrange("p a x -> p (a x)"), [(0, s), (1, s)])

        def quantize_first(a):
            quantize_wd(rounded[0, a][:, 0, :], [(a, 0)])

        def quantize_dealt(a, ts):
            source = rounded[dealt, a, ts.start][:].rearrange("p t m j -> p (t m j)")
            quantize_wd(source, [(a, PACK + t) for t in range(ts.start, ts.stop)])

        w4_dealt = keep.tile([P, 2, 2 * PASS], U8, name="w4_dealt", align_bytes=64)

        def deal_w4_words():
            nc.vector.tensor_copy(
                out=w4_dealt[:].bitcast(U16).rearrange("p a (t m) -> p a m t", t=PACK),
                in_=w4_second[:].bitcast(U16).rearrange("p a (m t) -> p a m t", t=PACK),
            )

        banks_taken = []
        first_banks = (0, 2, 3, 1, 4, 5, 6, 7, 4, 5, 6, 7, 0, 3, 2, 1, 4, 5, 6, 7, 0, 3)
        later_banks = (2, 1, 4, 5, 6, 7, 0, 3, 0, 3, 2, 1, 6, 2, 1, 7, 1, 5, 0, 3, 6, 4)

        def bank(index=None):
            if index is None:
                taken = len(banks_taken)
                index = first_banks[taken] if taken < len(first_banks) else later_banks[taken - len(first_banks)]
                banks_taken.append(index)
            return psum.tile([P, BANK], F32, name="acc%d" % index)

        def one_pass(acc, s, is_act, h, a, opens):
            if not is_act:
                lhs = wq[a, s].bitcast(FP8X4)
                lhs_sc = wq_sc[a, s]
            else:
                if s < EARLY_ACTS:
                    words, t = w4_early, s
                elif s < PACK:
                    words, t = w4_late, s - EARLY_ACTS
                else:
                    words, t = w4_dealt, s - PACK
                lhs = words[:, a, 2 * P * t : 2 * P * (t + 1)].bitcast(FP4X4)
                lhs_sc = (w4_sc, w4_dealt_sc)[s // PACK][:, a, P * (s % PACK) : P * (s % PACK + 1)]
            nc.tensor.matmul_mx(
                out=acc[:], lhsT=lhs, lhsT_scale=lhs_sc, rhs=v[a, h][:].bitcast(FP8X4),
                rhs_scale=v_sc[:, a, BANK * h : BANK * (h + 1)], start=opens, stop=not opens,
            )

        def in_region(s, shape, name):
            return arena.tile(shape, F32, name=name, align_bytes=64, offset=region_bytes * s if s < PACK else after_raw + 4 * S * (s - PACK))

        act = {}
        dough = {}
        share = {}
        prev = {}
        diff = {}
        prod = {}

        def new_window(s, is_act):
            if is_act:
                act[s] = in_region(s, [P, S], "act_w%d" % s)
                return act[s]
            dough[s] = ring.tile([P, S], F32, name="dough_w", bufs=4)
            return dough[s]

        def empty(window, h, acc, copy=nc.scalar.copy):
            copy(out=window[:, BANK * h : BANK * (h + 1)], in_=acc[:])

        def first_stage(s, is_act, order=(0, 1)):
            window = new_window(s, is_act)
            for h in range(2):
                acc = bank()
                for a in order:
                    one_pass(acc, s, is_act, h, a, a == order[0])
                empty(window, h, acc)

        tiles = M // P
        turned = keep.tile([P, 2, tiles, P, 2], BF16, name="turned", align_bytes=64)
        prev_dealt = keep.tile([P, PACK, M], F32, name="prev_dealt", align_bytes=64)
        prod_dealt = keep.tile([P, PACK, M], F32, name="prod_dealt", align_bytes=64)
        z_bf = {(0, 2 * P * h): late_z.tile([P, 2 * P, PACK], BF16, name="z_half%d" % h, align_bytes=64, offset=16 * P * h) for h in range(2)}
        zq = [keep.tile([P, M], U32, name="zq%d" % b, align_bytes=64) for b in range(2)]
        zq_sc = [keep.tile([P, M], U8, name="zq_sc%d" % b, align_bytes=64) for b in range(2)]

        def make_share(s):
            if s == 0:
                share[s] = arena.tile([P, M], F32, name="share0", align_bytes=64, offset=raw_at[2, 1] + 4 * S)
            elif s == 1:
                share[s] = codes_then.tile([P, M], F32, name="share1", align_bytes=64, offset=codes_at[2])
            elif s == 2:
                share[s] = codes_then.tile([P, M], F32, name="share2", align_bytes=64, offset=codes_at[3])
            else:
                share[s] = ring.tile([P, M], F32, name="share", bufs=3)
            nc.scalar.activation(out=share[s][:], in_=act[s][:].indirect(pos1_sb[:]), func=ACT.Sigmoid)

        def entries(cols):
            return slice(cols.start // 16, cols.stop // 16)

        def pick_prev(s, cols):
            if s not in prev:
                if s < PACK:
                    prev[s] = keep.tile([P, M], F32, name="prev%d" % s, align_bytes=64)[:]
                    prod[s] = keep.tile([P, M], F32, name="prod%d" % s, align_bytes=64)[:]
                else:
                    prev[s] = prev_dealt[:, s - PACK, :]
                    prod[s] = prod_dealt[:, s - PACK, :]
            nc.vector.tensor_copy(out=prev[s][:, cols], in_=dough[s][:].indirect(pos3_sb[:, entries(cols)]))

        def pick_diff(s, cols):
            if s not in diff:
                if s == 0:
                    diff[s] = keep.tile([P, M], F32, name="diff0", align_bytes=64)
                elif s == 3:
                    diff[s] = arena.tile([P, M], F32, name="diff3", align_bytes=64, offset=dealt_at[1, 0])
                else:
                    diff[s] = in_region(s - 1, [P, M], "diff%d" % s)
            nc.vector.tensor_tensor(
                out=diff[s][:, cols], in0=dough[s][:].indirect(pos2_sb[:, entries(cols)]), in1=prev[s][:, cols], op=ALU.subtract
            )

        def weigh(s, cols, engine=nc.vector):
            engine.tensor_tensor(out=prod[s][:, cols], in0=diff[s][:, cols], in1=share[s][:, cols], op=ALU.mult)

        def turn(cols):
            acc = bank()
            for t in range(PACK):
                for i, term in enumerate((prod[t], prev[t])):
                    nc.tensor.matmul(
                        out=acc[:, P * t : P * (t + 1)], lhsT=term[:, cols], rhs=ident[:], is_transpose=True, start=(i == 0), stop=(i == 1)
                    )
            nc.scalar.copy(out=turned[:, :, cols.start // P, :, :], in_=acc[:].rearrange("m (q u e) -> m u q e", u=2, e=2))

        def turn_back(cols):
            first, last = cols.start // P, cols.stop // P
            acc = bank()
            for c in range(first, last):
                for u in range(2):
                    words = turned[:, u, c, :, :].rearrange("m p e -> m (p e)").bitcast(F32)
                    k = 2 * (c - first) + u
                    nc.tensor.transpose(acc[:, P * k : P * (k + 1)], words, ident[:])
            nc.scalar.copy(
                out=z_bf[0, cols.start][:].rearrange("p m t -> p (m t)").bitcast(F32).rearrange("p (c m u) -> p c m u", m=P, u=2),
                in_=acc[:, : 2 * P * (last - first)].rearrange("p (c u m) -> p c m u", u=2, m=P),
            )

        def blend(cols):
            at = 8 * cols.start if cols.start > M // 2 else 0
            z_bf[1, cols.start] = late_z.tile([P, cols.stop - cols.start, PACK], BF16, name="z_piece%d" % cols.start, align_bytes=64, offset=at)
            nc.vector.tensor_tensor(
                out=z_bf[1, cols.start][:].rearrange("p (c i) t -> p c t i", i=4),
                in0=prod_dealt[:, :, cols].rearrange("p t (c i) -> p c t i", i=4),
                in1=prev_dealt[:, :, cols].rearrange("p t (c i) -> p c t i", i=4),
                op=ALU.add,
            )

        def quantize_z(b, cols):
            nc.vector.quantize_mx(
                out=zq[b][:, cols].bitcast(FP8X4), scales=zq_sc[b][:, cols], in_=z_bf[b, cols.start][:].rearrange("p m t -> p (m t)")
            )

        sums = {}
        per_bank = 2

        def last_pass(cols, b, opens):
            width = cols.stop - cols.start
            for c in range(N // P):
                group, i = divmod(c, per_bank)
                if (cols.start, group) not in sums:
                    sums[cols.start, group] = bank()
                nc.tensor.matmul_mx(
                    out=sums[cols.start, group][:, width * i : width * (i + 1)], lhsT=w8[:, b, P * c : P * (c + 1)].bitcast(FP8X4),
                    lhsT_scale=w8_sc[:, b, P * c : P * (c + 1)],
                    rhs=zq[b][:, cols].bitcast(FP8X4), rhs_scale=zq_sc[b][:, cols],
                    start=(opens and i == 0), stop=(not opens and i == per_bank - 1),
                )

        def finish(cols, on_vector):
            width = cols.stop - cols.start
            for group in range(N // P // per_bank):
                result = keep.tile([P, per_bank, width], F32, name="result%d%d" % (cols.start, group), align_bytes=64)
                acc = sums[cols.start, group]
                tiles_of = slice(per_bank * group, per_bank * (group + 1))
                if group in on_vector:
                    nc.vector.tensor_tensor(
                        out=result[:], in0=acc[:, : per_bank * width].rearrange("p (c m) -> p c m", c=per_bank),
                        in1=bias[:, tiles_of].unsqueeze(2).to_broadcast([P, per_bank, width]), op=ALU.add,
                    )
                else:
                    for i in range(per_bank):
                        c = per_bank * group + i
                        nc.scalar.activation(
                            out=result[:, i, :], in_=acc[:, width * i : width * (i + 1)], func=ACT.Identity, bias=bias[:, c : c + 1]
                        )
                (nc.sync if group in on_vector or cols.start == 0 else nc.scalar).dma_start(
                    out=out[P * tiles_of.start : P * tiles_of.stop, cols].rearrange("(c p) m -> p c m", p=P), in_=result[:]
                )

        whole = slice(0, M)
        halves = [slice(0, M // 2), slice(M // 2, M)]
        last = SLICES - 1
        edges = [sum(LAST_PIECES[:i]) for i in range(len(LAST_PIECES) + 1)]
        pieces = [slice(edges[i], edges[i + 1]) for i in range(len(LAST_PIECES))]
        on_vector, on_scalar = nc.vector.tensor_copy, nc.scalar.copy

        act_banks = {key: bank() for key in ((0, 0), (1, 0), (0, 1), (1, 1))}
        for (s, h), acc in act_banks.items():
            one_pass(acc, s, True, h, 0, True)
        gather_table(1)
        round_wd(0, 0, on_scalar, slice(0, 1))
        for s in range(EARLY_ACTS):
            new_window(s, True)
            one_pass(act_banks[s, 0], s, True, 0, 1, False)
            empty(act[s], 0, act_banks[s, 0])
        one_pass(act_banks[0, 1], 0, True, 1, 1, False)
        empty(act[0], 1, act_banks[0, 1])
        quantize_first(0)
        round_wd(0, 1, on_vector, slice(0, 1))
        round_wd(1, 0, on_vector, slice(0, 1))
        quantize_first(1)
        dough_banks = [bank() for h in range(2)]
        for h in range(2):
            one_pass(dough_banks[h], 0, False, h, 0, True)
        new_window(0, False)
        for h in range(2):
            one_pass(dough_banks[h], 0, False, h, 1, False)
        empty(dough[0], 0, dough_banks[0])
        round_wd(1, 1, on_vector, slice(0, 1))
        quantize_slice(1)
        deal_w4_words()
        empty(dough[0], 1, dough_banks[1], on_vector)
        one_pass(act_banks[1, 1], 1, True, 1, 1, False)
        empty(act[1], 1, act_banks[1, 1])
        first_stage(1, False)
        for cols in halves:
            pick_prev(0, cols)
        for cols in halves:
            pick_diff(0, cols)
        round_wd(2, 0, on_scalar, slice(0, 1))
        round_wd(2, 0, on_vector, slice(1, 2))
        round_wd(2, 1, on_scalar)
        make_share(0)
        pick_prev(1, whole)
        quantize_slice(2)
        quantize_slice(3)
        weigh(0, whole)
        pick_diff(1, whole)
        first_stage(2, True)
        first_stage(3, True)
        first_stage(2, False)
        make_share(1)
        round_dealt(0, slice(0, 2), slice(0, P), on_vector)
        round_dealt(0, slice(2, PACK), slice(0, P), on_vector)
        pick_prev(2, whole)
        quantize_dealt(0, slice(0, 2))
        weigh(1, whole)
        pick_diff(2, whole)
        first_stage(3, False)
        round_dealt(1, slice(0, 2), slice(0, P), on_vector)
        make_share(2)
        pick_prev(3, whole)
        quantize_dealt(1, slice(0, 2))
        round_dealt(1, slice(2, PACK), slice(0, P), on_vector)
        weigh(2, whole, nc.gpsimd)
        pick_diff(3, whole)
        first_stage(4, True)
        make_share(3)
        first_stage(5, True)
        first_stage(4, False)
        for s in range(PACK, last):
            pick_prev(s, whole)
            if s == PACK:
                quantize_dealt(0, slice(2, PACK))
                weigh(s - 1, whole, nc.gpsimd)
                quantize_dealt(1, slice(2, PACK))
            else:
                weigh(s - 1, whole, nc.gpsimd)
            pick_diff(s, whole)
            first_stage(s + 1, False)
            if s == last - 1:
                first_stage(s, True)
            make_share(s)
        for c in range(tiles // 2):
            turn(slice(P * c, P * (c + 1)))
        first_stage(last, True)
        turn_back(halves[0])
        make_share(last)
        for c in range(tiles // 2, tiles):
            turn(slice(P * c, P * (c + 1)))
        turn_back(halves[1])
        pick_prev(last, whole)
        weigh(last - 1, whole)
        pick_diff(last, pieces[0])
        pick_diff(last, pieces[1])
        weigh(last, pieces[0])
        pick_diff(last, pieces[2])
        quantize_z(0, halves[0])
        last_pass(pieces[0], 0, True)
        blend(pieces[0])
        weigh(last, pieces[1])
        quantize_z(1, pieces[0])
        last_pass(pieces[0], 1, False)
        weigh(last, pieces[2])
        blend(pieces[1])
        quantize_z(0, halves[1])
        last_pass(pieces[1], 0, True)
        last_pass(pieces[2], 0, True)
        blend(pieces[2])
        quantize_z(1, pieces[1])
        quantize_z(1, pieces[2])
        last_pass(pieces[1], 1, False)
        last_pass(pieces[2], 1, False)
        finish(pieces[0], ())
        finish(pieces[1], (1,))
        finish(pieces[2], (1,))
